import numpy as np, ml_dtypes
CORES = [48,51,52,55]
N = 4
import mx_ref
BF = ml_dtypes.bfloat16
def pick(q, e):
    c = np.concatenate([q[0].reshape(128, -1, 4), np.zeros((128, 1, 4), np.uint8)], axis=1); s = np.concatenate([q[1], np.ones((16, 1), np.uint8)], axis=1)
    return (np.ascontiguousarray(c[:, e].reshape(128, -1)), np.ascontiguousarray(s[:, e]))
def join(*qs):
    return (np.concatenate([q[0] for q in qs], axis=1), np.concatenate([q[1] for q in qs], axis=1))
def put(q, e, v):
    c, s = q[0].reshape(128, -1, 4).copy(), q[1].copy(); c[:, e] = v[0].reshape(128, -1, 4); s[:, e] = v[1]
    return (c.reshape(128, -1), s)
def pk(c, s):
    return (np.ascontiguousarray(c), mx_ref.live(s))
def emit(q):
    return q[0], q[1]
def decode(q):
    o = []
    for b in range(4):
        e = np.zeros((128, 128, 4), np.float32); e[np.arange(128), np.arange(128), b] = 1
        o.append(mx_ref.matmul(mx_ref.quantize(e.reshape(128, 512).astype(BF)), q))
    return np.stack(o, axis=2).reshape(128, -1)
def cut(t, i, w=512):
    return t[:, w * i:w * i + w]
def f(rng, *shape):
    return mx_ref.flush((rng.standard_normal(shape, dtype=np.float32) * np.exp2(rng.integers(-2, 3, shape[:-1] + (1,)))).astype(BF))
def wide(rng, *shape, cols=0):
    v = rng.standard_normal(shape, dtype=np.float32) * np.exp2(rng.integers(-12, 13, shape)).astype(np.float32)
    if cols: v *= np.repeat(np.exp2(rng.integers(-cols, cols + 1, shape[:-2] + (1, shape[-1] // 4))) * (rng.random(shape[:-2] + (1, shape[-1] // 4)) > 0.0625), 4, axis=-1).astype(np.float32)
    return mx_ref.flush(v.astype(BF))
P, O = 384, 1
PART = [2, 1]
def keep(v):
    v = v.astype(np.float32)
    v[np.abs(v) < np.float32(2.0 ** -16)] = 0
    return v.astype(BF)
def astile(m):
    return np.ascontiguousarray(m.reshape(128, 4, -1).transpose(0, 2, 1)).reshape(128, -1)
def setup_inputs(rng):
    return {"x": keep(f(rng, N, 128, 4 * P)), "u": f(rng, N, 128, 512), "w": f(rng, N, 128, 512 * O)}
def setup_inputs_spread(rng):
    return {**setup_inputs(rng), "x": keep(wide(rng, N, 128, 4 * P, cols=6)), "u": wide(rng, N, 128, 512)}
def setup_inputs_ties(rng):
    d, xs, bare = setup_inputs(rng), [], int(rng.integers(0, N))
    for r in range(N):
        which = rng.permutation(np.concatenate([np.zeros(7 * P // 8, int), rng.integers(1, 6, P // 8)]))
        v = np.array(f(rng, 128, 24)).reshape(128, 6, 4)
        if r == bare: v[:, 0] = 0
        xs.append(keep(v[:, which].reshape(128, -1)))
    return {**d, "x": np.stack(xs)}
def setup_inputs_near(rng):
    d, xs, us = setup_inputs(rng), [], np.array(f(rng, N, 128, 512))
    H, K = P // 2, P // 4
    rows = np.setdiff1d(np.arange(480), [0, 4, 32])
    R = len(rows)
    for r in range(N):
        at = np.concatenate([[P - 1], rng.permutation(np.arange(1, P - 1)), [0]])
        pair, rest = np.sort(at[:H].reshape(K, 2), axis=1), at[H:]
        base = np.zeros((512, K))
        base[rows] = np.stack([rng.permutation(R) % 4 + 4 for j in range(K)], axis=1) * rng.choice([-1.0, 1.0], (R, K))
        base[[0, 4, 32]] = 4
        m = np.zeros((512, P))
        m[:, pair[:, 0]] = base
        m[:, pair[:, 1]] = base
        m[480, pair[:, 0]] = 2.0 ** -5
        m[480, pair[:, 1]] = 2.0 ** -4
        m[484, pair[:, 0]] = 2.0 ** -5
        v = base[:, rng.permutation(np.repeat(np.arange(K), 2))]
        v[rows] *= np.stack([np.where(rng.permutation(R) < R // 4, -1.0, 1.0) for j in range(H)], axis=1)
        v[0, :K] = -4
        v[480] = 2.0 ** -5
        m[:, rest] = v
        xs.append(astile(m).astype(np.float32).astype(BF))
        us[r, :, :4] = 0
        us[r, 8, 0] = 2.0 ** 10
        us[r, 1, 0] = 2.0 ** -11
        us[r, 0, 0] = -2.0 ** -13
    return {**d, "x": np.stack(xs), "u": us}
def setup_inputs_far(rng):
    d, xs, us = setup_inputs(rng), [], []
    H, s = P // 2, rng.choice([-1.0, 1.0], (512, 1))
    for r in range(N):
        at, m = rng.permutation(P), np.zeros((512, P))
        m[:, at[:H]] = np.where(rng.random((512, H)) < 0.8, 1.0, 0.875)
        m[:, at[0]] = np.where(rng.random(512) < 0.9, 0.875, 0.75)
        m[:, at[H:]] = -np.where(rng.random((512, H)) < 0.5, 0.625, 0.75)
        xs.append(astile(m * s * 2.0 ** 28).astype(np.float32).astype(BF))
        us.append(astile(np.where(rng.random((512, 128)) < 0.5, 1.5, 1.75) * s * 2.0 ** 29).astype(np.float32).astype(BF))
    return {**d, "x": np.stack(xs), "u": np.stack(us)}
def setup_inputs_later(rng):
    d, xs = setup_inputs(rng), []
    H, K = P // 2, P // 4
    low = [r for r in range(N) if r < r ^ PART[0]]
    size = np.ones(N)
    for r in rng.permutation(low)[:len(low) // 2]: size[r ^ PART[0]] = 64
    for r in range(N):
        at, m = rng.permutation(P), np.zeros((512, P))
        z = rng.standard_normal((512, H))
        m[:, at[:H]] = z
        m[:, at[H:H + K]] = 0.6 * z[:, rng.integers(0, H, K)] + 0.05 * rng.standard_normal((512, K))
        m[:, at[H + K:]] = 0.45 * rng.standard_normal((512, P - H - K))
        xs.append(keep(astile(m * size[r])))
    return {**d, "x": np.stack(xs)}
def check_inputs(d):
    b = []
    for k, lo, hi in (("x", -20, 28), ("u", -30, 30), ("w", -30, 30)):
        v = np.abs(d[k].astype(np.float32))
        if not (np.isfinite(v).all() and ((v == 0) | (v >= 2.0 ** lo) & (v <= 2.0 ** hi)).all()): b.append("a value of " + k)
    return b
def gram(q):
    n = q[1].shape[1]
    g = np.zeros((n, n), np.float32)
    for i in range(0, n, 128):
        e = np.arange(i, i + 128)
        e[e >= n] = -1
        z = mx_ref.matmul(pick(q, e), pick(q, np.arange(i, n)))[:n - i]
        g[i:i + 128, i:] = z
        g[i:, i:i + 128] = z.T
    return g + np.float32(0)
def score(q, k):
    n = q[1].shape[1]
    e = np.arange(n + -n % 128)
    e[n:] = -1
    return np.concatenate([mx_ref.matmul(pick(q, e[i:i + 128]), pick(k, np.arange(4))) for i in range(0, len(e), 128)])[:n] + np.float32(0)
def high(s, k):
    return np.sort(np.argsort(-s, kind="stable")[:k])
def opened(qs):
    q, out, i = join(*qs), [], 0
    n = q[1].shape[1]
    e = np.arange(n + -n % 4)
    e[n:] = -1
    v = decode(pick(q, e)).reshape(128, -1, 4)
    for p in qs:
        k = p[1].shape[1]
        out.append(v[:, i:i + k])
        i += k
    return out
def anew(v):
    n = v.shape[1]
    v = np.concatenate([v, np.zeros((128, -n % 4, 4), np.float32)], axis=1)
    return pick(mx_ref.quantize(np.ascontiguousarray(v.reshape(128, -1).astype(BF))), np.arange(n))
def reference(x, u, w):
    y, pa = np.zeros((N, 128, O * P), np.float32), np.zeros((N, 1, P + P // 2 + P // 4), np.float32)
    oc, osc = np.zeros((N, 128, 4 * P), np.uint8), np.zeros((N, 16, P), np.uint8)
    uq = [mx_ref.quantize(np.ascontiguousarray(u[r])) for r in range(N)]
    front = [mx_ref.quantize(np.ascontiguousarray(x[r])) for r in range(N)]
    fronts, kin, ways, at = [], [], [], 0
    for l in range(3):
        n = P >> l
        who, done, kept, way = [], [], [], []
        for r in range(N):
            g = gram(front[r])
            piv = high(np.diagonal(g), n // 2)
            non = np.setdiff1d(np.arange(n), piv)
            par = piv[np.argmax(g[piv][:, non], axis=0)]
            pa[r, 0, at + piv] = piv
            pa[r, 0, at + non] = par
            have, first = np.unique(par, return_index=True)
            who.append((non, par, have, non[first]))
        v = opened([pick(front[r], np.concatenate([who[r][0], who[r][2]])) for r in range(N)])
        for r in range(N):
            non, par, have, kid = who[r]
            dn, dp = v[r][:, :n // 2], v[r][:, n // 2:]
            new = anew(dn - np.float32(0.5) * dp[:, np.searchsorted(have, par)])
            done.append(put(front[r], non, new))
            kept.append((have, kid, dp))
            if l < 2:
                go = non[high(score(new, uq[r])[:, l], n // 4)]
                way.append((np.setdiff1d(non, go), go))
        at += n
        fronts.append(done)
        kin.append(kept)
        ways.append(way)
        if l < 2: front = [join(pick(done[r], way[r][0]), pick(done[r ^ PART[l]], way[r ^ PART[l]][1])) for r in range(N)]
    below = None
    for l in (2, 1, 0):
        n = P >> l
        now = fronts[l]
        if l < 2:
            k = n // 4
            for r in range(N):
                stay, go = ways[l][r]
                now[r] = put(now[r], stay, pick(below[r], np.arange(k)))
                now[r] = put(now[r], go, pick(below[r ^ PART[l]], np.arange(k, 2 * k)))
        v = opened([pick(now[r], kin[l][r][1]) for r in range(N)])
        for r in range(N):
            have, kid, dp = kin[l][r]
            now[r] = put(now[r], have, anew((dp + v[r]) * np.float32(0.5)))
        below = now
    for r in range(N):
        for o in range(O):
            y[r, :, o * P:o * P + P] = mx_ref.matmul(mx_ref.quantize(np.ascontiguousarray(cut(w[r], o))), below[r])
        oc[r], osc[r] = emit(below[r])
    return {"y": y, "oc": oc, "osc": osc, "pa": pa}

@@ -1,0 +1,698 @@
+from concourse.bass import DstId, RemoteDMATransfer
+from concourse.mybir import dt, AluOpType, AxisListType, ActivationFunctionType
+
+A = AluOpType
+F = ActivationFunctionType
+P = 384
+PART = [2, 1]
+NS = [384, 192, 192]
+FO = [384, 192, 0]
+AV = [384, 192, 192]
+BE = [576, 320, 320]
+PPO = [576, 480, 384]
+CO = [0, 192, 288]
+PAO = [0, 384, 576]
+C16 = 201326592.0
+X4, U8, F32, BF, U16, I32 = "float8_e4m3fn_x4", "uint8", "float32", "bfloat16", "uint16", "int32"
+
+SCRATCH = {"ps": ("psum", [128, 4096], F32)}
+for _n, _w in (("f", 768), ("s0", 768), ("s1", 416), ("s2", 448), ("pc", 768), ("nw0", 224), ("nw1", 128), ("cq", 1280),
+               ("lq", 1152), ("sq", 1536), ("uq", 128), ("ur", 256), ("wq", 128), ("fin", 384), ("up0", 96), ("dn1", 96)):
+    SCRATCH[_n] = ("sbuf", [128, _w], X4)
+    SCRATCH[_n + "s"] = ("sbuf", [128, _w], U8)
+for _n, _w, _d in (("xt", 1536, BF), ("ut", 512, BF), ("wt", 512, BF), ("on", 512, BF), ("idn", 128, BF), ("cw", 512, BF),
+                   ("et", 520, BF), ("eh", 520, BF), ("xp", 512, BF), ("xo", 512, BF), ("xl", 1536, BF), ("xm", 768, BF),
+                   ("xk", 512, BF), ("xc", 512, BF), ("xn", 768, BF), ("ht", 896, BF), ("r16", 128, BF), ("qrow", 384, BF),
+                   ("iot", 768, F32), ("pi", 2, I32), ("cc", 96, F32), ("wk0", 48, F32), ("wk", 384, F32), ("off", 320, U16),
+                   ("col", 320, F32), ("tf", 12288, F32), ("tb", 10240, BF), ("pat", 672, F32), ("yt", 384, F32)):
+    SCRATCH[_n] = ("sbuf", [128, _w], _d)
+
+SEMAPHORES = ["v", "a", "t", "g", "lx0", "lx1", "lx2", "lu", "lw", "sent", "ar0", "ar1", "ar2", "st1", "st3"]
+
+PM, FX, JA, JB, JC, Q96, OH, OHM, QW, KS, V16, FS, NM, OHN = 0, 1, 2, 5, 7, 8, 10, 16, 22, 34, 44, 56, 57, 58
+CYC, HOP, FAR = 0.001, 0.05, 2.0
+PLANS, TRIES = {}, 2500
+
+
+def R(name, c0, c1, step=1, p0=0, p1=128):
+    return (name, p0, p1, c0, c1, step)
+
+
+def sub(r, a, b, step=1, p0=0, p1=None):
+    return (r[0], p0, r[2] if p1 is None else p1, r[3] + a, r[3] + b, step)
+
+
+def width(r):
+    return len(range(r[3], r[4], r[5]))
+
+
+def meet(a, b, banks):
+    if banks:
+        return a[3] // 512 <= (b[4] - 1) // 512 and b[3] // 512 <= (a[4] - 1) // 512
+    if a[2] <= b[1] or b[2] <= a[1] or a[4] <= b[3] or b[4] <= a[3]:
+        return False
+    if a[5] == 1 and b[5] == 1:
+        return True
+    return bool(set(range(a[3], a[4], a[5])) & set(range(b[3], b[4], b[5])))
+
+
+def arrange(ops):
+    seen = {}
+    for i, o in enumerate(ops):
+        pre = set(o["after"])
+        for a, wr in [(r, False) for r in o["r"]] + [(r, True) for r in o["w"]]:
+            for j, b, w2 in seen.get(a[0], []):
+                bk = a[0] == "ps" and ops[j]["q"] != o["q"]
+                if (wr or w2 or bk) and meet(a, b, bk):
+                    pre.add(j)
+        for a, wr in [(r, False) for r in o["r"]] + [(r, True) for r in o["w"]]:
+            seen.setdefault(a[0], []).append((i, a, wr))
+        o["pre"] = pre
+    top = 0.0
+    for turn in range(2):
+        rank = [top - o["by"] if o["by"] else 0.0 for o in ops]
+        for i in range(len(ops) - 1, -1, -1):
+            rank[i] += ops[i]["c"] + ops[i]["lat"]
+            for j in ops[i]["pre"]:
+                rank[j] = max(rank[j], rank[i] + HOP)
+        top = max(rank)
+    n = len(ops)
+    post = [[] for o in ops]
+    for i, o in enumerate(ops):
+        for j in o["pre"]:
+            post[j].append(i)
+    gap = [[(j, 0.001 if o["q"] == "t" == ops[j]["q"] else ops[j]["lat"] + HOP) for j in o["pre"]] for o in ops]
+
+    def plan(bonus):
+        left = [len(o["pre"]) for o in ops]
+        ready = [i for i in range(n) if not left[i]]
+        busy, start, end = {}, [0.0] * n, [0.0] * n
+        while ready:
+            i = max(ready, key=lambda k: rank[k] + bonus[k])
+            ready.remove(i)
+            o = ops[i]
+            t = max([end[j] + d for j, d in gap[i]] + [0.0])
+            slots = busy.setdefault(o["q"], [])
+            at = len(slots)
+            for k, (s, e) in enumerate(slots):
+                if e <= t:
+                    continue
+                if t + o["c"] <= s:
+                    at = k
+                    break
+                t = e
+            start[i], end[i] = t, t + o["c"]
+            if o["q"]:
+                slots.insert(at, (t, end[i]))
+            for j in post[i]:
+                left[j] -= 1
+                if not left[j]:
+                    ready.append(j)
+        return sorted(range(n), key=lambda k: (start[k], k))
+
+    def span(order):
+        tot = 0.0
+        for slow in ("", "v", "a", "t"):
+            free, end = {}, [0.0] * n
+            for i in order:
+                o = ops[i]
+                t = max([end[j] + d for j, d in gap[i]] + [free.get(o["q"], 0.0)])
+                end[i] = t + o["c"] * (1.2 if o["q"] == slow else 1.0)
+                if o["q"]:
+                    free[o["q"]] = end[i]
+            tot += max(end[i] + ops[i]["lat"] for i in order)
+        return tot
+
+    if n not in PLANS:
+        bonus, seed = [0.0] * n, 1
+        best = plan(bonus)
+        least = span(best)
+        for turn in range(TRIES):
+            other = list(bonus)
+            for k in range(6):
+                seed = (seed * 1103515245 + 12345) % 2147483648
+                other[seed // 64 % n] = (seed // 65536 % 9 - 4) * (0.5 if k & 1 else 2.0)
+            order = plan(other)
+            t = span(order)
+            if t <= least:
+                bonus, best, least = other, order, t
+        PLANS[n] = best
+    return PLANS[n]
+
+
+def rank_program(g, core, T, topo):
+    rank = T.rank_of(core)
+    if rank is None:
+        return
+    ops = []
+    queue = {"v": g.vector, "a": g.scalar, "t": g.tensor, "g": g, "y": g.sync}
+    size = {n: v[2] for n, v in SCRATCH.items()}
+
+    def ap(r):
+        if not isinstance(r, tuple):
+            return r
+        if r[5] == 1:
+            return T[r[0]][r[1]:r[2], r[3]:r[4]]
+        return T[r[0]][r[1]:r[2], r[3]:r[4]:r[5]]
+
+    def op(q, fn, reads, writes, c, lat=0.0, sem=None, inc=1, after=()):
+        ops.append({"q": q, "fn": fn, "r": [r for r in reads if isinstance(r, tuple)], "w": writes, "sem": sem, "inc": inc,
+                    "c": c, "lat": lat, "after": after, "by": 0.0})
+        return len(ops) - 1
+
+    def sc(r):
+        return (r[0] + "s",) + r[1:]
+
+    def cyc(n, *sides):
+        return CYC * max(64, n / 2 if sides and all(size[s[0]] in (BF, U16) for s in sides) else n)
+
+    def memset(out, c):
+        op("v", lambda: g.vector.memset(ap(out), c), [], [out], cyc(width(out), out))
+
+    def copy(q, out, in_, scale=None):
+        if q == "a":
+            act(out, in_, F.Copy, scale=1.0 if scale is None else scale)
+        elif scale is None:
+            op("v", lambda: g.vector.tensor_copy(ap(out), ap(in_)), [in_], [out], cyc(width(out), out, in_))
+        else:
+            ts(out, in_, scale, A.mult)
+
+    def ts(out, in0, s1, op0, s2=None, op1=None):
+        if op1 is None:
+            op("v", lambda: g.vector.tensor_scalar(ap(out), ap(in0), ap(s1), None, op0), [in0, s1], [out], cyc(width(out), out, in0))
+        else:
+            op("v", lambda: g.vector.tensor_scalar(ap(out), ap(in0), ap(s1), ap(s2), op0, op1), [in0, s1, s2], [out], cyc(width(out), out, in0))
+
+    def tt(out, a, b, o):
+        op("v", lambda: g.vector.tensor_tensor(ap(out), ap(a), ap(b), o), [a, b], [out], cyc(width(out) * (1 if a[0] == "ps" else 2)))
+
+    def scan(out, d0, d1, init, o0, o1):
+        op("v", lambda: g.vector.tensor_tensor_scan(ap(out), ap(d0), ap(d1), init, o0, o1), [d0, d1], [out], cyc(width(out), out, d0, d1))
+
+    def turn(out, in_):
+        op("v", lambda: g.vector.transpose(ap(out), ap(in_)), [in_], [out], cyc(width(out)))
+
+    def minus_abs_sum(out, in_):
+        op("v", lambda: g.vector.tensor_reduce(ap(out), ap(in_), AxisListType.X, A.add, negate=True, apply_absolute_value=True),
+           [in_], [out], cyc(width(in_)))
+
+    def act(out, in_, func, bias=0.0, scale=1.0, acc=None, off=None):
+        def fn():
+            src = ap(in_) if off is None else ap(in_).indirect(ap(off))
+            if func == F.Copy and scale == 1.0 and acc is None:
+                return g.scalar.activation(ap(out), src, func)
+            if func == F.Copy:
+                return g.scalar.activation(ap(out), src, func, scale=ap(scale), accum_out=ap(acc))
+            return g.scalar.activation(ap(out), src, func, bias=ap(bias), scale=ap(scale), accum_out=ap(acc))
+        c = cyc(width(out)) if off is None else 0.065 + 1.5 * CYC * width(out)
+        op("a", fn, [in_, bias, scale, off], [out] + ([acc] if acc else []), c + (0.02 if acc else 0.0))
+
+    def fill(out, c):
+        copy("a", out, R("on", 0, width(out), 1, out[1], out[2]), scale=c)
+
+    def quant(out, in_):
+        op("v", lambda: g.vector.quantize_mx(ap(out), ap(sc(out)), ap(in_)), [in_], [out, sc(out)], 0.015 + 0.26 * CYC * width(in_))
+
+    def mm(bank, w, x, start=True, stop=True):
+        out = R("ps", 512 * bank, 512 * bank + x[4] - x[3])
+        op("t", lambda: g.tensor.matmul_mx(ap(out), ap(w), ap(sc(w)), ap(x), ap(sc(x)), start, stop), [w, sc(w), x, sc(x)], [out],
+           0.6 * CYC * (width(x) + 16), 0.05)
+
+    def pick(out, win, off):
+        op("v", lambda: g.vector.tensor_copy(ap(out).bitcast(dt.uint32), ap(win).bitcast(dt.uint32).indirect(ap(off))), [win, off], [out],
+           0.05 + 1.5 * CYC * width(out))
+        act(sc(out), sc(win), F.Copy, off=off)
+
+    def scatter(win, off, in_):
+        op("v", lambda: g.vector.tensor_copy(ap(win).indirect(ap(off)), ap(in_)), [in_, off], [win], 0.05 + 3.8 * CYC * width(in_))
+
+    def iota(out, pattern, base, cm, small=True):
+        if small:
+            op("g", lambda: g.iota(ap(out), pattern, base, cm, allow_small_or_imprecise_dtypes=True), [], [out], 0.13 + 2 * CYC * width(out))
+        else:
+            op("g", lambda: g.iota(ap(out), pattern, base, cm), [], [out], 0.13 + 2 * CYC * width(out))
+
+    def select(out, in_, pattern, cmp, base, cm):
+        op("g", lambda: g.affine_select(ap(out), ap(in_), pattern, cmp, 0.0, base, cm), [in_], [out], 0.17 + 2 * CYC * width(out))
+
+    def dma(q, out, in_, reads, writes, sem):
+        op(q, lambda: queue[q].dma_start(out, in_), reads, writes, 0.06, FAR, sem=sem, inc=16)
+
+    def exchange(pairs, part, sem):
+        other = T.cores[rank ^ part]
+        rid, pid = topo.addr(other)[:2]
+        eng = topo.engines(core, other)
+        per = len(eng) // (2 * len(pairs))
+        calls = []
+        for kind in range(2):
+            sides = [(s, d) if kind == 0 else (sc(s), sc(d)) for s, d in pairs]
+            masks = [sum(1 << e for e in eng[per * (kind * len(pairs) + i):][:per]) for i in range(len(pairs))]
+
+            def fn(kind=kind, sides=sides, masks=masks):
+                raw = [(ap(s).bitcast(dt.uint8), ap(d).bitcast(dt.uint8)) if kind == 0 else (ap(s), ap(d)) for s, d in sides]
+                if len(raw) == 1:
+                    return g.remote_dma(raw[0][1], raw[0][0], T.sem[sem], T.sem.sent, pid, rid, masks[0])
+                return g.remote_dma_fused([RemoteDMATransfer(dst_ids=[DstId(rid=rid, pnc=pid)], dma_engine_mask=m, remote_sem=T.sem[sem], src=s, dst=d)
+                                           for (s, d), m in zip(raw, masks)], local_sem=T.sem.sent)
+            calls.append(op("g", fn, [s for s, d in sides], [], 0.2, FAR, sem="sent", inc=per * len(pairs)))
+        op(None, None, [], [d for s, d in pairs] + [sc(d) for s, d in pairs], 0.0, sem=sem, inc=2 * per * len(pairs), after=calls)
+
+    used = {}
+
+    def take(name, k, p1=128, unit=2):
+        a = used.get(name, 0)
+        used[name] = a + -(-k // unit) * unit
+        return R(name, a, a + k, p1=p1)
+
+    def tf(k, p1=128):
+        return take("tf", k, p1, 16)
+
+    def tb(k, p1=128):
+        return take("tb", k, p1, 16)
+
+    def cc(c, k=1, pb=128):
+        return R("cc", c, c + k, p1=pb)
+
+    def one(r, k):
+        return sub(r, k, k + 1)
+
+    def bank(b, c0, c1, pb=128):
+        return R("ps", 512 * b + c0, 512 * b + c1, p1=pb)
+
+    def on(k, pb=128):
+        return R("on", 0, k, p1=pb)
+
+    CW, ONES = R("cq", 0, 128), R("cq", 128, 256)
+
+    def ET(b):
+        return R("cq", 256 + 128 * b, 384 + 128 * b)
+
+    def EH(b):
+        return R("cq", 768 + 128 * b, 896 + 128 * b)
+
+    for k in range(3):
+        dma("yay"[k], T.xt[:, 512 * k:512 * k + 512], T.x[:, 512 * k:512 * k + 512], [], [R("xt", 512 * k, 512 * k + 512)], "lx%d" % k)
+        quant(R("f", FO[0] + 128 * k, FO[0] + 128 * k + 128), R("xt", 512 * k, 512 * k + 512))
+    dma("y", T.ut[:], T.u[:], [], [R("ut", 0, 512)], "lu")
+    dma("y", T.wt[:], T.w[:], [], [R("wt", 0, 512)], "lw")
+    memset(on(512), 1.0)
+    iota(R("pi", 0, 1), [[0, 1]], 0, 1, small=False)
+    iota(R("r16", 0, 128), [[0, 8], [1, 16]], 0, 0)
+    select(R("idn", 0, 128), on(128), [[-1, 128]], A.is_equal, 0, 1)
+    select(R("cw", 0, 512, 4), on(128), [[1, 128]], A.is_ge, 0, -1)
+    iota(R("qrow", 0, 384), [[1, 384]], -192, 0)
+    iota(cc(JA, 3), [[128, 3]], 1 - 192, 1)
+    ts(cc(JA, 3), cc(JA, 3), -0.5, A.add)
+    iota(cc(JB, 2), [[96, 2]], 1 - 96, 1)
+    iota(cc(JC, 1), [[0, 1]], 1 - 48, 1)
+    memset(R("et", 0, 520), 0.0)
+    copy("a", R("et", 3, 512, 4), R("idn", 0, 128))
+    fill(R("eh", 0, 260), 0.0)
+    fill(R("eh", 260, 520), 0.0)
+    copy("a", R("eh", 3, 512, 4), R("idn", 0, 128), scale=-0.5)
+    iota(cc(V16, 12), [[16, 12]], 0, -1)
+    iota(cc(Q96, 2), [[96, 2]], 0, 1)
+    iota(cc(QW, 12), [[16, 12]], 0, 0)
+    iota(R("iot", 0, 768), [[1, 768]], 0, 0)
+    for name, w in (("xp", 512), ("xo", 512), ("xk", 512), ("xc", 512), ("xm", 768), ("xn", 768)):
+        for a in range(0, w, 256):
+            fill(R(name, a, a + 256), 0.0)
+    fill(R("xn", 192, 384, 4, p1=96), 1.0)
+    fill(R("xn", 576, 768, 4, p1=96), 1.0)
+    fill(R("xl", 3, 1536, 4), 0.0)
+    fill(R("ht", 768, 896), 0.0)
+    fill(R("cw", 1, 512, 4), 1.0)
+    fill(cc(KS, 9), 1.0)
+    fill(cc(KS + 4), 0.0)
+    quant(ONES, on(512))
+    ts(R("pi", 1, 2), R("pi", 0, 1), 15, A.bitwise_and)
+    copy("v", cc(PM), R("pi", 1, 2))
+    ts(R("cw", 2, 512, 4), R("r16", 0, 128), cc(PM), A.is_equal)
+    copy("a", R("cw", 3, 512, 4), R("cw", 2, 512, 4), scale=-1.0)
+    o_pm, o_u = take("off", 24), take("off", 16)
+    ts(o_pm, on(24), cc(PM), A.mult)
+    ts(R("wk0", 16, 32), R("r16", 0, 16), cc(PM), A.is_le, -4096.0, A.mult)
+    ts(R("wk0", 32, 48), R("r16", 0, 16), cc(PM), A.subtract, 1.0, A.is_equal)
+    ts(cc(FX), cc(PM), 14.5, A.is_lt, 2048.0, A.mult)
+    act(cc(FS), cc(FX), F.Identity, bias=-float(P))
+    copy("a", R("wk0", 32, 48), R("wk0", 32, 48), scale=2048.0)
+    tt(R("wk0", 0, 16), R("wk0", 16, 32), R("wk0", 32, 48), A.add)
+    memset(sub(o_u, 0, 8), 0)
+    memset(sub(o_u, 8, 16), 1)
+    act(R("wk", 0, 384), R("wk0", 0, 16), F.Copy, off=o_pm)
+    quant(CW, R("cw", 0, 512))
+    ts(cc(OH, 6), cc(V16, 6), cc(PM), A.add, 0.0, A.is_equal)
+    ts(cc(OHM, 6), cc(OH, 6), 1024.0, A.mult, -C16 - 1024.0, A.add)
+    for b in range(4):
+        quant(ET(b), R("et", 3 - b, 515 - b))
+        ops[-1]["by"] = 3.0
+        quant(EH(b), R("eh", 3 - b, 515 - b))
+        ops[-1]["by"] = 7.0
+    quant(R("uq", 0, 128), R("ut", 0, 512))
+    for l in range(2):
+        pick(R("ur", 128 * l, 128 * l + 128), R("uq", 0, 128), sub(o_u, 8 * l, 8 * l + 8))
+        ops[-2]["by"] = 9.0 if l == 0 else 0.0
+    quant(R("s1", 192, 320), on(512))
+    quant(R("s2", 192, 320), on(512))
+    quant(R("wq", 0, 128), R("wt", 0, 512))
+    copy("a", cc(NM), cc(PM), scale=-1.0)
+    act(cc(OHN, 3), cc(OHM, 3), F.Identity, bias=48.0)
+
+    def wrap(src, out, signs=False):
+        n = width(src)
+        ws = tf(n)
+        scan(ws, R("wk", 0, n), src, 0.0, A.add, A.max)
+        if signs:
+            ts(out, sub(ws, 15, n, 16), cc(FS), A.subtract, 0.5, A.mult)
+        else:
+            ts(out, sub(ws, 15, n, 16), cc(FX), A.subtract)
+
+    def half(n, K, pb, rows, vals, tile, apart=False, turned=False):
+        h = n // 2
+        s, sb, sn, cn = [take("col", K, pb) for i in range(4)]
+        run = tf(h + K, pb)
+        a = sub(run, h - 1, h - 1 + K)
+        xp = take("xp", 48, pb)
+        c0 = xp[3] // 4
+        for k in range(K - 1, -1, -1):
+            sg = tb(n, pb)
+            act(sg, rows[k], F.Sign, bias=vals[k], scale=-1.0, acc=one(s, k))
+            if k == 0 and K > 1 and not apart and rows[k][0] != "ps":
+                eq = tb(n, pb)
+                ts(eq, rows[k], vals[k], A.is_equal)
+                scan(sub(run, 0, h), sub(eq, 0, h), sub(eq, h, n), -float(n), A.add, A.add)
+            else:
+                minus_abs_sum(one(a, k), sg)
+        act(sb, s, F.Identity, bias=0.5 - n)
+        act(sn, s, F.Identity, bias=0.5 - n, scale=-1.0)
+        if K == 1:
+            ts(sub(xp, 0, 6, 5), on(2, pb), sb, A.mult, a, A.is_lt)
+        else:
+            tt(sub(xp, 0, 4 * K, 4), sb, a, A.is_lt)
+        tt(sub(xp, 20, 20 + 4 * K, 4), sn, a, A.is_gt)
+        if K == 1:
+            fill(one(xp, 21), -h / pb)
+        elif apart:
+            fill(sub(xp, 21, 21 + 4 * K, 4), -h / pb)
+            tt(sub(xp, 4 * K + 1, 8 * K + 1, 4), sb, a, A.is_lt)
+        else:
+            fill(one(xp, 16), -h / pb)
+            scan(sub(xp, 5, 41, 4), cc(KS, 9, pb), sub(xp, 0, 36, 4), 0.0, A.mult, A.add)
+        sq = take("sq", 128)
+        quant(sq, R("xp", 0, 512))
+        mm(3, CW, sq)
+        for k in range(K):
+            t = c0 + K + (k if apart else 0)
+            ts(one(cn, k), bank(3, c0 + k, c0 + k + 1, pb), bank(3, t, t + 1, pb), A.subtract, bank(3, c0 + 5 + k, c0 + 6 + k, pb), A.max)
+        q = [R("qrow", 192 - h, 192, p1=pb), R("qrow", 192, 192 + h, p1=pb)]
+        tot = n * K if apart else n
+        out = take("off", tot // 16)
+        if h >= 128:
+            cj = take("col", K, pb)
+            tt(cj, cn, cc(JA, K), A.subtract)
+        for side in ((1, 0) if turned else (0, 1)):
+            for k in range(K):
+                e = 4 * ((side ^ turned) * tot // 2 + (h * k if apart else 0)) + k
+                x = R(tile, e, e + 4 * h - k, 4, p1=pb)
+                if side == 0:
+                    ts(x, q[0], one(cn, k), A.is_ge)
+                elif h >= 128:
+                    act(x, q[1], F.Sign, bias=one(cj, k))
+                else:
+                    ts(x, q[1], one(cn, k), A.add, cc({96: JB, 48: JC}[h] + (0 if apart else k), 1, pb), A.is_ge)
+        cuts = [(0, h), (h, n)] if h >= 128 else [(0, tot)]
+        for i, (a0, a1) in enumerate(cuts):
+            m = max(a1 - a0, 128)
+            lq = take("lq", m)
+            quant(lq, R(tile, 4 * a0, 4 * (a0 + m)))
+            mm(i, ONES, lq)
+            wrap(bank(i, 0, a1 - a0), sub(out, a0 // 16, a1 // 16), signs=i == 1)
+        return out
+
+    def spread(cnt, K, pb, tile, b, more=0, under=None, step=0.0):
+        t, nl, has = take("col", K, pb), take("col", K, pb), take("col", K, pb)
+        G = pb // 16
+        xp = take(tile, 4 * K * G * (2 if under else 1), pb)
+        ts(t, cnt, -7.5, A.add, C16, A.add)
+        if under:
+            ts(has, cnt, under, A.is_lt, step, A.mult)
+            act(sub(xp, 4 * K * G + 1, 8 * K * G, 4, 0, 32), cc(QW, K * G, 32), F.Copy, scale=1 / 32)
+        for k in range(K):
+            e = 4 * G * k
+            act(sub(xp, e + 2, e + 4 * G, 4), cc(OHN if more and k else OHM, G, pb), F.Relu, bias=one(t, k))
+            ts(one(nl, k), one(t, k), C16, A.subtract, one(cnt, k), A.subtract)
+            ts(sub(xp, e + 3, e + 4 * G, 4), cc(OH, G, pb), one(nl, k), A.mult)
+            if under:
+                e += 4 * K * G
+                act(sub(xp, e + 2, e + 4 * G, 4), cc(OH, G, pb), F.Copy, scale=one(has, k))
+                act(sub(xp, e + 3, e + 4 * G, 4), cc(OH, G, pb), F.Copy, scale=cc(NM, 1, pb))
+        sq = take("sq", 128)
+        quant(sq, R(tile, 0, 512))
+        mm(b, CW, sq)
+        return bank(b, xp[3] // 4, xp[4] // 4)
+
+    L = {}
+
+    def casts(h, scale):
+        for b in range(4):
+            copy("va"[b & 1], R("ht", b, 4 * h, 4), bank(4 + b, 0, h), scale=scale)
+
+    def up(l):
+        n = NS[l]
+        h, fo, s = n // 2, FO[l], "s%d" % l
+        m = max(h, 128)
+        K, pb = (3, 128) if l == 0 else (2, 96)
+        w = 32 * K
+        for k in range(K):
+            win = R("f", fo + pb * k, fo + pb * k + 128)
+            mm(k, win, win)
+        d, xb, row = take("col", K, pb), tf(w, pb), tf(n, pb)
+        for k in range(K):
+            mk = tf(pb + 32, pb)
+            tt(sub(mk, 0, pb), bank(k, 0, pb, pb), R("idn", 0, pb, p1=pb), A.mult)
+            if k < K - 1:
+                act(tb(pb, pb), sub(mk, 0, pb), F.Copy, acc=one(d, k))
+                act(sub(xb, 32 * k, 32 * k + 32), on(32, pb), F.Copy, scale=one(d, k))
+            else:
+                fill(sub(mk, pb, pb + 32), 0.0)
+                last = tf(pb + 32, pb)
+                scan(last, mk, mk, 0.0, A.max, A.max)
+        vals = [one(d, k) for k in range(K - 1)] + [one(last, pb + 31)]
+        if l < 2:
+            turn(sub(row, w - 32, w), sub(last, pb, pb + 32))
+            turn(sub(row, 0, w - 32), sub(xb, 0, w - 32))
+        else:
+            turn(sub(row, 1, w, 2), sub(last, pb, pb + 32))
+            turn(sub(row, 0, w, 2), sub(xb, 0, 32))
+        if pb == 128:
+            for q in range(4):
+                copy("va"[q & 1], sub(row, w, 2 * w, 1, 32 * q, 32 * q + 32), sub(row, 0, w, 1, 32 * (q ^ 1), 32 * (q ^ 1) + 32))
+            for q in range(2):
+                copy("va"[q], sub(row, 2 * w, 4 * w, 1, 64 * q, 64 * q + 64), sub(row, 0, 2 * w, 1, 64 - 64 * q, 128 - 64 * q))
+        else:
+            for i in range(6):
+                q, sl = i % 3, 1 + i // 3
+                r = (q + sl) % 3
+                copy("va"[i & 1], sub(row, sl * w, sl * w + w, 1, 32 * q, 32 * q + 32), sub(row, 0, w, 1, 32 * r, 32 * r + 32))
+        if l < 2:
+            lw = half(n, K, pb, [row] * K, vals, "xl" if l == 0 else "xm")
+        else:
+            lw = half(h, K, pb, [sub(row, k, n, 2) for k in range(K)], vals, "xn", apart=True)
+        L["l", l] = lw
+        if l == 0:
+            pick(R(s, 0, h), R("f", fo, fo + n), sub(lw, 0, h // 16))
+            pick(R(s, h, n), R("f", fo, fo + n), sub(lw, h // 16, n // 16))
+        else:
+            pick(R(s, 0, n), R("f", fo, fo + n), lw)
+        K, pb, hp = [(2, 96, 192), (1, 96, 96), (2, 48, 48)][l]
+        par = take("col", K, pb)
+        for k in range(K):
+            a = h + (hp * k if l == 2 else 0)
+            mm(k, R(s, pb * k, pb * k + 128), R(s, a, a + m))
+            rm = tf(hp, pb)
+            scan(rm, bank(k, 0, hp, pb), on(hp, pb), -1e29, A.max, A.mult)
+            act(tb(hp, pb), rm, F.Sign, bias=one(rm, hp - 1), scale=-1.0, acc=one(par, k))
+        L["par", l] = par
+        for b in range(4):
+            mm(4 + b, ET(b), R(s, 0, m), True, False)
+        pw = take("off", h // 16)
+        L["p", l] = pw
+        ts(pw, spread(par, K, pb, "xp", 3, more=l == 2), float(h), A.add)
+        pick(R("pc", PPO[l], PPO[l] + h), R(s, 0, n), pw)
+        for b in range(4):
+            mm(4 + b, EH(b), R("pc", PPO[l], PPO[l] + m), False, True)
+        casts(h, None)
+        if l == 2:
+            quant(R(s, BE[l], BE[l] + 128), R("ht", 0, 512))
+            return
+        nw, mq = "nw%d" % l, 224 if l == 0 else 128
+        quant(R(nw, 0, mq), R("ht", 0, 4 * mq))
+        ur = R("ur", 128 * l, 128 * l + 128)
+        for k in range(K):
+            mm(1 + k, R(nw, pb * k, pb * k + 128), ur)
+        mm(0, ur, R(nw, 0, m))
+        sv = take("col", K, pb)
+        for k in range(K):
+            copy("va"[k], one(sv, k), bank(1 + k, 0, 1, pb))
+        both = half(h, K, pb, [bank(0, 0, h, pb)] * K, [one(sv, k) for k in range(K)], "xm" if l == 0 else "xk", turned=True)
+        L["s", l] = both
+        q, fo = h // 2, FO[l + 1]
+        if l == 0:
+            pick(R("up0", 0, q), R(nw, 0, h), sub(both, 0, q // 16))
+            exchange([(R("up0", 0, q), R("f", fo + q, fo + h))], PART[l], "ar0")
+            pick(R("f", fo, fo + q), R(nw, 0, h), sub(both, q // 16, h // 16))
+        else:
+            pick(R("f", fo + q, fo + q + h), R(nw, 0, h), both)
+            exchange([(R("f", fo + q, fo + h), R("f", fo + q + h, fo + 2 * h)), (R("f", fo + h, fo + q + h), R("f", fo, fo + q))], PART[l], "ar1")
+
+    def children(l):
+        h = NS[l] // 2
+        K, pb, k16 = h // 96, 96, h // 16
+        prow, cnt = tb(h), take("col", K, pb)
+        if l == 2:
+            for k in range(2):
+                ts(R("xc", 192 * k, 192 * k + 192, 4, p1=48), R("qrow", 192, 240, p1=48), one(L["par", l], k), A.is_equal)
+            sq = take("sq", 128)
+            quant(sq, R("xc", 0, 512))
+            mm(2, sq, CW)
+            act(tb(48, pb), bank(2, 0, 48, pb), F.Relu, bias=1.0, scale=-1.0, acc=cnt)
+        else:
+            act(prow, R("iot", 0, 2 * h), F.Identity, bias=-float(h), off=L["p", l])
+        for k in range(K if l < 2 else 0):
+            ne, cp = tb(h, pb), tb(h, pb)
+            ts(ne, sub(prow, 0, h, 1, 0, pb), cc(Q96 + k, 1, pb), A.not_equal)
+            scan(cp, ne, ne, 1.0, A.mult, A.mult)
+            act(tb(h, pb), cp, F.Copy, acc=one(cnt, k))
+        both = spread(cnt, K, pb, "xo", 2, under=(h if l < 2 else 48) - 0.5, step=float(AV[l] - h))
+        res = sub(both, 0, k16)
+        mw, ow, v = take("off", k16), take("off", k16), tf(2 * h)
+        if l == 2:
+            for k in range(2):
+                ts(sub(mw, 3 * k, 3 * k + 3), sub(res, 3 * k, 3 * k + 3), float(BE[l] + 48 * k), A.add)
+            L["c", l] = mw
+            copy("a", sub(v, 0, h), R("iot", BE[l], BE[l] + h))
+        else:
+            ts(mw, res, float(h - 1), A.min)
+            for a in range(0, h, 96):
+                scatter(sub(v, 0, h), sub(L["s", l], a // 16, a // 16 + 6), R("iot", BE[l] + a, BE[l] + a + 96))
+            row = tf(h)
+            act(row, sub(v, 0, h), F.Copy, off=mw)
+            L["c", l] = take("off", k16)
+            wrap(row, L["c", l])
+        ts(ow, sub(both, k16, 2 * k16), float(h), A.add)
+        act(sub(v, h, 2 * h), R("iot", 0, BE[l]), F.Copy, off=ow)
+        fl = tf(2 * h)
+        for a, k in [(0, 32), (32, 32), (64, 32), (96, 96)] if l == 2 else [(a, 96) for a in range(0, 2 * h, 96)]:
+            scatter(fl, sub(L["l", l], a // 16, (a + k) // 16), sub(v, a, a + k))
+        return fl
+
+    def parents(l, fw):
+        n = NS[l]
+        h = n // 2
+        z = tf(BE[l] + h)
+        for a in range(0, n, 96):
+            act(sub(z, a, a + 96), R("iot", 0, n), F.Copy, off=sub(L["l", l], a // 16, a // 16 + 6))
+        copy("a", sub(z, AV[l], AV[l] + h), sub(z, h, n))
+        if l == 2:
+            act(sub(z, BE[l], BE[l] + h), sub(z, 0, n), F.Copy, off=L["p", l])
+        else:
+            pr = tf(h)
+            act(pr, sub(z, 0, n), F.Copy, off=L["p", l])
+            act(sub(z, BE[l], BE[l] + h), pr, F.Copy, off=L["s", l])
+        for a in range(0, P >> l, 96):
+            act(R("pat", PAO[l] + a, PAO[l] + a + 96), z, F.Identity, bias=-96.0 if l == 2 else 0.0, off=sub(fw, a // 16, a // 16 + 6))
+
+    def down(l):
+        n, s = NS[l], "s%d" % l
+        h = n // 2
+        m = max(h, 128)
+        for b in range(4):
+            mm(4 + b, ET(b), R(s, h, h + m), True, False)
+        pick(R("pc", CO[l], CO[l] + h), R(s, 0, BE[l] + (128 if l == 2 else h)), L["c", l])
+        for b in range(4):
+            mm(4 + b, ET(b), R("pc", CO[l], CO[l] + m), False, True)
+        casts(h, 0.5)
+        quant(R(s, AV[l], AV[l] + m), R("ht", 0, 4 * m))
+        return R(s, 0, BE[l] + h)
+
+    up(0)
+    fl0 = children(0)
+    up(1)
+    fl1 = children(1)
+    up(2)
+    fl2 = children(2)
+    fw = [take("off", 24), take("off", 12), take("off", 6), take("off", 6)]
+    wrap(sub(fl2, 48, 144), fw[3])
+    pick(R("s1", BE[1], BE[1] + 96), down(2), fw[3])
+    wrap(sub(fl1, 96, 192), sub(fw[1], 6, 12))
+    wrap(sub(fl1, 0, 96), sub(fw[1], 0, 6))
+    win = down(1)
+    pick(R("dn1", 0, 96), win, sub(fw[1], 6, 12))
+    exchange([(R("dn1", 0, 96), R("s0", BE[0], BE[0] + 96))], PART[0], "ar2")
+    pick(R("s0", BE[0] + 96, BE[0] + 192), win, sub(fw[1], 0, 6))
+    wrap(sub(fl2, 96, 192), fw[2])
+    for a in (0, 192):
+        wrap(sub(fl0, a, a + 192), sub(fw[0], a // 16, a // 16 + 12))
+    for l in range(3):
+        parents(l, fw[l])
+    dma("g", T.pa[0:1, :], T.pat[0:1, :], [R("pat", 0, 672, p1=1)], [], "st3")
+    win = down(0)
+    for i, a in enumerate((0, 192)):
+        fin = R("fin", a, a + 192)
+        pick(fin, win, sub(fw[0], a // 16, a // 16 + 12))
+        mm(i, R("wq", 0, 128), fin)
+        copy("av"[i], R("yt", a, a + 192), bank(i, 0, 192))
+        dma("y", T.y[:, a:a + 192], T.yt[:, a:a + 192], [R("yt", a, a + 192)], [], "st1")
+    fin = R("fin", 0, P)
+    dma("g", T.oc[:, :], T.fin[:, 0:P].bitcast(dt.uint8), [fin], [], "st3")
+    for k in range(4):
+        dma("ayag"[k], T.osc[4 * k:4 * k + 4, :], T.fins[32 * k:32 * k + 4, 0:P], [sc(fin)], [], "st3" if k == 3 else "st1")
+
+    order = arrange(ops)
+    place = {j: i for i, j in enumerate(order)}
+    total = {}
+    for o in ops:
+        if o["sem"]:
+            total[o["sem"]] = total.get(o["sem"], 0) + o["inc"]
+    clock = {q: {} for q in queue}
+    for i in order:
+        o = ops[i]
+        o["need"], o["mark"], o["clk"] = [], False, {}
+        q = o["q"]
+        if q is None:
+            continue
+        want = {}
+        for j in o["pre"]:
+            key = ops[j]["sem"] or ops[j]["q"]
+            if not (key == q == "t"):
+                want[key] = max(want.get(key, -1), place[j])
+        for key, pj in sorted(want.items(), key=lambda kv: -kv[1]):
+            if clock[q].get(key, -1) >= pj:
+                continue
+            e = ops[order[pj]]
+            o["need"].append(e)
+            e["mark"] = True
+            for k2, p2 in list(e["clk"].items()) + [(key, len(ops) if e["sem"] else pj)]:
+                clock[q][k2] = max(clock[q].get(k2, -1), p2)
+        o["clk"] = dict(clock[q])
+    count = {q: 0 for q in queue}
+    for i in order:
+        o = ops[i]
+        q = o["q"]
+        if q is None:
+            continue
+        for e in o["need"]:
+            if e["sem"]:
+                queue[q].wait_ge(T.sem[e["sem"]], total[e["sem"]])
+            else:
+                queue[q].wait_ge(T.sem[e["q"]], e["n"])
+        ins = o["fn"]()
+        if o["sem"]:
+            if o["sem"] != "sent":
+                ins.then_inc(T.sem[o["sem"]], 16)
+        elif o["mark"]:
+            count[q] += 1
+            o["n"] = count[q]
+            ins.then_inc(T.sem[q], 1)
+    for s in ("sent", "st1", "st3"):
+        g.wait_ge(T.sem[s], total[s])

@@ -12,25 +12,25 @@ BE = [576, 320, 320]
 PPO = [576, 480, 384]
 CO = [0, 192, 288]
 PAO = [0, 384, 576]
-C16 = 201326592.0
 X4, U8, F32, BF, U16, I32 = "float8_e4m3fn_x4", "uint8", "float32", "bfloat16", "uint16", "int32"
 
 SCRATCH = {"ps": ("psum", [128, 4096], F32)}
-for _n, _w in (("f", 768), ("s0", 768), ("s1", 416), ("s2", 448), ("pc", 768), ("nw0", 224), ("nw1", 128), ("cq", 1280),
+for _n, _w in (("f", 768), ("s0", 768), ("s1", 416), ("s2", 448), ("pc", 768), ("nw0", 224), ("nw1", 128), ("cq", 1536),
                ("lq", 1152), ("sq", 1536), ("uq", 128), ("ur", 256), ("wq", 128), ("fin", 384), ("up0", 96), ("dn1", 96)):
     SCRATCH[_n] = ("sbuf", [128, _w], X4)
     SCRATCH[_n + "s"] = ("sbuf", [128, _w], U8)
 for _n, _w, _d in (("xt", 1536, BF), ("ut", 512, BF), ("wt", 512, BF), ("on", 512, BF), ("idn", 128, BF), ("cw", 512, BF),
+                   ("cx", 512, BF), ("tr", 512, BF),
                    ("et", 520, BF), ("eh", 520, BF), ("xp", 512, BF), ("xo", 512, BF), ("xl", 1536, BF), ("xm", 768, BF),
                    ("xk", 512, BF), ("xc", 512, BF), ("xn", 768, BF), ("ht", 896, BF), ("r16", 128, BF), ("qrow", 384, BF),
                    ("iot", 768, F32), ("pi", 2, I32), ("cc", 96, F32), ("wk0", 48, F32), ("wk", 384, F32), ("off", 320, U16),
-                   ("col", 320, F32), ("tf", 12288, F32), ("tb", 10240, BF), ("pat", 672, F32), ("yt", 384, F32)):
+                   ("col", 320, F32), ("tf", 12288, F32), ("tb", 12288, BF), ("pat", 672, F32), ("yt", 384, F32)):
     SCRATCH[_n] = ("sbuf", [128, _w], _d)
 
 SEMAPHORES = ["v", "a", "t", "g", "lx0", "lx1", "lx2", "lu", "lw", "sent", "ar0", "ar1", "ar2", "st1", "st3"]
 
-PM, FX, JA, JB, JC, Q96, OH, OHM, QW, KS, V16, FS, NM, OHN = 0, 1, 2, 5, 7, 8, 10, 16, 22, 34, 44, 56, 57, 58
-CYC, HOP, FAR = 0.001, 0.05, 2.0
+PM, FX, JA, JB, JC, Q96, OH, OHM, QW, KS, V16, NM, OHN = 0, 1, 2, 5, 7, 8, 10, 16, 22, 34, 44, 57, 58
+CYC, HOP, FAR = 0.0009, 0.17, 2.0
 PLANS, TRIES = {}, 2500
 
 
@@ -282,7 +282,7 @@ def rank_program(g, core, T, topo):
     def on(k, pb=128):
         return R("on", 0, k, p1=pb)
 
-    CW, ONES = R("cq", 0, 128), R("cq", 128, 256)
+    CW, ONES, CX, TR = R("cq", 0, 128), R("cq", 128, 256), R("cq", 1280, 1408), R("cq", 1408, 1536)
 
     def ET(b):
         return R("cq", 256 + 128 * b, 384 + 128 * b)
@@ -302,7 +302,6 @@ def rank_program(g, core, T, topo):
     select(R("cw", 0, 512, 4), on(128), [[1, 128]], A.is_ge, 0, -1)
     iota(R("qrow", 0, 384), [[1, 384]], -192, 0)
     iota(cc(JA, 3), [[128, 3]], 1 - 192, 1)
-    ts(cc(JA, 3), cc(JA, 3), -0.5, A.add)
     iota(cc(JB, 2), [[96, 2]], 1 - 96, 1)
     iota(cc(JC, 1), [[0, 1]], 1 - 48, 1)
     memset(R("et", 0, 520), 0.0)
@@ -334,7 +333,6 @@ def rank_program(g, core, T, topo):
     ts(R("wk0", 16, 32), R("r16", 0, 16), cc(PM), A.is_le, -4096.0, A.mult)
     ts(R("wk0", 32, 48), R("r16", 0, 16), cc(PM), A.subtract, 1.0, A.is_equal)
     ts(cc(FX), cc(PM), 14.5, A.is_lt, 2048.0, A.mult)
-    act(cc(FS), cc(FX), F.Identity, bias=-float(P))
     copy("a", R("wk0", 32, 48), R("wk0", 32, 48), scale=2048.0)
     tt(R("wk0", 0, 16), R("wk0", 16, 32), R("wk0", 32, 48), A.add)
     memset(sub(o_u, 0, 8), 0)
@@ -342,7 +340,16 @@ def rank_program(g, core, T, topo):
     act(R("wk", 0, 384), R("wk0", 0, 16), F.Copy, off=o_pm)
     quant(CW, R("cw", 0, 512))
     ts(cc(OH, 6), cc(V16, 6), cc(PM), A.add, 0.0, A.is_equal)
-    ts(cc(OHM, 6), cc(OH, 6), 1024.0, A.mult, -C16 - 1024.0, A.add)
+    ts(cc(OHM, 6), cc(OH, 6), 1008.0, A.mult, -1024.0, A.add)
+    copy("a", cc(OHN, 6), cc(OH, 6), scale=-16.0)
+    act(R("cx", 0, 512, 4), R("cw", 0, 512, 4), F.Identity, bias=-1.0)
+    fill(R("cx", 1, 512, 4), -1.0)
+    copy("a", R("cx", 2, 512, 4), R("cw", 0, 512, 4))
+    fill(R("cx", 3, 512, 4), 1.0)
+    quant(CX, R("cx", 0, 512))
+    fill(R("tr", 0, 512), 0.0)
+    select(R("tr", 0, 512, 4), on(128), [[1, 128]], A.is_ge, -16, -1)
+    quant(TR, R("tr", 0, 512))
     for b in range(4):
         quant(ET(b), R("et", 3 - b, 515 - b))
         ops[-1]["by"] = 3.0
@@ -356,16 +363,12 @@ def rank_program(g, core, T, topo):
     quant(R("s2", 192, 320), on(512))
     quant(R("wq", 0, 128), R("wt", 0, 512))
     copy("a", cc(NM), cc(PM), scale=-1.0)
-    act(cc(OHN, 3), cc(OHM, 3), F.Identity, bias=48.0)
 
-    def wrap(src, out, signs=False):
+    def wrap(src, out):
         n = width(src)
         ws = tf(n)
         scan(ws, R("wk", 0, n), src, 0.0, A.add, A.max)
-        if signs:
-            ts(out, sub(ws, 15, n, 16), cc(FS), A.subtract, 0.5, A.mult)
-        else:
-            ts(out, sub(ws, 15, n, 16), cc(FX), A.subtract)
+        ts(out, sub(ws, 15, n, 16), cc(FX), A.subtract)
 
     def half(n, K, pb, rows, vals, tile, apart=False, turned=False):
         h = n // 2
@@ -374,77 +377,91 @@ def rank_program(g, core, T, topo):
         a = sub(run, h - 1, h - 1 + K)
         xp = take("xp", 48, pb)
         c0 = xp[3] // 4
-        for k in range(K - 1, -1, -1):
-            sg = tb(n, pb)
-            act(sg, rows[k], F.Sign, bias=vals[k], scale=-1.0, acc=one(s, k))
-            if k == 0 and K > 1 and not apart and rows[k][0] != "ps":
-                eq = tb(n, pb)
-                ts(eq, rows[k], vals[k], A.is_equal)
-                scan(sub(run, 0, h), sub(eq, 0, h), sub(eq, h, n), -float(n), A.add, A.add)
-            else:
-                minus_abs_sum(one(a, k), sg)
-        act(sb, s, F.Identity, bias=0.5 - n)
-        act(sn, s, F.Identity, bias=0.5 - n, scale=-1.0)
+        sq = take("sq", 128)
         if K == 1:
-            ts(sub(xp, 0, 6, 5), on(2, pb), sb, A.mult, a, A.is_lt)
+            above = []
+            for cmp in (A.is_ge, A.is_gt):
+                fl, cs = tb(n, pb), tf(h, pb)
+                ts(fl, rows[0], vals[0], cmp)
+                scan(cs, sub(fl, 0, h), sub(fl, h, n), 0.0, A.add, A.add)
+                above.append(one(cs, h - 1))
         else:
+            for k in range(K - 1, -1, -1):
+                sg = tb(n, pb)
+                act(sg, rows[k], F.Sign, bias=vals[k], scale=-1.0, acc=one(s, k))
+                if k == 0 and not apart and rows[k][0] != "ps":
+                    eq = tb(n, pb)
+                    ts(eq, rows[k], vals[k], A.is_equal)
+                    scan(sub(run, 0, h), sub(eq, 0, h), sub(eq, h, n), -float(n), A.add, A.add)
+                else:
+                    minus_abs_sum(one(a, k), sg)
+            act(sb, s, F.Identity, bias=0.5 - n)
+            act(sn, s, F.Identity, bias=0.5 - n, scale=-1.0)
+        if K == 3:
             tt(sub(xp, 0, 4 * K, 4), sb, a, A.is_lt)
-        tt(sub(xp, 20, 20 + 4 * K, 4), sn, a, A.is_gt)
-        if K == 1:
-            fill(one(xp, 21), -h / pb)
-        elif apart:
-            fill(sub(xp, 21, 21 + 4 * K, 4), -h / pb)
-            tt(sub(xp, 4 * K + 1, 8 * K + 1, 4), sb, a, A.is_lt)
-        else:
+            tt(sub(xp, 20, 20 + 4 * K, 4), sn, a, A.is_gt)
             fill(one(xp, 16), -h / pb)
             scan(sub(xp, 5, 41, 4), cc(KS, 9, pb), sub(xp, 0, 36, 4), 0.0, A.mult, A.add)
-        sq = take("sq", 128)
-        quant(sq, R("xp", 0, 512))
-        mm(3, CW, sq)
-        for k in range(K):
-            t = c0 + K + (k if apart else 0)
-            ts(one(cn, k), bank(3, c0 + k, c0 + k + 1, pb), bank(3, t, t + 1, pb), A.subtract, bank(3, c0 + 5 + k, c0 + 6 + k, pb), A.max)
+            quant(sq, R("xp", 0, 512))
+            mm(3, CW, sq)
+            for k in range(K):
+                ts(one(cn, k), bank(3, c0 + k, c0 + k + 1, pb), bank(3, c0 + K, c0 + K + 1, pb), A.subtract, bank(3, c0 + 5 + k, c0 + 6 + k, pb), A.max)
+        else:
+            fill(sub(xp, 9, 9 + 4 * K, 4), h / pb)
+            if K == 1:
+                ts(one(xp, 0), above[0], h + 0.5, A.is_gt)
+                ts(one(xp, 10), above[1], h - 0.5, A.is_gt)
+            elif apart:
+                tt(sub(xp, 0, 8, 4), sb, a, A.is_lt)
+                tt(sub(xp, 10, 18, 4), sn, a, A.is_gt)
+            else:
+                ts(sub(xp, 1, 5, 3), on(2, pb), one(sb, 1), A.mult, one(a, 1), A.is_lt)
+                ts(one(xp, 14), one(sn, 1), one(a, 1), A.is_gt)
+                ts(one(xp, 0), one(sb, 0), one(a, 0), A.is_lt)
+                ts(sub(xp, 10, 16, 5), on(2, pb), one(sn, 0), A.mult, one(a, 0), A.is_gt)
+            quant(sq, R("xp", 0, 512))
+            mm(3, CX, sq)
+            for k in range(K):
+                ts(one(cn, k), bank(3, c0 + k, c0 + k + 1, pb), bank(3, c0 + 2 + k, c0 + 3 + k, pb), A.max)
         q = [R("qrow", 192 - h, 192, p1=pb), R("qrow", 192, 192 + h, p1=pb)]
         tot = n * K if apart else n
         out = take("off", tot // 16)
-        if h >= 128:
-            cj = take("col", K, pb)
-            tt(cj, cn, cc(JA, K), A.subtract)
         for side in ((1, 0) if turned else (0, 1)):
             for k in range(K):
                 e = 4 * ((side ^ turned) * tot // 2 + (h * k if apart else 0)) + k
                 x = R(tile, e, e + 4 * h - k, 4, p1=pb)
                 if side == 0:
                     ts(x, q[0], one(cn, k), A.is_ge)
-                elif h >= 128:
-                    act(x, q[1], F.Sign, bias=one(cj, k))
                 else:
-                    ts(x, q[1], one(cn, k), A.add, cc({96: JB, 48: JC}[h] + (0 if apart else k), 1, pb), A.is_ge)
+                    ts(x, q[1], one(cn, k), A.add, cc({192: JA, 96: JB, 48: JC}[h] + (0 if apart else k), 1, pb), A.is_ge)
         cuts = [(0, h), (h, n)] if h >= 128 else [(0, tot)]
         for i, (a0, a1) in enumerate(cuts):
             m = max(a1 - a0, 128)
             lq = take("lq", m)
             quant(lq, R(tile, 4 * a0, 4 * (a0 + m)))
             mm(i, ONES, lq)
-            wrap(bank(i, 0, a1 - a0), sub(out, a0 // 16, a1 // 16), signs=i == 1)
+            wrap(bank(i, 0, a1 - a0), sub(out, a0 // 16, a1 // 16))
         return out
 
-    def spread(cnt, K, pb, tile, b, more=0, under=None, step=0.0):
-        t, nl, has = take("col", K, pb), take("col", K, pb), take("col", K, pb)
+    def count(src, func, bias, scale, cnt, hi):
+        n, pb = width(src), src[2]
+        act(tb(n, pb), src, func, bias=bias, scale=scale, acc=cnt)
+        act(tb(n // 16, pb), sub(src, 15, n, 16), func, bias=bias, scale=scale, acc=hi)
+
+    def spread(cnt, hi, K, pb, tile, b, under=None, step=0.0):
+        has = take("col", K, pb)
         G = pb // 16
         xp = take(tile, 4 * K * G * (2 if under else 1), pb)
-        ts(t, cnt, -7.5, A.add, C16, A.add)
         if under:
             ts(has, cnt, under, A.is_lt, step, A.mult)
             act(sub(xp, 4 * K * G + 1, 8 * K * G, 4, 0, 32), cc(QW, K * G, 32), F.Copy, scale=1 / 32)
         for k in range(K):
             e = 4 * G * k
-            act(sub(xp, e + 2, e + 4 * G, 4), cc(OHN if more and k else OHM, G, pb), F.Relu, bias=one(t, k))
-            ts(one(nl, k), one(t, k), C16, A.subtract, one(cnt, k), A.subtract)
-            ts(sub(xp, e + 3, e + 4 * G, 4), cc(OH, G, pb), one(nl, k), A.mult)
+            act(sub(xp, e + 2, e + 4 * G, 4), cc(OHM, G, pb), F.Relu, bias=one(cnt, k), scale=one(hi, k))
+            ts(sub(xp, e + 3, e + 4 * G, 4), cc(OHN, G, pb), one(hi, k), A.mult)
             if under:
                 e += 4 * K * G
-                act(sub(xp, e + 2, e + 4 * G, 4), cc(OH, G, pb), F.Copy, scale=one(has, k))
+                ts(sub(xp, e + 2, e + 4 * G, 4), cc(OH, G, pb), one(has, k), A.mult)
                 act(sub(xp, e + 3, e + 4 * G, 4), cc(OH, G, pb), F.Copy, scale=cc(NM, 1, pb))
         sq = take("sq", 128)
         quant(sq, R(tile, 0, 512))
@@ -466,24 +483,22 @@ def rank_program(g, core, T, topo):
         for k in range(K):
             win = R("f", fo + pb * k, fo + pb * k + 128)
             mm(k, win, win)
-        d, xb, row = take("col", K, pb), tf(w, pb), tf(n, pb)
+        d, xb, row, vals = take("col", K, pb), tf(w, pb), tf(n, pb), []
         for k in range(K):
             mk = tf(pb + 32, pb)
             tt(sub(mk, 0, pb), bank(k, 0, pb, pb), R("idn", 0, pb, p1=pb), A.mult)
-            if k < K - 1:
+            if k < K - 1 and l == 0:
+                vals.append(one(d, k))
                 act(tb(pb, pb), sub(mk, 0, pb), F.Copy, acc=one(d, k))
                 act(sub(xb, 32 * k, 32 * k + 32), on(32, pb), F.Copy, scale=one(d, k))
             else:
                 fill(sub(mk, pb, pb + 32), 0.0)
                 last = tf(pb + 32, pb)
                 scan(last, mk, mk, 0.0, A.max, A.max)
-        vals = [one(d, k) for k in range(K - 1)] + [one(last, pb + 31)]
-        if l < 2:
-            turn(sub(row, w - 32, w), sub(last, pb, pb + 32))
+                vals.append(one(last, pb + 31))
+                turn(sub(row, 32 * k, 32 * k + 32) if l < 2 else sub(row, k, w, 2), sub(last, pb, pb + 32))
+        if l == 0:
             turn(sub(row, 0, w - 32), sub(xb, 0, w - 32))
-        else:
-            turn(sub(row, 1, w, 2), sub(last, pb, pb + 32))
-            turn(sub(row, 0, w, 2), sub(xb, 0, 32))
         if pb == 128:
             for q in range(4):
                 copy("va"[q & 1], sub(row, w, 2 * w, 1, 32 * q, 32 * q + 32), sub(row, 0, w, 1, 32 * (q ^ 1), 32 * (q ^ 1) + 32))
@@ -505,19 +520,21 @@ def rank_program(g, core, T, topo):
         else:
             pick(R(s, 0, n), R("f", fo, fo + n), lw)
         K, pb, hp = [(2, 96, 192), (1, 96, 96), (2, 48, 48)][l]
-        par = take("col", K, pb)
+        par, hi = take("col", K, pb), take("col", K, pb)
         for k in range(K):
             a = h + (hp * k if l == 2 else 0)
             mm(k, R(s, pb * k, pb * k + 128), R(s, a, a + m))
-            rm = tf(hp, pb)
-            scan(rm, bank(k, 0, hp, pb), on(hp, pb), -1e29, A.max, A.mult)
-            act(tb(hp, pb), rm, F.Sign, bias=one(rm, hp - 1), scale=-1.0, acc=one(par, k))
+            pad = 64 if l == 2 and k else 16
+            rm = tf(pad + hp, pb)
+            fill(sub(rm, 0, pad), -1e29)
+            scan(sub(rm, pad, pad + hp), bank(k, 0, hp, pb), on(hp, pb), -1e29, A.max, A.mult)
+            count(rm, F.Sign, one(rm, pad + hp - 1), -1.0, one(par, k), one(hi, k))
         L["par", l] = par
         for b in range(4):
             mm(4 + b, ET(b), R(s, 0, m), True, False)
         pw = take("off", h // 16)
         L["p", l] = pw
-        ts(pw, spread(par, K, pb, "xp", 3, more=l == 2), float(h), A.add)
+        ts(pw, spread(par, hi, K, pb, "xp", 3), float(h - 16), A.add)
         pick(R("pc", PPO[l], PPO[l] + h), R(s, 0, n), pw)
         for b in range(4):
             mm(4 + b, EH(b), R("pc", PPO[l], PPO[l] + m), False, True)
@@ -532,9 +549,10 @@ def rank_program(g, core, T, topo):
             mm(1 + k, R(nw, pb * k, pb * k + 128), ur)
         mm(0, ur, R(nw, 0, m))
         sv = take("col", K, pb)
-        for k in range(K):
+        for k in range(K if l == 0 else 0):
             copy("va"[k], one(sv, k), bank(1 + k, 0, 1, pb))
-        both = half(h, K, pb, [bank(0, 0, h, pb)] * K, [one(sv, k) for k in range(K)], "xm" if l == 0 else "xk", turned=True)
+        vals = [one(sv, k) for k in range(K)] if l == 0 else [bank(1, 0, 1, pb)]
+        both = half(h, K, pb, [bank(0, 0, h, pb)] * K, vals, "xm" if l == 0 else "xk", turned=True)
         L["s", l] = both
         q, fo = h // 2, FO[l + 1]
         if l == 0:
@@ -548,31 +566,32 @@ def rank_program(g, core, T, topo):
     def children(l):
         h = NS[l] // 2
         K, pb, k16 = h // 96, 96, h // 16
-        prow, cnt = tb(h), take("col", K, pb)
+        prow, cnt, hi = tb(h), take("col", K, pb), take("col", K, pb)
         if l == 2:
             for k in range(2):
-                ts(R("xc", 192 * k, 192 * k + 192, 4, p1=48), R("qrow", 192, 240, p1=48), one(L["par", l], k), A.is_equal)
+                ts(R("xc", 192 * k, 192 * k + 192, 4, p1=48), R("qrow", 208 + 48 * k, 256 + 48 * k, p1=48), one(L["par", l], k), A.is_equal)
             sq = take("sq", 128)
             quant(sq, R("xc", 0, 512))
-            mm(2, sq, CW)
-            act(tb(48, pb), bank(2, 0, 48, pb), F.Relu, bias=1.0, scale=-1.0, acc=cnt)
+            mm(2, sq, TR)
+            count(bank(2, 0, 64, pb), F.Relu, 1.0, -1.0, cnt, hi)
         else:
             act(prow, R("iot", 0, 2 * h), F.Identity, bias=-float(h), off=L["p", l])
         for k in range(K if l < 2 else 0):
-            ne, cp = tb(h, pb), tb(h, pb)
+            ne, cp = tb(h, pb), tb(h + 16, pb)
+            fill(sub(cp, 0, 16), 1.0)
             ts(ne, sub(prow, 0, h, 1, 0, pb), cc(Q96 + k, 1, pb), A.not_equal)
-            scan(cp, ne, ne, 1.0, A.mult, A.mult)
-            act(tb(h, pb), cp, F.Copy, acc=one(cnt, k))
-        both = spread(cnt, K, pb, "xo", 2, under=(h if l < 2 else 48) - 0.5, step=float(AV[l] - h))
+            scan(sub(cp, 16, h + 16), ne, ne, 1.0, A.mult, A.mult)
+            count(cp, F.Copy, 0.0, 1.0, one(cnt, k), one(hi, k))
+        both = spread(cnt, hi, K, pb, "xo", 2, under=(h if l < 2 else 48) + 15.5, step=float(AV[l] - h))
         res = sub(both, 0, k16)
         mw, ow, v = take("off", k16), take("off", k16), tf(2 * h)
         if l == 2:
             for k in range(2):
-                ts(sub(mw, 3 * k, 3 * k + 3), sub(res, 3 * k, 3 * k + 3), float(BE[l] + 48 * k), A.add)
+                ts(sub(mw, 3 * k, 3 * k + 3), sub(res, 3 * k, 3 * k + 3), float(BE[l] + 48 * k - 16), A.add)
             L["c", l] = mw
             copy("a", sub(v, 0, h), R("iot", BE[l], BE[l] + h))
         else:
-            ts(mw, res, float(h - 1), A.min)
+            ts(mw, res, -16.0, A.add, float(h - 1), A.min)
             for a in range(0, h, 96):
                 scatter(sub(v, 0, h), sub(L["s", l], a // 16, a // 16 + 6), R("iot", BE[l] + a, BE[l] + a + 96))
             row = tf(h)
@@ -637,12 +656,12 @@ def rank_program(g, core, T, topo):
         parents(l, fw[l])
     dma("g", T.pa[0:1, :], T.pat[0:1, :], [R("pat", 0, 672, p1=1)], [], "st3")
     win = down(0)
-    for i, a in enumerate((0, 192)):
-        fin = R("fin", a, a + 192)
-        pick(fin, win, sub(fw[0], a // 16, a // 16 + 12))
+    for i, (a, b) in enumerate(((0, 256), (256, P))):
+        fin = R("fin", a, b)
+        pick(fin, win, sub(fw[0], a // 16, b // 16))
         mm(i, R("wq", 0, 128), fin)
-        copy("av"[i], R("yt", a, a + 192), bank(i, 0, 192))
-        dma("y", T.y[:, a:a + 192], T.yt[:, a:a + 192], [R("yt", a, a + 192)], [], "st1")
+        copy("av"[i], R("yt", a, b), bank(i, 0, b - a))
+        dma("y", T.y[:, a:b], T.yt[:, a:b], [R("yt", a, b)], [], "st1")
     fin = R("fin", 0, P)
     dma("g", T.oc[:, :], T.fin[:, 0:P].bitcast(dt.uint8), [fin], [], "st3")
     for k in range(4):
@@ -675,7 +694,7 @@ def rank_program(g, core, T, topo):
             for k2, p2 in list(e["clk"].items()) + [(key, len(ops) if e["sem"] else pj)]:
                 clock[q][k2] = max(clock[q].get(k2, -1), p2)
         o["clk"] = dict(clock[q])
-    count = {q: 0 for q in queue}
+    count_of = {q: 0 for q in queue}
     for i in order:
         o = ops[i]
         q = o["q"]
@@ -691,8 +710,8 @@ def rank_program(g, core, T, topo):
             if o["sem"] != "sent":
                 ins.then_inc(T.sem[o["sem"]], 16)
         elif o["mark"]:
-            count[q] += 1
-            o["n"] = count[q]
+            count_of[q] += 1
+            o["n"] = count_of[q]
             ins.then_inc(T.sem[q], 1)
     for s in ("sent", "st1", "st3"):
         g.wait_ge(T.sem[s], total[s])

@@ -6,32 +6,36 @@ F = ActivationFunctionType
 P = 384
 PART = [2, 1]
 NS = [384, 192, 192]
-FO = [384, 192, 0]
 AV = [384, 192, 192]
 BE = [576, 320, 320]
+SO = [0, 0, 320]
 PPO = [576, 480, 384]
 CO = [0, 192, 288]
 PAO = [0, 384, 576]
+UW = [384, 384, 352]
+WO = [0, 16, 34, 50]
 X4, U8, F32, BF, U16, I32 = "float8_e4m3fn_x4", "uint8", "float32", "bfloat16", "uint16", "int32"
 
 SCRATCH = {"ps": ("psum", [128, 4096], F32)}
-for _n, _w in (("f", 768), ("s0", 768), ("s1", 416), ("s2", 448), ("pc", 768), ("nw0", 224), ("nw1", 128), ("cq", 1536),
-               ("lq", 1152), ("sq", 1536), ("uq", 128), ("ur", 256), ("wq", 128), ("fin", 384), ("up0", 96), ("dn1", 96)):
+for _n, _w in (("f", 512), ("s0", 768), ("s1", 768), ("pc", 768), ("nw0", 512), ("nwb", 224), ("nw1", 352), ("cq", 1536),
+               ("lq", 1280), ("sq", 1536), ("uq", 128), ("uv", 32), ("ur", 512), ("wq", 128), ("fin", 384), ("dn1", 96),
+               ("ca", 416), ("cb", 256), ("wv", 360)):
     SCRATCH[_n] = ("sbuf", [128, _w], X4)
     SCRATCH[_n + "s"] = ("sbuf", [128, _w], U8)
 for _n, _w, _d in (("xt", 1536, BF), ("ut", 512, BF), ("wt", 512, BF), ("on", 512, BF), ("idn", 128, BF), ("cw", 512, BF),
-                   ("cx", 512, BF), ("tr", 512, BF),
+                   ("cx", 512, BF), ("tr", 512, BF), ("wkd", 160, BF), ("mt", 288, BF), ("tm", 96, BF), ("cm", 132, BF),
                    ("et", 520, BF), ("eh", 520, BF), ("xp", 512, BF), ("xo", 512, BF), ("xl", 1536, BF), ("xm", 768, BF),
-                   ("xk", 512, BF), ("xc", 512, BF), ("xn", 768, BF), ("ht", 896, BF), ("r16", 128, BF), ("qrow", 384, BF),
-                   ("iot", 768, F32), ("pi", 2, I32), ("cc", 96, F32), ("wk0", 48, F32), ("wk", 384, F32), ("off", 320, U16),
-                   ("col", 320, F32), ("tf", 12288, F32), ("tb", 12288, BF), ("pat", 672, F32), ("yt", 384, F32)):
+                   ("xk", 512, BF), ("xc", 512, BF), ("xn", 768, BF), ("xs", 1152, BF), ("xa", 1664, BF), ("xb", 1024, BF),
+                   ("xw", 1440, BF), ("ht", 1024, BF), ("r16", 128, BF), ("qrow", 384, BF),
+                   ("iot", 768, F32), ("pi", 2, I32), ("cc", 96, F32), ("wk0", 48, F32), ("wk", 384, F32), ("off", 384, U16),
+                   ("col", 384, F32), ("tf", 20480, F32), ("tb", 16384, BF), ("pat", 672, F32), ("yt", 384, F32)):
     SCRATCH[_n] = ("sbuf", [128, _w], _d)
 
-SEMAPHORES = ["v", "a", "t", "g", "lx0", "lx1", "lx2", "lu", "lw", "sent", "ar0", "ar1", "ar2", "st1", "st3"]
+SEMAPHORES = ["v", "a", "t", "g", "lx0", "lx1", "lx2", "lu", "lw", "sent", "aru", "ar0", "ar1", "ar2", "st1", "st3"]
 
-PM, FX, JA, JB, JC, Q96, OH, OHM, QW, KS, V16, NM, OHN = 0, 1, 2, 5, 7, 8, 10, 16, 22, 34, 44, 57, 58
+PM, FX, JA, JB, Q96, OH, OHM, QW, KS, V16, NM, OHN = 0, 1, 2, 5, 8, 10, 16, 22, 34, 44, 57, 58
 CYC, HOP, FAR = 0.0009, 0.17, 2.0
-PLANS, TRIES = {}, 2500
+PLANS, TRIES = {}, 3000
 
 
 def R(name, c0, c1, step=1, p0=0, p1=128):
@@ -111,31 +115,50 @@ def arrange(ops):
         return sorted(range(n), key=lambda k: (start[k], k))
 
     def span(order):
-        tot = 0.0
+        tot, held = 0.0, []
         for slow in ("", "v", "a", "t"):
-            free, end = {}, [0.0] * n
+            free, last, end, why = {}, {}, [0.0] * n, [None] * n
             for i in order:
-                o = ops[i]
-                t = max([end[j] + d for j, d in gap[i]] + [free.get(o["q"], 0.0)])
-                end[i] = t + o["c"] * (1.2 if o["q"] == slow else 1.0)
-                if o["q"]:
-                    free[o["q"]] = end[i]
-            tot += max(end[i] + ops[i]["lat"] for i in order)
-        return tot
+                q, t = queues[i], 0.0
+                for j, d in gap[i]:
+                    if end[j] + d > t:
+                        t, why[i] = end[j] + d, j
+                if free.get(q, 0.0) > t:
+                    t, why[i] = free[q], -1 - last[q]
+                end[i] = t + ops[i]["c"] * (1.2 if q == slow else 1.0)
+                if q:
+                    free[q], last[q] = end[i], i
+            i = max(order, key=lambda k: end[k] + ops[k]["lat"])
+            tot += end[i] + ops[i]["lat"]
+            while why[i] is not None:
+                j = why[i]
+                if j < 0:
+                    j = -1 - j
+                    held.append((j, i))
+                i = j
+        return tot, held
 
     if n not in PLANS:
+        queues = [o["q"] for o in ops]
         bonus, seed = [0.0] * n, 1
         best = plan(bonus)
-        least = span(best)
+        least, held = span(best)
         for turn in range(TRIES):
             other = list(bonus)
-            for k in range(6):
+            for k in range(3):
                 seed = (seed * 1103515245 + 12345) % 2147483648
-                other[seed // 64 % n] = (seed // 65536 % 9 - 4) * (0.5 if k & 1 else 2.0)
+                j, i = held[seed // 64 % len(held)]
+                step = (1 + seed // 65536 % 4) * (0.15 if seed // 1024 & 1 else 0.6)
+                if k == 2:
+                    other[seed // 64 % n] = (seed // 65536 % 9 - 4) * 0.5
+                elif seed // 4096 & 1:
+                    other[j] -= step
+                else:
+                    other[i] += step
             order = plan(other)
-            t = span(order)
+            t, now = span(order)
             if t <= least:
-                bonus, best, least = other, order, t
+                bonus, best, least, held = other, order, t, now
         PLANS[n] = best
     return PLANS[n]
 
@@ -187,7 +210,7 @@ def rank_program(g, core, T, topo):
         op("v", lambda: g.vector.tensor_tensor(ap(out), ap(a), ap(b), o), [a, b], [out], cyc(width(out) * (1 if a[0] == "ps" else 2)))
 
     def scan(out, d0, d1, init, o0, o1):
-        op("v", lambda: g.vector.tensor_tensor_scan(ap(out), ap(d0), ap(d1), init, o0, o1), [d0, d1], [out], cyc(width(out), out, d0, d1))
+        op("v", lambda: g.vector.tensor_tensor_scan(ap(out), ap(d0), ap(d1), ap(init), o0, o1), [d0, d1, init], [out], cyc(width(out), out, d0, d1))
 
     def turn(out, in_):
         op("v", lambda: g.vector.transpose(ap(out), ap(in_)), [in_], [out], cyc(width(out)))
@@ -232,30 +255,32 @@ def rank_program(g, core, T, topo):
         else:
             op("g", lambda: g.iota(ap(out), pattern, base, cm), [], [out], 0.13 + 2 * CYC * width(out))
 
-    def select(out, in_, pattern, cmp, base, cm):
-        op("g", lambda: g.affine_select(ap(out), ap(in_), pattern, cmp, 0.0, base, cm), [in_], [out], 0.17 + 2 * CYC * width(out))
+    def select(out, in_, pattern, cmp, base, cm, other=0.0):
+        op("g", lambda: g.affine_select(ap(out), ap(in_), pattern, cmp, other, base, cm), [in_], [out], 0.17 + 2 * CYC * width(out))
 
     def dma(q, out, in_, reads, writes, sem):
         op(q, lambda: queue[q].dma_start(out, in_), reads, writes, 0.06, FAR, sem=sem, inc=16)
 
-    def exchange(pairs, part, sem):
-        other = T.cores[rank ^ part]
-        rid, pid = topo.addr(other)[:2]
-        eng = topo.engines(core, other)
-        per = len(eng) // (2 * len(pairs))
-        calls = []
+    def exchange(items, sem):
+        calls, total = [], 0
         for kind in range(2):
-            sides = [(s, d) if kind == 0 else (sc(s), sc(d)) for s, d in pairs]
-            masks = [sum(1 << e for e in eng[per * (kind * len(pairs) + i):][:per]) for i in range(len(pairs))]
+            sides = []
+            for i, (s, d, part) in enumerate(items):
+                other = T.cores[rank ^ part]
+                eng = topo.engines(core, other)
+                per = len(eng) // len(items)
+                total += per
+                sides.append(((s, d) if kind == 0 else (sc(s), sc(d))) + (topo.addr(other)[:2], sum(1 << e for e in eng[per * i:][:per])))
 
-            def fn(kind=kind, sides=sides, masks=masks):
-                raw = [(ap(s).bitcast(dt.uint8), ap(d).bitcast(dt.uint8)) if kind == 0 else (ap(s), ap(d)) for s, d in sides]
+            def fn(kind=kind, sides=sides):
+                raw = [(ap(s).bitcast(dt.uint8), ap(d).bitcast(dt.uint8), at, m) if kind == 0 else (ap(s), ap(d), at, m) for s, d, at, m in sides]
                 if len(raw) == 1:
-                    return g.remote_dma(raw[0][1], raw[0][0], T.sem[sem], T.sem.sent, pid, rid, masks[0])
-                return g.remote_dma_fused([RemoteDMATransfer(dst_ids=[DstId(rid=rid, pnc=pid)], dma_engine_mask=m, remote_sem=T.sem[sem], src=s, dst=d)
-                                           for (s, d), m in zip(raw, masks)], local_sem=T.sem.sent)
-            calls.append(op("g", fn, [s for s, d in sides], [], 0.2, FAR, sem="sent", inc=per * len(pairs)))
-        op(None, None, [], [d for s, d in pairs] + [sc(d) for s, d in pairs], 0.0, sem=sem, inc=2 * per * len(pairs), after=calls)
+                    s, d, at, m = raw[0]
+                    return g.remote_dma(d, s, T.sem[sem], T.sem.sent, at[1], at[0], m)
+                return g.remote_dma_fused([RemoteDMATransfer(dst_ids=[DstId(rid=at[0], pnc=at[1])], dma_engine_mask=m, remote_sem=T.sem[sem], src=s, dst=d)
+                                           for s, d, at, m in raw], local_sem=T.sem.sent)
+            calls.append(op("g", fn, [x[0] for x in sides], [], 0.2, FAR, sem="sent", inc=per * len(items)))
+        op(None, None, [], [x[1] for x in items] + [sc(x[1]) for x in items], 0.0, sem=sem, inc=total, after=calls)
 
     used = {}
 
@@ -282,6 +307,10 @@ def rank_program(g, core, T, topo):
     def on(k, pb=128):
         return R("on", 0, k, p1=pb)
 
+    def zeros(name, a, b):
+        for c in range(a, b, 256):
+            fill(R(name, c, min(b, c + 256)), 0.0)
+
     CW, ONES, CX, TR = R("cq", 0, 128), R("cq", 128, 256), R("cq", 1280, 1408), R("cq", 1408, 1536)
 
     def ET(b):
@@ -292,18 +321,20 @@ def rank_program(g, core, T, topo):
 
     for k in range(3):
         dma("yay"[k], T.xt[:, 512 * k:512 * k + 512], T.x[:, 512 * k:512 * k + 512], [], [R("xt", 512 * k, 512 * k + 512)], "lx%d" % k)
-        quant(R("f", FO[0] + 128 * k, FO[0] + 128 * k + 128), R("xt", 512 * k, 512 * k + 512))
+        quant(R("f", 128 * k, 128 * k + 128), R("xt", 512 * k, 512 * k + 512))
     dma("y", T.ut[:], T.u[:], [], [R("ut", 0, 512)], "lu")
     dma("y", T.wt[:], T.w[:], [], [R("wt", 0, 512)], "lw")
     memset(on(512), 1.0)
+    quant(R("f", 384, 512), on(512))
+    select(R("wkd", 0, 160), on(160), [[1, 160]], A.is_ge, -2, -1)
+    select(R("wkd", 0, 160), R("wkd", 0, 160), [[1, 160]], A.not_equal, -1, -1, 2.0 ** 60)
     iota(R("pi", 0, 1), [[0, 1]], 0, 1, small=False)
     iota(R("r16", 0, 128), [[0, 8], [1, 16]], 0, 0)
     select(R("idn", 0, 128), on(128), [[-1, 128]], A.is_equal, 0, 1)
     select(R("cw", 0, 512, 4), on(128), [[1, 128]], A.is_ge, 0, -1)
     iota(R("qrow", 0, 384), [[1, 384]], -192, 0)
     iota(cc(JA, 3), [[128, 3]], 1 - 192, 1)
-    iota(cc(JB, 2), [[96, 2]], 1 - 96, 1)
-    iota(cc(JC, 1), [[0, 1]], 1 - 48, 1)
+    iota(cc(JB, 2), [[96, 2]], 1, 1)
     memset(R("et", 0, 520), 0.0)
     copy("a", R("et", 3, 512, 4), R("idn", 0, 128))
     fill(R("eh", 0, 260), 0.0)
@@ -313,13 +344,17 @@ def rank_program(g, core, T, topo):
     iota(cc(Q96, 2), [[96, 2]], 0, 1)
     iota(cc(QW, 12), [[16, 12]], 0, 0)
     iota(R("iot", 0, 768), [[1, 768]], 0, 0)
-    for name, w in (("xp", 512), ("xo", 512), ("xk", 512), ("xc", 512), ("xm", 768), ("xn", 768)):
-        for a in range(0, w, 256):
-            fill(R(name, a, a + 256), 0.0)
-    fill(R("xn", 192, 384, 4, p1=96), 1.0)
-    fill(R("xn", 576, 768, 4, p1=96), 1.0)
+    for name, w in (("xp", 512), ("xo", 512), ("xk", 512), ("xc", 512), ("xb", 1024), ("xs", 1152), ("xw", 1440)):
+        zeros(name, 0, w)
+    for name, w in (("xm", 768), ("xn", 768), ("xa", 1536)):
+        memset(R(name, 0, w, 1, 96, 128), 0.0)
+    fill(R("xa", 1536, 1664), 0.0)
+    for k in range(4):
+        fill(R("xn", 192 * k, 192 * k + 192, 4, 96, 128), -2.0 if k & 1 else 1.0)
+    fill(R("xk", 0, 384, 4, 96, 128), 1.0)
     fill(R("xl", 3, 1536, 4), 0.0)
-    fill(R("ht", 768, 896), 0.0)
+    fill(R("ht", 0, 128), 0.0)
+    fill(R("ht", 896, 1024), 0.0)
     fill(R("cw", 1, 512, 4), 1.0)
     fill(cc(KS, 9), 1.0)
     fill(cc(KS + 4), 0.0)
@@ -328,39 +363,47 @@ def rank_program(g, core, T, topo):
     copy("v", cc(PM), R("pi", 1, 2))
     ts(R("cw", 2, 512, 4), R("r16", 0, 128), cc(PM), A.is_equal)
     copy("a", R("cw", 3, 512, 4), R("cw", 2, 512, 4), scale=-1.0)
-    o_pm, o_u = take("off", 24), take("off", 16)
+    o_pm, o_u = take("off", 24), take("off", 24)
     ts(o_pm, on(24), cc(PM), A.mult)
     ts(R("wk0", 16, 32), R("r16", 0, 16), cc(PM), A.is_le, -4096.0, A.mult)
     ts(R("wk0", 32, 48), R("r16", 0, 16), cc(PM), A.subtract, 1.0, A.is_equal)
     ts(cc(FX), cc(PM), 14.5, A.is_lt, 2048.0, A.mult)
     copy("a", R("wk0", 32, 48), R("wk0", 32, 48), scale=2048.0)
     tt(R("wk0", 0, 16), R("wk0", 16, 32), R("wk0", 32, 48), A.add)
-    memset(sub(o_u, 0, 8), 0)
-    memset(sub(o_u, 8, 16), 1)
+    for k, c in enumerate((0, 1, 17)):
+        memset(sub(o_u, 8 * k, 8 * k + 8), c)
     act(R("wk", 0, 384), R("wk0", 0, 16), F.Copy, off=o_pm)
     quant(CW, R("cw", 0, 512))
     ts(cc(OH, 6), cc(V16, 6), cc(PM), A.add, 0.0, A.is_equal)
     ts(cc(OHM, 6), cc(OH, 6), 1008.0, A.mult, -1024.0, A.add)
     copy("a", cc(OHN, 6), cc(OH, 6), scale=-16.0)
-    act(R("cx", 0, 512, 4), R("cw", 0, 512, 4), F.Identity, bias=-1.0)
-    fill(R("cx", 1, 512, 4), -1.0)
-    copy("a", R("cx", 2, 512, 4), R("cw", 0, 512, 4))
-    fill(R("cx", 3, 512, 4), 1.0)
+    fill(R("cx", 0, 512), 1.0)
+    copy("a", R("cx", 0, 512, 4), R("cw", 0, 512, 4))
     quant(CX, R("cx", 0, 512))
     fill(R("tr", 0, 512), 0.0)
     select(R("tr", 0, 512, 4), on(128), [[1, 128]], A.is_ge, -16, -1)
     quant(TR, R("tr", 0, 512))
+    fill(R("mt", 0, 288), 1.0)
+    act(R("mt", 96, 192), R("idn", 0, 96), F.Identity, bias=1.0, scale=-2.0)
+    act(R("tm", 0, 96), R("cw", 0, 384, 4), F.Identity, bias=-1.0)
+    fill(R("cm", 0, 66), -1024.0)
+    for a, b in ((0, 1), (5, 14), (20, 21), (26, 31), (32, 33), (42, 43), (49, 50), (62, 63)):
+        fill(R("cm", a, b, 4), 0.0)
+    copy("a", R("cm", 66, 132), R("cm", 0, 66), scale=-1.0)
     for b in range(4):
         quant(ET(b), R("et", 3 - b, 515 - b))
         ops[-1]["by"] = 3.0
         quant(EH(b), R("eh", 3 - b, 515 - b))
         ops[-1]["by"] = 7.0
     quant(R("uq", 0, 128), R("ut", 0, 512))
+    exchange([(R("uq", 0, 2), R("uv", 16 * l, 16 * l + 2), PART[l]) for l in range(2)], "aru")
+    ops[-2]["by"] = ops[-3]["by"] = 7.0
     for l in range(2):
         pick(R("ur", 128 * l, 128 * l + 128), R("uq", 0, 128), sub(o_u, 8 * l, 8 * l + 8))
-        ops[-2]["by"] = 9.0 if l == 0 else 0.0
+        pick(R("ur", 256 + 128 * l, 384 + 128 * l), R("uv", 0, 32), sub(o_u, 16 * l, 16 * l + 8))
+    quant(R("nw0", 384, 512), on(512))
     quant(R("s1", 192, 320), on(512))
-    quant(R("s2", 192, 320), on(512))
+    quant(R("s1", 512, 640), on(512))
     quant(R("wq", 0, 128), R("wt", 0, 512))
     copy("a", cc(NM), cc(PM), scale=-1.0)
 
@@ -370,78 +413,190 @@ def rank_program(g, core, T, topo):
         scan(ws, R("wk", 0, n), src, 0.0, A.add, A.max)
         ts(out, sub(ws, 15, n, 16), cc(FX), A.subtract)
 
-    def half(n, K, pb, rows, vals, tile, apart=False, turned=False):
-        h = n // 2
+    def listed(tile, a0, a1, m, b, out):
+        lq = take("lq", m)
+        quant(lq, R(tile, 4 * a0, 4 * (a0 + m)))
+        mm(b, ONES, lq)
+        wrap(bank(b, 0, a1 - a0), out)
+
+    def own_products(b, win, wide, pb):
+        mm(b, win, sub(win, 0, wide))
+        last = tf(wide, pb)
+        scan(last, R("wkd", 0, wide, p1=pb), bank(b, 0, wide, pb), 0.0, A.mult, A.max)
+        return last
+
+    def half(n, row, vals):
+        h, K, pb = n // 2, 3, 128
         s, sb, sn, cn = [take("col", K, pb) for i in range(4)]
         run = tf(h + K, pb)
         a = sub(run, h - 1, h - 1 + K)
         xp = take("xp", 48, pb)
         c0 = xp[3] // 4
         sq = take("sq", 128)
-        if K == 1:
-            above = []
-            for cmp in (A.is_ge, A.is_gt):
-                fl, cs = tb(n, pb), tf(h, pb)
-                ts(fl, rows[0], vals[0], cmp)
-                scan(cs, sub(fl, 0, h), sub(fl, h, n), 0.0, A.add, A.add)
-                above.append(one(cs, h - 1))
-        else:
-            for k in range(K - 1, -1, -1):
-                sg = tb(n, pb)
-                act(sg, rows[k], F.Sign, bias=vals[k], scale=-1.0, acc=one(s, k))
-                if k == 0 and not apart and rows[k][0] != "ps":
-                    eq = tb(n, pb)
-                    ts(eq, rows[k], vals[k], A.is_equal)
-                    scan(sub(run, 0, h), sub(eq, 0, h), sub(eq, h, n), -float(n), A.add, A.add)
-                else:
-                    minus_abs_sum(one(a, k), sg)
-            act(sb, s, F.Identity, bias=0.5 - n)
-            act(sn, s, F.Identity, bias=0.5 - n, scale=-1.0)
-        if K == 3:
-            tt(sub(xp, 0, 4 * K, 4), sb, a, A.is_lt)
-            tt(sub(xp, 20, 20 + 4 * K, 4), sn, a, A.is_gt)
-            fill(one(xp, 16), -h / pb)
-            scan(sub(xp, 5, 41, 4), cc(KS, 9, pb), sub(xp, 0, 36, 4), 0.0, A.mult, A.add)
-            quant(sq, R("xp", 0, 512))
-            mm(3, CW, sq)
-            for k in range(K):
-                ts(one(cn, k), bank(3, c0 + k, c0 + k + 1, pb), bank(3, c0 + K, c0 + K + 1, pb), A.subtract, bank(3, c0 + 5 + k, c0 + 6 + k, pb), A.max)
-        else:
-            fill(sub(xp, 9, 9 + 4 * K, 4), h / pb)
-            if K == 1:
-                ts(one(xp, 0), above[0], h + 0.5, A.is_gt)
-                ts(one(xp, 10), above[1], h - 0.5, A.is_gt)
-            elif apart:
-                tt(sub(xp, 0, 8, 4), sb, a, A.is_lt)
-                tt(sub(xp, 10, 18, 4), sn, a, A.is_gt)
+        for k in range(K - 1, -1, -1):
+            sg = tb(n, pb)
+            act(sg, row, F.Sign, bias=vals[k], scale=-1.0, acc=one(s, k))
+            if k == 0:
+                eq = tb(n, pb)
+                ts(eq, row, vals[k], A.is_equal)
+                scan(sub(run, 0, h), sub(eq, 0, h), sub(eq, h, n), -float(n), A.add, A.add)
             else:
-                ts(sub(xp, 1, 5, 3), on(2, pb), one(sb, 1), A.mult, one(a, 1), A.is_lt)
-                ts(one(xp, 14), one(sn, 1), one(a, 1), A.is_gt)
-                ts(one(xp, 0), one(sb, 0), one(a, 0), A.is_lt)
-                ts(sub(xp, 10, 16, 5), on(2, pb), one(sn, 0), A.mult, one(a, 0), A.is_gt)
-            quant(sq, R("xp", 0, 512))
-            mm(3, CX, sq)
+                minus_abs_sum(one(a, k), sg)
+        act(sb, s, F.Identity, bias=0.5 - n)
+        act(sn, s, F.Identity, bias=0.5 - n, scale=-1.0)
+        tt(sub(xp, 0, 4 * K, 4), sb, a, A.is_lt)
+        tt(sub(xp, 20, 20 + 4 * K, 4), sn, a, A.is_gt)
+        fill(one(xp, 16), -h / pb)
+        scan(sub(xp, 5, 41, 4), cc(KS, 9, pb), sub(xp, 0, 36, 4), 0.0, A.mult, A.add)
+        quant(sq, R("xp", 0, 512))
+        mm(2, CW, sq)
+        for k in range(K):
+            ts(one(cn, k), bank(2, c0 + k, c0 + k + 1, pb), bank(2, c0 + K, c0 + K + 1, pb), A.subtract, bank(2, c0 + 5 + k, c0 + 6 + k, pb), A.max)
+        out = take("off", n // 16)
+        for side in range(2):
             for k in range(K):
-                ts(one(cn, k), bank(3, c0 + k, c0 + k + 1, pb), bank(3, c0 + 2 + k, c0 + 3 + k, pb), A.max)
-        q = [R("qrow", 192 - h, 192, p1=pb), R("qrow", 192, 192 + h, p1=pb)]
-        tot = n * K if apart else n
-        out = take("off", tot // 16)
-        for side in ((1, 0) if turned else (0, 1)):
-            for k in range(K):
-                e = 4 * ((side ^ turned) * tot // 2 + (h * k if apart else 0)) + k
-                x = R(tile, e, e + 4 * h - k, 4, p1=pb)
+                e = 4 * side * h + k
+                x = R("xl", e, e + 4 * h - k, 4, p1=pb)
                 if side == 0:
-                    ts(x, q[0], one(cn, k), A.is_ge)
+                    ts(x, R("qrow", 0, h), one(cn, k), A.is_ge)
                 else:
-                    ts(x, q[1], one(cn, k), A.add, cc({192: JA, 96: JB, 48: JC}[h] + (0 if apart else k), 1, pb), A.is_ge)
-        cuts = [(0, h), (h, n)] if h >= 128 else [(0, tot)]
-        for i, (a0, a1) in enumerate(cuts):
-            m = max(a1 - a0, 128)
-            lq = take("lq", m)
-            quant(lq, R(tile, 4 * a0, 4 * (a0 + m)))
-            mm(i, ONES, lq)
-            wrap(bank(i, 0, a1 - a0), sub(out, a0 // 16, a1 // 16))
+                    ts(x, R("qrow", h, n), one(cn, k), A.add, cc(JA + k), A.is_ge)
+        for i in range(2):
+            listed("xl", h * i, h * i + h, h, i, sub(out, h * i // 16, (h * i + h) // 16))
         return out
+
+    def sizes(wins):
+        K = len(wins)
+        tmp, row, d, bound = tf(32 * K, 96), tf(96 * K, 96), [], []
+        for k in range(K):
+            last = own_products(k, wins[k], 128, 96)
+            d.append(one(last, 127))
+            turn(sub(tmp, k, 32 * K, K), sub(last, 96, 128))
+            e = take("col", 1, 96)
+            act(e, d[k], F.Identity, bias=2.0 ** -30, scale=1.25 * 2.0 ** -24)
+            bound.append(tf(96, 96))
+            act(bound[k], R("tm", 0, 96, p1=96), F.Identity, bias=d[k], scale=e)
+        for i in range(9):
+            q, r = i // 3, i % 3
+            copy("av"[i & 1], sub(row, 32 * K * r, 32 * K * (r + 1), 1, 32 * q, 32 * q + 32), sub(tmp, 0, 32 * K, 1, 32 * r, 32 * r + 32))
+        return row, [sub(row, k, 96 * K, K) for k in range(K)], d, bound
+
+    def scores(wins, cols, ur):
+        K = len(wins)
+        n = 96 * K
+        for k in range(K):
+            mm(6 + k, wins[k], ur)
+        mm(5, ur, cols)
+        sv, s, nx = take("col", K, 96), take("col", K, 96), []
+        for k in range(K):
+            copy("a", one(sv, k), bank(6 + k, 0, 1, 96))
+        for k in range(K):
+            sg, eq, run = tb(n, 96), tb(n, 96), tb(n, 96)
+            act(sg, bank(5, 0, n, 96), F.Sign, bias=one(sv, k), scale=-1.0, acc=one(s, k))
+            ts(eq, sg, 0.0, A.is_equal, -1.0, A.mult)
+            scan(run, R("mt", 96 - 96 * k, 96 - 96 * k + n, p1=96), eq, one(s, k), A.mult, A.add)
+            nx.append(one(run, n - 1))
+        return nx
+
+    def member(l, t, a, b, sx, sent):
+        out = R("xw", 720 * l + 4 * a + t, 720 * l + 4 * b, 4, p1=96)
+        if sent:
+            ts(out, R("cm", a, b, p1=96), sx, A.is_gt)
+        else:
+            ts(out, R("cm", 66 + a, 66 + b, p1=96), sx, A.is_le)
+
+    def cell(l, t, j):
+        return R("xb", 512 * j + t, 512 * j + 384, 4, p1=96) if l else R("xa", 384 * j + t, 384 * j + 384, 4, p1=96)
+
+    def candidates(l):
+        if l == 0:
+            quant(R("nw0", 0, 192), R("ht", 128, 896))
+            exchange([(R("nw0", 0, 192), R("nw0", 192, 384), PART[l])], "ar0")
+            quant(R("nwb", 0, 224), R("ht", 128, 1024))
+            wins = [[R("nwb", 0, 128), R("nwb", 96, 224)], [R("nw0", 192, 320), R("nw0", 288, 416)]]
+            cols = [R("nwb", 0, 192), R("nw0", 192, 384)]
+        else:
+            quant(R("nw1", 0, 128), R("ht", 0, 512))
+            exchange([(R("nw1", 32, 128), R("nw1", 128, 224), PART[l])], "ar1")
+            quant(R("nw1", 224, 352), R("ht", 128, 640))
+            wins = [[R("nw1", 224, 352)], [R("nw1", 128, 256)]]
+            cols = [wins[0][0], wins[1][0]]
+        K = 2 - l
+        got = []
+        for s in range(2):
+            row, rows, d, bound = sizes(wins[s])
+            sx = scores(wins[s], cols[s], R("ur", 256 * s + 128 * l, 256 * s + 128 * l + 128))
+            got.append((row, rows, d))
+            if l == 0:
+                for k in range(2):
+                    member(l, 2 * s + k, 0, 66, sx[k], s == 1)
+                ts(cell(l, 2 * s, 2 * s + 1), rows[1], d[0], A.is_le)
+                ts(cell(l, 2 * s + 1, 2 * s), rows[0], d[1], A.is_lt)
+            else:
+                member(l, s, 0, 34, sx[0], s == 1)
+                member(l, s, 34, 66, sx[0], s == 0)
+                member(l, 3 - s, 32, 66, sx[0], s == 0)
+            for k in range(K):
+                tt(cell(l, K * s + k, K * s + k), rows[k], bound[k], A.is_le)
+        if l == 0:
+            sg = tb(192, 96)
+            act(sg, got[0][0], F.Sign, bias=got[1][2][0], scale=-1.0)
+            for j in range(2):
+                act(cell(l, 2, j), sub(sg, j, 192, 2), F.Relu)
+                ts(cell(l, 3, j), got[0][1][j], got[1][2][1], A.is_lt)
+                for k in range(2):
+                    ts(cell(l, k, 2 + j), got[1][1][j], got[0][2][k], A.is_le)
+            quant(R("ca", 0, 192), R("xa", 0, 768))
+            quant(R("ca", 192, 416), R("xa", 768, 1664))
+            cw = [R("ca", 96 * k, 96 * k + 128) for k in range(4)]
+        else:
+            ts(cell(l, 1, 0), got[0][0], got[1][2][0], A.is_lt)
+            ts(cell(l, 2, 0), got[0][0], got[1][2][0], A.is_equal)
+            ts(cell(l, 0, 1), got[1][0], got[0][2][0], A.is_le)
+            ts(cell(l, 3, 1), got[1][0], got[0][2][0], A.is_equal, -1.0, A.mult)
+            for k in range(2):
+                quant(R("cb", 128 * k, 128 * k + 128), R("xb", 512 * k, 512 * k + 512))
+            cw = [R("cb", 128 * k, 128 * k + 128) for k in (0, 1, 1, 0)]
+        quant(R("wv", 180 * l, 180 * l + 178), R("xw", 720 * l, 720 * l + 712))
+        for k in range(4):
+            mm(2, cw[k], R("wv", 180 * l + WO[k], 180 * l + WO[k] + 128), k == 0, k == 3)
+        xp, thr, sq = take("xp", 32, 96), take("col", 16, 96), take("sq", 128)
+        c0 = xp[3] // 4
+        flags = R("xw", 720 * l + 128, 720 * l + 132, p1=96)
+        copy("a", sub(xp, 16, 32, 4), flags)
+        for k in range(1, 4):
+            copy("a", sub(xp, 17 + 4 * k, 17 + 5 * k), sub(flags, 0, k))
+        act(thr, sub(xp, 16, 32), F.Identity, bias=1000.0, scale=(96.5 if l == 0 else 48.5) - 1000.0)
+        tt(sub(xp, 0, 16), bank(2, 0, 16, 96), thr, A.is_gt)
+        quant(sq, R("xp", 0, 512))
+        mm(1, CX, sq)
+        tile, q = "xm" if l == 0 else "xn", R("qrow", 192, 288, p1=96)
+        for k in range(4):
+            ts(R(tile, k, 384, 4, p1=96), q, bank(1, c0 + k, c0 + k + 1, 96), A.is_ge)
+            ts(R(tile, 384 + k, 768, 4, p1=96), q, bank(1, c0 + k, c0 + k + 1, 96), A.add, bank(1, c0 + 4 + k, c0 + 5 + k, 96), A.is_ge)
+        pa = take("col", 4, 96)
+        copy("v", pa, bank(1, c0 + 4, c0 + 8, 96))
+        out = take("off", 12)
+        listed(tile, 0, 192, 192, 0, out)
+        L["l", l + 1] = out
+        L["a", l + 1] = pa
+
+    def members(l):
+        pa = L["a", l]
+        if l == 1:
+            out = take("off", 18)
+            for k in range(2):
+                ts(R("xs", k, 384, 4, p1=96), R("qrow", 192, 288, p1=96), one(pa, k), A.add, cc(JB + k, 1, 96), A.is_ge)
+            for k in range(4):
+                ts(R("xs", 384 + k, 1152, 4, p1=96), R("qrow", 192, 384, p1=96), one(pa, k), A.is_ge)
+            listed("xs", 0, 288, 288, 3, out)
+            L["s", 0] = sub(out, 0, 12)
+            L["m", 1] = sub(out, 6, 18)
+        else:
+            L["m", 2] = take("off", 6)
+            for k in range(2):
+                ts(R("xk", k, 384, 4, p1=96), R("qrow", 192, 288, p1=96), one(pa, k), A.is_ge)
+            listed("xk", 0, 96, 128, 3, L["m", 2])
 
     def count(src, func, bias, scale, cnt, hi):
         n, pb = width(src), src[2]
@@ -470,60 +625,41 @@ def rank_program(g, core, T, topo):
 
     L = {}
 
+    def S(l, a, b):
+        return R("s1" if l else "s0", SO[l] + a, SO[l] + b)
+
     def casts(h, scale):
         for b in range(4):
-            copy("va"[b & 1], R("ht", b, 4 * h, 4), bank(4 + b, 0, h), scale=scale)
+            copy("va"[b & 1], R("ht", 128 + b, 128 + 4 * h, 4), bank(4 + b, 0, h), scale=scale)
+
+    def first():
+        row, vals = tf(P), []
+        for k in range(3):
+            last = own_products(k, R("f", 128 * k, 128 * k + 128), 160, 128)
+            vals.append(one(last, 159))
+            turn(sub(row, 32 * k, 32 * k + 32), sub(last, 128, 160))
+        w = 96
+        for q in range(4):
+            copy("va"[q & 1], sub(row, w, 2 * w, 1, 32 * q, 32 * q + 32), sub(row, 0, w, 1, 32 * (q ^ 1), 32 * (q ^ 1) + 32))
+        for q in range(2):
+            copy("va"[q], sub(row, 2 * w, 4 * w, 1, 64 * q, 64 * q + 64), sub(row, 0, 2 * w, 1, 64 - 64 * q, 128 - 64 * q))
+        L["l", 0] = half(P, row, vals)
 
     def up(l):
         n = NS[l]
-        h, fo, s = n // 2, FO[l], "s%d" % l
+        h = n // 2
         m = max(h, 128)
-        K, pb = (3, 128) if l == 0 else (2, 96)
-        w = 32 * K
-        for k in range(K):
-            win = R("f", fo + pb * k, fo + pb * k + 128)
-            mm(k, win, win)
-        d, xb, row, vals = take("col", K, pb), tf(w, pb), tf(n, pb), []
-        for k in range(K):
-            mk = tf(pb + 32, pb)
-            tt(sub(mk, 0, pb), bank(k, 0, pb, pb), R("idn", 0, pb, p1=pb), A.mult)
-            if k < K - 1 and l == 0:
-                vals.append(one(d, k))
-                act(tb(pb, pb), sub(mk, 0, pb), F.Copy, acc=one(d, k))
-                act(sub(xb, 32 * k, 32 * k + 32), on(32, pb), F.Copy, scale=one(d, k))
-            else:
-                fill(sub(mk, pb, pb + 32), 0.0)
-                last = tf(pb + 32, pb)
-                scan(last, mk, mk, 0.0, A.max, A.max)
-                vals.append(one(last, pb + 31))
-                turn(sub(row, 32 * k, 32 * k + 32) if l < 2 else sub(row, k, w, 2), sub(last, pb, pb + 32))
+        lw, win = L["l", l], R(("f", "nw0", "nw1")[l], 0, UW[l])
         if l == 0:
-            turn(sub(row, 0, w - 32), sub(xb, 0, w - 32))
-        if pb == 128:
-            for q in range(4):
-                copy("va"[q & 1], sub(row, w, 2 * w, 1, 32 * q, 32 * q + 32), sub(row, 0, w, 1, 32 * (q ^ 1), 32 * (q ^ 1) + 32))
-            for q in range(2):
-                copy("va"[q], sub(row, 2 * w, 4 * w, 1, 64 * q, 64 * q + 64), sub(row, 0, 2 * w, 1, 64 - 64 * q, 128 - 64 * q))
+            pick(S(l, 0, h), win, sub(lw, 0, h // 16))
+            pick(S(l, h, n), win, sub(lw, h // 16, n // 16))
         else:
-            for i in range(6):
-                q, sl = i % 3, 1 + i // 3
-                r = (q + sl) % 3
-                copy("va"[i & 1], sub(row, sl * w, sl * w + w, 1, 32 * q, 32 * q + 32), sub(row, 0, w, 1, 32 * r, 32 * r + 32))
-        if l < 2:
-            lw = half(n, K, pb, [row] * K, vals, "xl" if l == 0 else "xm")
-        else:
-            lw = half(h, K, pb, [sub(row, k, n, 2) for k in range(K)], vals, "xn", apart=True)
-        L["l", l] = lw
-        if l == 0:
-            pick(R(s, 0, h), R("f", fo, fo + n), sub(lw, 0, h // 16))
-            pick(R(s, h, n), R("f", fo, fo + n), sub(lw, h // 16, n // 16))
-        else:
-            pick(R(s, 0, n), R("f", fo, fo + n), lw)
+            pick(S(l, 0, n), win, lw)
         K, pb, hp = [(2, 96, 192), (1, 96, 96), (2, 48, 48)][l]
         par, hi = take("col", K, pb), take("col", K, pb)
         for k in range(K):
             a = h + (hp * k if l == 2 else 0)
-            mm(k, R(s, pb * k, pb * k + 128), R(s, a, a + m))
+            mm(k, S(l, pb * k, pb * k + 128), S(l, a, a + m))
             pad = 64 if l == 2 and k else 16
             rm = tf(pad + hp, pb)
             fill(sub(rm, 0, pad), -1e29)
@@ -531,37 +667,16 @@ def rank_program(g, core, T, topo):
             count(rm, F.Sign, one(rm, pad + hp - 1), -1.0, one(par, k), one(hi, k))
         L["par", l] = par
         for b in range(4):
-            mm(4 + b, ET(b), R(s, 0, m), True, False)
+            mm(4 + b, ET(b), S(l, 0, m), True, False)
         pw = take("off", h // 16)
         L["p", l] = pw
-        ts(pw, spread(par, hi, K, pb, "xp", 3), float(h - 16), A.add)
-        pick(R("pc", PPO[l], PPO[l] + h), R(s, 0, n), pw)
+        ts(pw, spread(par, hi, K, pb, "xp", 2), float(h - 16), A.add)
+        pick(R("pc", PPO[l], PPO[l] + h), S(l, 0, n), pw)
         for b in range(4):
             mm(4 + b, EH(b), R("pc", PPO[l], PPO[l] + m), False, True)
         casts(h, None)
         if l == 2:
-            quant(R(s, BE[l], BE[l] + 128), R("ht", 0, 512))
-            return
-        nw, mq = "nw%d" % l, 224 if l == 0 else 128
-        quant(R(nw, 0, mq), R("ht", 0, 4 * mq))
-        ur = R("ur", 128 * l, 128 * l + 128)
-        for k in range(K):
-            mm(1 + k, R(nw, pb * k, pb * k + 128), ur)
-        mm(0, ur, R(nw, 0, m))
-        sv = take("col", K, pb)
-        for k in range(K if l == 0 else 0):
-            copy("va"[k], one(sv, k), bank(1 + k, 0, 1, pb))
-        vals = [one(sv, k) for k in range(K)] if l == 0 else [bank(1, 0, 1, pb)]
-        both = half(h, K, pb, [bank(0, 0, h, pb)] * K, vals, "xm" if l == 0 else "xk", turned=True)
-        L["s", l] = both
-        q, fo = h // 2, FO[l + 1]
-        if l == 0:
-            pick(R("up0", 0, q), R(nw, 0, h), sub(both, 0, q // 16))
-            exchange([(R("up0", 0, q), R("f", fo + q, fo + h))], PART[l], "ar0")
-            pick(R("f", fo, fo + q), R(nw, 0, h), sub(both, q // 16, h // 16))
-        else:
-            pick(R("f", fo + q, fo + q + h), R(nw, 0, h), both)
-            exchange([(R("f", fo + q, fo + h), R("f", fo + q + h, fo + 2 * h)), (R("f", fo + h, fo + q + h), R("f", fo, fo + q))], PART[l], "ar1")
+            quant(S(l, BE[l], BE[l] + 128), R("ht", 128, 640))
 
     def children(l):
         h = NS[l] // 2
@@ -572,8 +687,8 @@ def rank_program(g, core, T, topo):
                 ts(R("xc", 192 * k, 192 * k + 192, 4, p1=48), R("qrow", 208 + 48 * k, 256 + 48 * k, p1=48), one(L["par", l], k), A.is_equal)
             sq = take("sq", 128)
             quant(sq, R("xc", 0, 512))
-            mm(2, sq, TR)
-            count(bank(2, 0, 64, pb), F.Relu, 1.0, -1.0, cnt, hi)
+            mm(0, sq, TR)
+            count(bank(0, 0, 64, pb), F.Relu, 1.0, -1.0, cnt, hi)
         else:
             act(prow, R("iot", 0, 2 * h), F.Identity, bias=-float(h), off=L["p", l])
         for k in range(K if l < 2 else 0):
@@ -582,88 +697,114 @@ def rank_program(g, core, T, topo):
             ts(ne, sub(prow, 0, h, 1, 0, pb), cc(Q96 + k, 1, pb), A.not_equal)
             scan(sub(cp, 16, h + 16), ne, ne, 1.0, A.mult, A.mult)
             count(cp, F.Copy, 0.0, 1.0, one(cnt, k), one(hi, k))
-        both = spread(cnt, hi, K, pb, "xo", 2, under=(h if l < 2 else 48) + 15.5, step=float(AV[l] - h))
+        both = spread(cnt, hi, K, pb, "xo", 1 if l == 2 else 3, under=(h if l < 2 else 48) + 15.5, step=float(AV[l] - h))
         res = sub(both, 0, k16)
         mw, ow, v = take("off", k16), take("off", k16), tf(2 * h)
+        L["c", l] = mw
         if l == 2:
             for k in range(2):
                 ts(sub(mw, 3 * k, 3 * k + 3), sub(res, 3 * k, 3 * k + 3), float(BE[l] + 48 * k - 16), A.add)
-            L["c", l] = mw
             copy("a", sub(v, 0, h), R("iot", BE[l], BE[l] + h))
         else:
             ts(mw, res, -16.0, A.add, float(h - 1), A.min)
+        if l == 0:
             for a in range(0, h, 96):
                 scatter(sub(v, 0, h), sub(L["s", l], a // 16, a // 16 + 6), R("iot", BE[l] + a, BE[l] + a + 96))
-            row = tf(h)
-            act(row, sub(v, 0, h), F.Copy, off=mw)
-            L["c", l] = take("off", k16)
-            wrap(row, L["c", l])
+            L["c", l] = through(sub(v, 0, h), mw)
         ts(ow, sub(both, k16, 2 * k16), float(h), A.add)
         act(sub(v, h, 2 * h), R("iot", 0, BE[l]), F.Copy, off=ow)
-        fl = tf(2 * h)
-        for a, k in [(0, 32), (32, 32), (64, 32), (96, 96)] if l == 2 else [(a, 96) for a in range(0, 2 * h, 96)]:
-            scatter(fl, sub(L["l", l], a // 16, (a + k) // 16), sub(v, a, a + k))
-        return fl
+        return v
+
+    def through(row, off, bias=None):
+        n = 16 * width(off)
+        got, out = tf(n), take("off", n // 16)
+        if bias is None:
+            act(got, row, F.Copy, off=off)
+        else:
+            act(got, row, F.Identity, bias=bias, off=off)
+        wrap(got, out)
+        return out
+
+    def inverse(off, w):
+        row = tf(w)
+        fill(row, 0.0)
+        for a in range(0, width(off), 6):
+            scatter(row, sub(off, a, a + 6), R("iot", 16 * a, 16 * a + 96))
+        return row
 
     def parents(l, fw):
         n = NS[l]
         h = n // 2
-        z = tf(BE[l] + h)
-        for a in range(0, n, 96):
-            act(sub(z, a, a + 96), R("iot", 0, n), F.Copy, off=sub(L["l", l], a // 16, a // 16 + 6))
-        copy("a", sub(z, AV[l], AV[l] + h), sub(z, h, n))
-        if l == 2:
-            act(sub(z, BE[l], BE[l] + h), sub(z, 0, n), F.Copy, off=L["p", l])
+        if l:
+            place, z, y = inverse(L["m", l], UW[l]), tf(n), tf(n)
+            act(sub(z, h, n), place, F.Copy, off=sub(L["l", l], h // 16, n // 16))
+            copy("a", sub(z, 0, h), sub(z, h, n))
+            act(sub(y, 0, h), z, F.Copy, off=L["p", l])
+            copy("a", sub(y, h, n), sub(z, h, n))
+            z = y
         else:
-            pr = tf(h)
+            z, pr = tf(BE[l] + h), tf(h)
+            for a in range(0, n, 96):
+                act(sub(z, a, a + 96), R("iot", 0, n), F.Copy, off=sub(L["l", l], a // 16, a // 16 + 6))
+            copy("a", sub(z, AV[l], AV[l] + h), sub(z, h, n))
             act(pr, sub(z, 0, n), F.Copy, off=L["p", l])
             act(sub(z, BE[l], BE[l] + h), pr, F.Copy, off=L["s", l])
         for a in range(0, P >> l, 96):
-            act(R("pat", PAO[l] + a, PAO[l] + a + 96), z, F.Identity, bias=-96.0 if l == 2 else 0.0, off=sub(fw, a // 16, a // 16 + 6))
+            act(R("pat", PAO[l] + a, PAO[l] + a + 96), z, F.Copy, off=sub(fw, a // 16, a // 16 + 6))
 
     def down(l):
-        n, s = NS[l], "s%d" % l
+        n = NS[l]
         h = n // 2
         m = max(h, 128)
         for b in range(4):
-            mm(4 + b, ET(b), R(s, h, h + m), True, False)
-        pick(R("pc", CO[l], CO[l] + h), R(s, 0, BE[l] + (128 if l == 2 else h)), L["c", l])
+            mm(4 + b, ET(b), S(l, h, h + m), True, False)
+        pick(R("pc", CO[l], CO[l] + h), S(l, 0, 448 if l == 2 else 768), L["c", l])
         for b in range(4):
             mm(4 + b, ET(b), R("pc", CO[l], CO[l] + m), False, True)
         casts(h, 0.5)
-        quant(R(s, AV[l], AV[l] + m), R("ht", 0, 4 * m))
-        return R(s, 0, BE[l] + h)
+        quant(S(l, AV[l], AV[l] + m), R("ht", 128, 128 + 4 * m))
 
+    first()
     up(0)
-    fl0 = children(0)
+    candidates(0)
+    members(1)
+    v0 = children(0)
     up(1)
-    fl1 = children(1)
+    v1 = children(1)
+    at1 = through(inverse(L["l", 1], UW[1]), L["m", 1])
+    candidates(1)
+    members(2)
     up(2)
-    fl2 = children(2)
-    fw = [take("off", 24), take("off", 12), take("off", 6), take("off", 6)]
-    wrap(sub(fl2, 48, 144), fw[3])
-    pick(R("s1", BE[1], BE[1] + 96), down(2), fw[3])
-    wrap(sub(fl1, 96, 192), sub(fw[1], 6, 12))
-    wrap(sub(fl1, 0, 96), sub(fw[1], 0, 6))
-    win = down(1)
-    pick(R("dn1", 0, 96), win, sub(fw[1], 6, 12))
-    exchange([(R("dn1", 0, 96), R("s0", BE[0], BE[0] + 96))], PART[0], "ar2")
-    pick(R("s0", BE[0] + 96, BE[0] + 192), win, sub(fw[1], 0, 6))
-    wrap(sub(fl2, 96, 192), fw[2])
+    inv, mine, own = inverse(L["l", 2], UW[2]), tf(96), take("off", 6)
+    tt(mine, sub(inv, 32, 128), sub(inv, 224, 320), A.add)
+    wrap(mine, own)
+    kid = through(mine, L["c", 1])
+    v2 = children(2)
+    L["c", 1] = through(v2, kid, float(SO[2]))
+    act(sub(v1, 0, 96), v2, F.Identity, bias=float(SO[2]), off=own)
+    down(2)
+    down(1)
+    pick(R("dn1", 0, 96), S(1, 0, 768), through(v1, sub(at1, 6, 12)))
+    exchange([(R("dn1", 0, 96), R("s0", BE[0], BE[0] + 96), PART[0])], "ar2")
+    pick(R("s0", BE[0] + 96, BE[0] + 192), S(1, 0, 768), through(v1, sub(at1, 0, 6)))
+    fl0, fw = tf(P), take("off", 24)
+    for a in range(0, P, 96):
+        scatter(fl0, sub(L["l", 0], a // 16, a // 16 + 6), sub(v0, a, a + 96))
     for a in (0, 192):
-        wrap(sub(fl0, a, a + 192), sub(fw[0], a // 16, a // 16 + 12))
-    for l in range(3):
-        parents(l, fw[l])
+        wrap(sub(fl0, a, a + 192), sub(fw, a // 16, a // 16 + 12))
+    parents(0, fw)
+    parents(1, at1)
+    parents(2, through(inv, L["m", 2]))
     dma("g", T.pa[0:1, :], T.pat[0:1, :], [R("pat", 0, 672, p1=1)], [], "st3")
-    win = down(0)
+    down(0)
     for i, (a, b) in enumerate(((0, 256), (256, P))):
         fin = R("fin", a, b)
-        pick(fin, win, sub(fw[0], a // 16, b // 16))
+        pick(fin, S(0, 0, 768), sub(fw, a // 16, b // 16))
+        dma("g", T.oc[:, 4 * a:4 * b], T.fin[:, a:b].bitcast(dt.uint8), [fin], [], "st3")
         mm(i, R("wq", 0, 128), fin)
         copy("av"[i], R("yt", a, b), bank(i, 0, b - a))
         dma("y", T.y[:, a:b], T.yt[:, a:b], [R("yt", a, b)], [], "st1")
     fin = R("fin", 0, P)
-    dma("g", T.oc[:, :], T.fin[:, 0:P].bitcast(dt.uint8), [fin], [], "st3")
     for k in range(4):
         dma("ayag"[k], T.osc[4 * k:4 * k + 4, :], T.fins[32 * k:32 * k + 4, 0:P], [sc(fin)], [], "st3" if k == 3 else "st1")
 

@@ -18,24 +18,25 @@ X4, U8, F32, BF, U16, I32 = "float8_e4m3fn_x4", "uint8", "float32", "bfloat16", 
 
 SCRATCH = {"ps": ("psum", [128, 4096], F32)}
 for _n, _w in (("f", 512), ("s0", 768), ("s1", 768), ("pc", 768), ("nw0", 512), ("nwb", 224), ("nw1", 352), ("cq", 1536),
-               ("lq", 1280), ("sq", 1536), ("uq", 128), ("uv", 32), ("ur", 512), ("wq", 128), ("fin", 384), ("dn1", 96),
+               ("lq", 1280), ("sq", 1672), ("uq", 128), ("uv", 32), ("ur", 512), ("wq", 128), ("fin", 384), ("dn1", 96),
                ("ca", 416), ("cb", 256), ("wv", 360)):
     SCRATCH[_n] = ("sbuf", [128, _w], X4)
     SCRATCH[_n + "s"] = ("sbuf", [128, _w], U8)
 for _n, _w, _d in (("xt", 1536, BF), ("ut", 512, BF), ("wt", 512, BF), ("on", 512, BF), ("idn", 128, BF), ("cw", 512, BF),
-                   ("cx", 512, BF), ("tr", 512, BF), ("wkd", 160, BF), ("mt", 288, BF), ("tm", 96, BF), ("cm", 132, BF),
-                   ("et", 520, BF), ("eh", 520, BF), ("xp", 512, BF), ("xo", 512, BF), ("xl", 1536, BF), ("xm", 768, BF),
-                   ("xk", 512, BF), ("xc", 512, BF), ("xn", 768, BF), ("xs", 1152, BF), ("xa", 1664, BF), ("xb", 1024, BF),
-                   ("xw", 1440, BF), ("ht", 1024, BF), ("r16", 128, BF), ("qrow", 384, BF),
-                   ("iot", 768, F32), ("pi", 2, I32), ("cc", 96, F32), ("wk0", 48, F32), ("wk", 384, F32), ("off", 384, U16),
+                   ("cx", 512, BF), ("tr", 512, BF), ("wkd", 160, BF), ("mt", 288, BF), ("tm", 96, BF), ("mz", 96, BF), ("cm", 132, BF),
+                   ("et", 520, BF), ("eh", 520, BF), ("xp", 528, BF), ("xo", 512, BF), ("xl", 1536, BF), ("xm", 768, BF),
+                   ("xk", 512, BF), ("xc", 512, BF), ("xn", 768, BF), ("xs", 768, BF), ("xa", 1664, BF), ("xb", 1024, BF),
+                   ("xw", 1440, BF), ("ht", 1024, BF), ("r16", 128, BF), ("qrow", 384, BF), ("iot", 768, F32), ("pi", 2, I32),
+                   ("cc", 112, F32), ("c4", 512, BF), ("wk0", 192, BF), ("wk", 192, BF), ("xg", 1024, BF), ("off", 384, U16),
                    ("col", 384, F32), ("tf", 20480, F32), ("tb", 16384, BF), ("pat", 672, F32), ("yt", 384, F32)):
     SCRATCH[_n] = ("sbuf", [128, _w], _d)
 
-SEMAPHORES = ["v", "a", "t", "g", "lx0", "lx1", "lx2", "lu", "lw", "sent", "aru", "ar0", "ar1", "ar2", "st1", "st3"]
+SEMAPHORES = ["v", "a", "t", "g", "lx0", "lx1", "lx2", "lu", "lw", "lz", "sent", "aru", "ar0", "ar1", "ar2", "st1", "st3"]
 
-PM, FX, JA, JB, Q96, OH, OHM, QW, KS, V16, NM, OHN = 0, 1, 2, 5, 8, 10, 16, 22, 34, 44, 57, 58
-CYC, HOP, FAR = 0.0009, 0.17, 2.0
-PLANS, TRIES = {}, 3000
+PM, FX, JA, JB, Q96, OH, OHM, QW, V16, NM, OHN, MK = 0, 1, 2, 5, 8, 10, 16, 22, 44, 57, 58, 64
+CYC, HOP, FAR = 0.00095, 0.23, 0.9
+CASES = ((1.0, 0.23, 1.0), (0.87, 0.26, 0.85), (1.1, 0.21, 1.0), (1.3, 0.23, 1.5))
+PLANS, TRIES = {}, 4000
 
 
 def R(name, c0, c1, step=1, p0=0, p1=128):
@@ -116,16 +117,16 @@ def arrange(ops):
 
     def span(order):
         tot, held = 0.0, []
-        for slow in ("", "v", "a", "t"):
+        for (slow, hop, far), gaps in zip(CASES, cases):
             free, last, end, why = {}, {}, [0.0] * n, [None] * n
             for i in order:
                 q, t = queues[i], 0.0
-                for j, d in gap[i]:
+                for j, d in gaps[i]:
                     if end[j] + d > t:
                         t, why[i] = end[j] + d, j
                 if free.get(q, 0.0) > t:
                     t, why[i] = free[q], -1 - last[q]
-                end[i] = t + ops[i]["c"] * (1.2 if q == slow else 1.0)
+                end[i] = t + ops[i]["c"] * slow
                 if q:
                     free[q], last[q] = end[i], i
             i = max(order, key=lambda k: end[k] + ops[k]["lat"])
@@ -140,6 +141,8 @@ def arrange(ops):
 
     if n not in PLANS:
         queues = [o["q"] for o in ops]
+        cases = [[[(j, 0.001 if o["q"] == "t" == ops[j]["q"] else ops[j]["lat"] * far + hop) for j in o["pre"]] for o in ops]
+                 for slow, hop, far in CASES]
         bonus, seed = [0.0] * n, 1
         best = plan(bonus)
         least, held = span(best)
@@ -307,11 +310,17 @@ def rank_program(g, core, T, topo):
     def on(k, pb=128):
         return R("on", 0, k, p1=pb)
 
-    def zeros(name, a, b):
-        for c in range(a, b, 256):
-            fill(R(name, c, min(b, c + 256)), 0.0)
+    def flat(name, a, b, c=0):
+        for k in range(a, b, 256):
+            iota(R(name, k, min(b, k + 256)), [[0, min(b, k + 256) - k]], c, 0)
 
-    CW, ONES, CX, TR = R("cq", 0, 128), R("cq", 128, 256), R("cq", 1280, 1408), R("cq", 1408, 1536)
+    def lay(out, in_):
+        raw = size[out[0]] == X4
+        dma("y", ap(out).bitcast(dt.uint8) if raw else ap(out), ap(in_).bitcast(dt.uint8) if raw else ap(in_), [in_], [out], "lz")
+        ops[-1]["lat"] = 3 * FAR
+
+    CW, ONES, CX, TR = R("cq", 0, 128), R("f", 384, 512), R("cq", 1280, 1408), R("cq", 1408, 1536)
+    C4 = R("cq", 128, 256)
 
     def ET(b):
         return R("cq", 256 + 128 * b, 384 + 128 * b)
@@ -337,54 +346,62 @@ def rank_program(g, core, T, topo):
     iota(cc(JB, 2), [[96, 2]], 1, 1)
     memset(R("et", 0, 520), 0.0)
     copy("a", R("et", 3, 512, 4), R("idn", 0, 128))
-    fill(R("eh", 0, 260), 0.0)
-    fill(R("eh", 260, 520), 0.0)
-    copy("a", R("eh", 3, 512, 4), R("idn", 0, 128), scale=-0.5)
+    for a in (0, 260):
+        copy("a", R("eh", a, a + 260), R("et", a, a + 260), scale=-0.5)
     iota(cc(V16, 12), [[16, 12]], 0, -1)
     iota(cc(Q96, 2), [[96, 2]], 0, 1)
     iota(cc(QW, 12), [[16, 12]], 0, 0)
     iota(R("iot", 0, 768), [[1, 768]], 0, 0)
-    for name, w in (("xp", 512), ("xo", 512), ("xk", 512), ("xc", 512), ("xb", 1024), ("xs", 1152), ("xw", 1440)):
-        zeros(name, 0, w)
-    for name, w in (("xm", 768), ("xn", 768), ("xa", 1536)):
-        memset(R(name, 0, w, 1, 96, 128), 0.0)
-    fill(R("xa", 1536, 1664), 0.0)
+    memset(R("xp", 0, 528), 0.0)
+    memset(R("xm", 0, 768), 0.0)
+    for name, a, b, p in (("xa", 0, 768, 96), ("xa", 768, 1536, 96), ("xa", 1536, 1664, 0), ("xw", 0, 720, 0), ("xn", 0, 768, 96),
+                          ("xg", 0, 512, 96), ("xg", 512, 1024, 96), ("xs", 0, 768, 96), ("ht", 0, 128, 0), ("ht", 896, 1024, 0)):
+        lay(R(name, a, b, 1, p, 128), R("xm", 0, b - a, 1, p, 128))
+    lay(R("mt", 0, 96), on(96))
+    lay(R("mt", 192, 288), on(96))
+    for name, a in (("nw0", 384), ("s1", 192), ("s1", 512)):
+        lay(R(name, a, a + 128), ONES)
+        lay(sc(R(name, a, a + 128)), sc(ONES))
+    for name, a, b in (("xo", 0, 512), ("xw", 720, 1440), ("xb", 0, 1024), ("xk", 0, 512), ("xc", 0, 512), ("tr", 0, 512)):
+        flat(name, a, b)
+    flat("cx", 0, 512, 1)
+    for t in (2, 3):
+        fill(R("xs", t, 768, 4, p1=96), 0.0)
     for k in range(4):
         fill(R("xn", 192 * k, 192 * k + 192, 4, 96, 128), -2.0 if k & 1 else 1.0)
     fill(R("xk", 0, 384, 4, 96, 128), 1.0)
     fill(R("xl", 3, 1536, 4), 0.0)
-    fill(R("ht", 0, 128), 0.0)
-    fill(R("ht", 896, 1024), 0.0)
     fill(R("cw", 1, 512, 4), 1.0)
-    fill(cc(KS, 9), 1.0)
-    fill(cc(KS + 4), 0.0)
-    quant(ONES, on(512))
+    fill(cc(MK, 24), 8192.5 - P)
+    for a, b, st in ((1, 5, 1), (10, 12, 1), (13, 14, 1), (19, 23, 3)):
+        fill(R("cc", MK + a, MK + b, st), 0.5 - P)
+    act(cc(MK + 24, 24), cc(MK, 24), F.Identity, bias=1.0 - 2 * P, scale=-1.0)
+    for t in range(4):
+        copy("a", R("c4", t, 512, 4), R("cw", 0, 512, 4))
+    quant(C4, R("c4", 0, 512))
     ts(R("pi", 1, 2), R("pi", 0, 1), 15, A.bitwise_and)
     copy("v", cc(PM), R("pi", 1, 2))
     ts(R("cw", 2, 512, 4), R("r16", 0, 128), cc(PM), A.is_equal)
     copy("a", R("cw", 3, 512, 4), R("cw", 2, 512, 4), scale=-1.0)
-    o_pm, o_u = take("off", 24), take("off", 24)
-    ts(o_pm, on(24), cc(PM), A.mult)
-    ts(R("wk0", 16, 32), R("r16", 0, 16), cc(PM), A.is_le, -4096.0, A.mult)
-    ts(R("wk0", 32, 48), R("r16", 0, 16), cc(PM), A.subtract, 1.0, A.is_equal)
+    o_u = take("off", 24)
+    ts(R("wk0", 0, 96), R("r16", 0, 96), cc(PM), A.is_le, -2.0, A.mult)
+    ts(R("wk0", 96, 192), R("r16", 0, 96), cc(PM), A.subtract, 1.0, A.is_equal)
     ts(cc(FX), cc(PM), 14.5, A.is_lt, 2048.0, A.mult)
-    copy("a", R("wk0", 32, 48), R("wk0", 32, 48), scale=2048.0)
-    tt(R("wk0", 0, 16), R("wk0", 16, 32), R("wk0", 32, 48), A.add)
+    tt(R("wk0", 0, 96), R("wk0", 0, 96), R("wk0", 96, 192), A.add)
+    for a in (0, 96):
+        copy("a", R("wk", a, a + 96), R("wk0", 0, 96), scale=2048.0)
     for k, c in enumerate((0, 1, 17)):
         memset(sub(o_u, 8 * k, 8 * k + 8), c)
-    act(R("wk", 0, 384), R("wk0", 0, 16), F.Copy, off=o_pm)
     quant(CW, R("cw", 0, 512))
     ts(cc(OH, 6), cc(V16, 6), cc(PM), A.add, 0.0, A.is_equal)
     ts(cc(OHM, 6), cc(OH, 6), 1008.0, A.mult, -1024.0, A.add)
     copy("a", cc(OHN, 6), cc(OH, 6), scale=-16.0)
-    fill(R("cx", 0, 512), 1.0)
     copy("a", R("cx", 0, 512, 4), R("cw", 0, 512, 4))
     quant(CX, R("cx", 0, 512))
-    fill(R("tr", 0, 512), 0.0)
     select(R("tr", 0, 512, 4), on(128), [[1, 128]], A.is_ge, -16, -1)
     quant(TR, R("tr", 0, 512))
-    fill(R("mt", 0, 288), 1.0)
     act(R("mt", 96, 192), R("idn", 0, 96), F.Identity, bias=1.0, scale=-2.0)
+    act(R("mz", 0, 96), R("idn", 0, 96), F.Identity, bias=1.0, scale=-1.0)
     act(R("tm", 0, 96), R("cw", 0, 384, 4), F.Identity, bias=-1.0)
     fill(R("cm", 0, 66), -1024.0)
     for a, b in ((0, 1), (5, 14), (20, 21), (26, 31), (32, 33), (42, 43), (49, 50), (62, 63)):
@@ -401,9 +418,6 @@ def rank_program(g, core, T, topo):
     for l in range(2):
         pick(R("ur", 128 * l, 128 * l + 128), R("uq", 0, 128), sub(o_u, 8 * l, 8 * l + 8))
         pick(R("ur", 256 + 128 * l, 384 + 128 * l), R("uv", 0, 32), sub(o_u, 16 * l, 16 * l + 8))
-    quant(R("nw0", 384, 512), on(512))
-    quant(R("s1", 192, 320), on(512))
-    quant(R("s1", 512, 640), on(512))
     quant(R("wq", 0, 128), R("wt", 0, 512))
     copy("a", cc(NM), cc(PM), scale=-1.0)
 
@@ -418,6 +432,7 @@ def rank_program(g, core, T, topo):
         quant(lq, R(tile, 4 * a0, 4 * (a0 + m)))
         mm(b, ONES, lq)
         wrap(bank(b, 0, a1 - a0), out)
+        return lq
 
     def own_products(b, win, wide, pb):
         mm(b, win, sub(win, 0, wide))
@@ -427,31 +442,29 @@ def rank_program(g, core, T, topo):
 
     def half(n, row, vals):
         h, K, pb = n // 2, 3, 128
-        s, sb, sn, cn = [take("col", K, pb) for i in range(4)]
+        s, cn = take("col", K, pb), take("col", K, pb)
         run = tf(h + K, pb)
         a = sub(run, h - 1, h - 1 + K)
-        xp = take("xp", 48, pb)
-        c0 = xp[3] // 4
-        sq = take("sq", 128)
-        for k in range(K - 1, -1, -1):
+        xp = take("xp", 64, pb)
+        sq = take("sq", 132)
+        fill(sub(xp, 35, 44, 4), -h / pb)
+        for k in range(K):
             sg = tb(n, pb)
             act(sg, row, F.Sign, bias=vals[k], scale=-1.0, acc=one(s, k))
-            if k == 0:
+            if k == K - 1:
                 eq = tb(n, pb)
                 ts(eq, row, vals[k], A.is_equal)
                 scan(sub(run, 0, h), sub(eq, 0, h), sub(eq, h, n), -float(n), A.add, A.add)
             else:
-                minus_abs_sum(one(a, k), sg)
-        act(sb, s, F.Identity, bias=0.5 - n)
-        act(sn, s, F.Identity, bias=0.5 - n, scale=-1.0)
-        tt(sub(xp, 0, 4 * K, 4), sb, a, A.is_lt)
-        tt(sub(xp, 20, 20 + 4 * K, 4), sn, a, A.is_gt)
-        fill(one(xp, 16), -h / pb)
-        scan(sub(xp, 5, 41, 4), cc(KS, 9, pb), sub(xp, 0, 36, 4), 0.0, A.mult, A.add)
-        quant(sq, R("xp", 0, 512))
-        mm(2, CW, sq)
+                minus_abs_sum(one(a, k + 1), sg)
+            ak = one(a, (k + 1) % K)
+            ts(sub(xp, k, 32, 4), cc(MK + 8 * k, 8), one(s, k), A.add, ak, A.is_lt)
+            ts(sub(xp, 32 + k, 64, 4), cc(MK + 24 + 8 * k, 8), one(s, k), A.subtract, ak, A.is_gt)
+        quant(sq, R("xp", 0, 528))
+        mm(2, ONES, sub(sq, 0, 128), True, False)
+        mm(2, C4, sub(sq, 4, 132), False, True)
         for k in range(K):
-            ts(one(cn, k), bank(2, c0 + k, c0 + k + 1, pb), bank(2, c0 + K, c0 + K + 1, pb), A.subtract, bank(2, c0 + 5 + k, c0 + 6 + k, pb), A.max)
+            ts(one(cn, k), bank(2, k, k + 1, pb), bank(2, K, K + 1, pb), A.subtract, bank(2, 8 + k, 9 + k, pb), A.max)
         out = take("off", n // 16)
         for side in range(2):
             for k in range(K):
@@ -478,7 +491,7 @@ def rank_program(g, core, T, topo):
             act(bound[k], R("tm", 0, 96, p1=96), F.Identity, bias=d[k], scale=e)
         for i in range(9):
             q, r = i // 3, i % 3
-            copy("av"[i & 1], sub(row, 32 * K * r, 32 * K * (r + 1), 1, 32 * q, 32 * q + 32), sub(tmp, 0, 32 * K, 1, 32 * r, 32 * r + 32))
+            copy(("aaaaaaaaa", "aavaavaav")[2 - K][i], sub(row, 32 * K * r, 32 * K * (r + 1), 1, 32 * q, 32 * q + 32), sub(tmp, 0, 32 * K, 1, 32 * r, 32 * r + 32))
         return row, [sub(row, k, 96 * K, K) for k in range(K)], d, bound
 
     def scores(wins, cols, ur):
@@ -487,6 +500,13 @@ def rank_program(g, core, T, topo):
         for k in range(K):
             mm(6 + k, wins[k], ur)
         mm(5, ur, cols)
+        if K == 1:
+            ge, eq, above, later = tb(n, 96), tb(n, 96), tb(n // 2, 96), tb(n, 96)
+            ts(ge, bank(5, 0, n, 96), bank(6, 0, 1, 96), A.is_ge)
+            ts(eq, bank(5, 0, n, 96), bank(6, 0, 1, 96), A.is_equal)
+            scan(above, sub(ge, 0, n // 2), sub(ge, n // 2, n), -n / 2, A.add, A.add)
+            scan(later, R("mz", 0, n, p1=96), eq, 0.0, A.mult, A.add)
+            return [(one(above, n // 2 - 1), one(later, n - 1))]
         sv, s, nx = take("col", K, 96), take("col", K, 96), []
         for k in range(K):
             copy("a", one(sv, k), bank(6 + k, 0, 1, 96))
@@ -500,7 +520,11 @@ def rank_program(g, core, T, topo):
 
     def member(l, t, a, b, sx, sent):
         out = R("xw", 720 * l + 4 * a + t, 720 * l + 4 * b, 4, p1=96)
-        if sent:
+        if l and sent:
+            ts(out, R("cm", 66 + a, 66 + b, p1=96), sx[0], A.add, sx[1], A.is_lt)
+        elif l:
+            ts(out, R("cm", a, b, p1=96), sx[0], A.add, sx[1], A.is_ge)
+        elif sent:
             ts(out, R("cm", a, b, p1=96), sx, A.is_gt)
         else:
             ts(out, R("cm", 66 + a, 66 + b, p1=96), sx, A.is_le)
@@ -539,12 +563,11 @@ def rank_program(g, core, T, topo):
             for k in range(K):
                 tt(cell(l, K * s + k, K * s + k), rows[k], bound[k], A.is_le)
         if l == 0:
-            sg = tb(192, 96)
-            act(sg, got[0][0], F.Sign, bias=got[1][2][0], scale=-1.0)
             for j in range(2):
-                act(cell(l, 2, j), sub(sg, j, 192, 2), F.Relu)
-                ts(cell(l, 3, j), got[0][1][j], got[1][2][1], A.is_lt)
+                sg = tb(192, 96)
+                act(sg, got[0][0], F.Sign, bias=got[1][2][j], scale=-1.0)
                 for k in range(2):
+                    act(cell(l, 2 + j, k), sub(sg, k, 192, 2), F.Relu)
                     ts(cell(l, k, 2 + j), got[1][1][j], got[0][2][k], A.is_le)
             quant(R("ca", 0, 192), R("xa", 0, 768))
             quant(R("ca", 192, 416), R("xa", 768, 1664))
@@ -574,24 +597,29 @@ def rank_program(g, core, T, topo):
         for k in range(4):
             ts(R(tile, k, 384, 4, p1=96), q, bank(1, c0 + k, c0 + k + 1, 96), A.is_ge)
             ts(R(tile, 384 + k, 768, 4, p1=96), q, bank(1, c0 + k, c0 + k + 1, 96), A.add, bank(1, c0 + 4 + k, c0 + 5 + k, 96), A.is_ge)
-        pa = take("col", 4, 96)
-        copy("v", pa, bank(1, c0 + 4, c0 + 8, 96))
+        pa = take("col", 8, 96)
+        copy("a", sub(pa, 4, 8), flags)
+        copy("v", sub(pa, 0, 4), bank(1, c0 + 4, c0 + 8, 96))
         out = take("off", 12)
-        listed(tile, 0, 192, 192, 0, out)
+        L["q", l + 1] = listed(tile, 0, 192, 192, 0, out)
         L["l", l + 1] = out
         L["a", l + 1] = pa
 
     def members(l):
         pa = L["a", l]
+        for k in range(4):
+            act(R("xg", 512 * l - 512 + k, 512 * l, 4, p1=96), on(128, 96), F.Copy, scale=one(pa, 4 + k))
+        sq = take("sq", 128)
+        quant(sq, R("xg", 512 * l - 512, 512 * l))
+        mm(3, sq, L["q", l])
+        L["z", l] = tf(192)
+        copy("a", L["z", l], bank(3, 0, 192))
         if l == 1:
-            out = take("off", 18)
+            L["s", 0] = take("off", 12)
             for k in range(2):
                 ts(R("xs", k, 384, 4, p1=96), R("qrow", 192, 288, p1=96), one(pa, k), A.add, cc(JB + k, 1, 96), A.is_ge)
-            for k in range(4):
-                ts(R("xs", 384 + k, 1152, 4, p1=96), R("qrow", 192, 384, p1=96), one(pa, k), A.is_ge)
-            listed("xs", 0, 288, 288, 3, out)
-            L["s", 0] = sub(out, 0, 12)
-            L["m", 1] = sub(out, 6, 18)
+                ts(R("xs", 384 + k, 768, 4, p1=96), R("qrow", 192, 288, p1=96), one(pa, k), A.is_ge)
+            listed("xs", 0, 192, 192, 3, L["s", 0])
         else:
             L["m", 2] = take("off", 6)
             for k in range(2):
@@ -725,9 +753,10 @@ def rank_program(g, core, T, topo):
         wrap(got, out)
         return out
 
-    def inverse(off, w):
+    def inverse(off, w, full=False):
         row = tf(w)
-        fill(row, 0.0)
+        if not full:
+            fill(row, 0.0)
         for a in range(0, width(off), 6):
             scatter(row, sub(off, a, a + 6), R("iot", 16 * a, 16 * a + 96))
         return row
@@ -736,9 +765,7 @@ def rank_program(g, core, T, topo):
         n = NS[l]
         h = n // 2
         if l:
-            place, z, y = inverse(L["m", l], UW[l]), tf(n), tf(n)
-            act(sub(z, h, n), place, F.Copy, off=sub(L["l", l], h // 16, n // 16))
-            copy("a", sub(z, 0, h), sub(z, h, n))
+            z, y = L["z", l], tf(n)
             act(sub(y, 0, h), z, F.Copy, off=L["p", l])
             copy("a", sub(y, h, n), sub(z, h, n))
             z = y
@@ -771,7 +798,9 @@ def rank_program(g, core, T, topo):
     v0 = children(0)
     up(1)
     v1 = children(1)
-    at1 = through(inverse(L["l", 1], UW[1]), L["m", 1])
+    z1, at1 = take("off", 12), take("off", 12)
+    wrap(L["z", 1], z1)
+    wrap(inverse(z1, 192, True), at1)
     candidates(1)
     members(2)
     up(2)

@@ -5,38 +5,38 @@ A = AluOpType
 F = ActivationFunctionType
 P = 384
 PART = [2, 1]
-NS = [384, 192, 192]
-AV = [384, 192, 192]
-BE = [576, 320, 320]
-SO = [0, 0, 320]
-PPO = [576, 480, 384]
+NS = [384, 192]
+AV = [384, 192]
+BE = 576
+PPO = [672, 576, 384]
 CO = [0, 192, 288]
 PAO = [0, 384, 576]
-UW = [384, 384, 352]
 WO = [0, 16, 34, 50]
+U = 2.0 ** 28
 X4, U8, F32, BF, U16, I32 = "float8_e4m3fn_x4", "uint8", "float32", "bfloat16", "uint16", "int32"
 
 SCRATCH = {"ps": ("psum", [128, 4096], F32)}
-for _n, _w in (("f", 512), ("s0", 768), ("s1", 768), ("pc", 768), ("nw0", 512), ("nwb", 224), ("nw1", 352), ("cq", 1536),
+for _n, _w in (("f", 512), ("s0", 768), ("s1", 1120), ("pc", 864), ("wm", 384), ("tq", 208), ("nw0", 512), ("nwb", 128), ("cq", 1536),
                ("lq", 1280), ("sq", 1672), ("uq", 128), ("uv", 32), ("ur", 512), ("wq", 128), ("fin", 384), ("dn1", 96),
-               ("ca", 416), ("cb", 256), ("wv", 360)):
+               ("ca", 416), ("cb", 416), ("wv", 180)):
     SCRATCH[_n] = ("sbuf", [128, _w], X4)
     SCRATCH[_n + "s"] = ("sbuf", [128, _w], U8)
 for _n, _w, _d in (("xt", 1536, BF), ("ut", 512, BF), ("wt", 512, BF), ("on", 512, BF), ("idn", 128, BF), ("cw", 512, BF),
-                   ("cx", 512, BF), ("tr", 512, BF), ("wkd", 160, BF), ("mt", 288, BF), ("tm", 96, BF), ("mz", 96, BF), ("cm", 132, BF),
+                   ("cx", 512, BF), ("tr", 832, BF), ("wkd", 160, BF), ("mt", 288, BF), ("tm", 96, BF), ("mz", 96, BF), ("cm", 132, BF),
                    ("et", 520, BF), ("eh", 520, BF), ("xp", 528, BF), ("xo", 512, BF), ("xl", 1536, BF), ("xm", 768, BF),
-                   ("xk", 512, BF), ("xc", 512, BF), ("xn", 768, BF), ("xs", 768, BF), ("xa", 1664, BF), ("xb", 1024, BF),
-                   ("xw", 1440, BF), ("ht", 1024, BF), ("r16", 128, BF), ("qrow", 384, BF), ("iot", 768, F32), ("pi", 2, I32),
-                   ("cc", 112, F32), ("c4", 512, BF), ("wk0", 192, BF), ("wk", 192, BF), ("xg", 1024, BF), ("off", 384, U16),
-                   ("col", 384, F32), ("tf", 20480, F32), ("tb", 16384, BF), ("pat", 672, F32), ("yt", 384, F32)):
+                   ("xk", 512, BF), ("xc", 512, BF), ("xs", 768, BF), ("xa", 1664, BF), ("xb", 1664, BF), ("xv", 1024, BF),
+                   ("c2", 512, BF), ("xw", 720, BF), ("ht", 1024, BF), ("r16", 128, BF), ("qrow", 384, BF), ("iot", 768, F32),
+                   ("pi", 2, I32), ("cc", 120, F32), ("zr", 256, BF), ("c4", 512, BF), ("wk0", 192, BF), ("wk", 192, BF),
+                   ("xg", 512, BF), ("off", 384, U16), ("col", 384, F32), ("tf", 20480, F32), ("tb", 16384, BF), ("pat", 672, F32),
+                   ("yt", 384, F32)):
     SCRATCH[_n] = ("sbuf", [128, _w], _d)
 
 SEMAPHORES = ["v", "a", "t", "g", "lx0", "lx1", "lx2", "lu", "lw", "lz", "sent", "aru", "ar0", "ar1", "ar2", "st1", "st3"]
 
-PM, FX, JA, JB, Q96, OH, OHM, QW, V16, NM, OHN, MK = 0, 1, 2, 5, 8, 10, 16, 22, 44, 57, 58, 64
+PM, FX, JA, JB, Q96, OH, OHM, QW, V16, NM, OHN, MK, OHQ, OHL = 0, 1, 2, 5, 8, 10, 16, 22, 44, 57, 58, 64, 34, 112
 CYC, HOP, FAR = 0.00095, 0.23, 0.9
 CASES = ((1.0, 0.23, 1.0), (0.87, 0.26, 0.85), (1.1, 0.21, 1.0), (1.3, 0.23, 1.5))
-PLANS, TRIES = {}, 4000
+PLANS, TRIES, MOVES = {}, 800, 14000
 
 
 def R(name, c0, c1, step=1, p0=0, p1=128):
@@ -162,6 +162,39 @@ def arrange(ops):
             t, now = span(order)
             if t <= least:
                 bonus, best, least, held = other, order, t, now
+        now, cost = best, least
+        for turn in range(MOVES):
+            seed = (seed * 1103515245 + 12345) % 2147483648
+            j, i = held[seed // 64 % len(held)]
+            a, b = now.index(j), now.index(i)
+            if seed // 4096 & 1:
+                for k in range(seed // 8192 % 3):
+                    a = max([x for x in range(max(a - 40, 0), a) if queues[now[x]] == queues[i]] + [-1])
+                    if a < 0:
+                        a = now.index(j)
+                        break
+                go = {i}
+                for x in now[b - 1:a - 1 if a else None:-1]:
+                    if go.intersection(post[x]):
+                        go.add(x)
+                if now[a] in go:
+                    continue
+                order = now[:a] + [x for x in now[a:b + 1] if x in go] + [x for x in now[a:b + 1] if x not in go] + now[b + 1:]
+            else:
+                for k in range(seed // 8192 % 4):
+                    b = min([x for x in range(b + 1, min(b + 40, n)) if queues[now[x]] == queues[i]] + [n - 1])
+                go = {j}
+                for x in now[a + 1:b + 1]:
+                    if go.intersection(ops[x]["pre"]):
+                        go.add(x)
+                if i in go:
+                    continue
+                order = now[:a] + [x for x in now[a:b + 1] if x not in go] + [x for x in now[a:b + 1] if x in go] + now[b + 1:]
+            t, got = span(order)
+            if t <= cost + 0.25 * (1 - turn / MOVES) * (seed // 16 % 4 == 0):
+                now, cost, held = order, t, got
+                if t < least:
+                    best, least = order, t
         PLANS[n] = best
     return PLANS[n]
 
@@ -319,7 +352,7 @@ def rank_program(g, core, T, topo):
         dma("y", ap(out).bitcast(dt.uint8) if raw else ap(out), ap(in_).bitcast(dt.uint8) if raw else ap(in_), [in_], [out], "lz")
         ops[-1]["lat"] = 3 * FAR
 
-    CW, ONES, CX, TR = R("cq", 0, 128), R("f", 384, 512), R("cq", 1280, 1408), R("cq", 1408, 1536)
+    CW, ONES, CX, C2, TR = R("cq", 0, 128), R("f", 384, 512), R("cq", 1280, 1408), R("cq", 1408, 1536), R("tq", 0, 208)
     C4 = R("cq", 128, 256)
 
     def ET(b):
@@ -354,22 +387,26 @@ def rank_program(g, core, T, topo):
     iota(R("iot", 0, 768), [[1, 768]], 0, 0)
     memset(R("xp", 0, 528), 0.0)
     memset(R("xm", 0, 768), 0.0)
-    for name, a, b, p in (("xa", 0, 768, 96), ("xa", 768, 1536, 96), ("xa", 1536, 1664, 0), ("xw", 0, 720, 0), ("xn", 0, 768, 96),
-                          ("xg", 0, 512, 96), ("xg", 512, 1024, 96), ("xs", 0, 768, 96), ("ht", 0, 128, 0), ("ht", 896, 1024, 0)):
+    for name, a, b, p in (("xa", 0, 768, 96), ("xa", 768, 1536, 96), ("xa", 1536, 1664, 0), ("xw", 0, 720, 0), ("xg", 0, 512, 96),
+                          ("xs", 0, 768, 96), ("ht", 0, 128, 0), ("ht", 896, 1024, 0), ("zr", 0, 256, 0)):
         lay(R(name, a, b, 1, p, 128), R("xm", 0, b - a, 1, p, 128))
     lay(R("mt", 0, 96), on(96))
     lay(R("mt", 192, 288), on(96))
-    for name, a in (("nw0", 384), ("s1", 192), ("s1", 512)):
+    for name, a in (("nw0", 384), ("s1", 192)):
         lay(R(name, a, a + 128), ONES)
         lay(sc(R(name, a, a + 128)), sc(ONES))
-    for name, a, b in (("xo", 0, 512), ("xw", 720, 1440), ("xb", 0, 1024), ("xk", 0, 512), ("xc", 0, 512), ("tr", 0, 512)):
+    for name, a, b in (("xo", 0, 512), ("xb", 0, 1664), ("xk", 0, 512), ("xc", 0, 512), ("tr", 0, 832)):
         flat(name, a, b)
     flat("cx", 0, 512, 1)
     for t in (2, 3):
         fill(R("xs", t, 768, 4, p1=96), 0.0)
-    for k in range(4):
-        fill(R("xn", 192 * k, 192 * k + 192, 4, 96, 128), -2.0 if k & 1 else 1.0)
-    fill(R("xk", 0, 384, 4, 96, 128), 1.0)
+    for k, t in enumerate((2, 3, 3, 2)):
+        copy("a", R("xb", 384 * k + t, 384 * k + 384, 4, p1=96), R("idn", 0, 96, p1=96), scale=-64.0)
+    for t in range(2):
+        fill(R("xb", t, 1536, 4, 96, 128), 1.0)
+    for t, c in enumerate((-U / 2, U / 64, 0.0, 0.0)):
+        fill(R("xv", t, 1024, 4, 96, 128), c)
+    quant(R("wm", 128, 256), R("xc", 0, 512))
     fill(R("xl", 3, 1536, 4), 0.0)
     fill(R("cw", 1, 512, 4), 1.0)
     fill(cc(MK, 24), 8192.5 - P)
@@ -396,10 +433,16 @@ def rank_program(g, core, T, topo):
     ts(cc(OH, 6), cc(V16, 6), cc(PM), A.add, 0.0, A.is_equal)
     ts(cc(OHM, 6), cc(OH, 6), 1008.0, A.mult, -1024.0, A.add)
     copy("a", cc(OHN, 6), cc(OH, 6), scale=-16.0)
+    copy("a", cc(OHL, 6), cc(OH, 6), scale=207.5)
+    tt(cc(OHQ, 6), cc(OH, 6), cc(QW, 6), A.mult)
     copy("a", R("cx", 0, 512, 4), R("cw", 0, 512, 4))
     quant(CX, R("cx", 0, 512))
-    select(R("tr", 0, 512, 4), on(128), [[1, 128]], A.is_ge, -16, -1)
-    quant(TR, R("tr", 0, 512))
+    for t in range(2):
+        select(R("tr", t, 832, 2, p1=96), on(416, 96), [[1, 208], [0, 2]], A.is_ge, -16 - 96 * t, -1)
+    quant(TR, R("tr", 0, 832))
+    for t in range(4):
+        copy("a", R("c2", t, 512, 4), R("cw", max(t, 2), 512, 4))
+    quant(C2, R("c2", 0, 512))
     act(R("mt", 96, 192), R("idn", 0, 96), F.Identity, bias=1.0, scale=-2.0)
     act(R("mz", 0, 96), R("idn", 0, 96), F.Identity, bias=1.0, scale=-1.0)
     act(R("tm", 0, 96), R("cw", 0, 384, 4), F.Identity, bias=-1.0)
@@ -491,7 +534,7 @@ def rank_program(g, core, T, topo):
             act(bound[k], R("tm", 0, 96, p1=96), F.Identity, bias=d[k], scale=e)
         for i in range(9):
             q, r = i // 3, i % 3
-            copy(("aaaaaaaaa", "aavaavaav")[2 - K][i], sub(row, 32 * K * r, 32 * K * (r + 1), 1, 32 * q, 32 * q + 32), sub(tmp, 0, 32 * K, 1, 32 * r, 32 * r + 32))
+            copy("av"[i & 1], sub(row, 32 * K * r, 32 * K * (r + 1), 1, 32 * q, 32 * q + 32), sub(tmp, 0, 32 * K, 1, 32 * r, 32 * r + 32))
         return row, [sub(row, k, 96 * K, K) for k in range(K)], d, bound
 
     def scores(wins, cols, ur):
@@ -506,7 +549,9 @@ def rank_program(g, core, T, topo):
             ts(eq, bank(5, 0, n, 96), bank(6, 0, 1, 96), A.is_equal)
             scan(above, sub(ge, 0, n // 2), sub(ge, n // 2, n), -n / 2, A.add, A.add)
             scan(later, R("mz", 0, n, p1=96), eq, 0.0, A.mult, A.add)
-            return [(one(above, n // 2 - 1), one(later, n - 1))]
+            y = take("col", 1, 96)
+            ts(y, one(above, n // 2 - 1), one(later, n - 1), A.subtract)
+            return y
         sv, s, nx = take("col", K, 96), take("col", K, 96), []
         for k in range(K):
             copy("a", one(sv, k), bank(6 + k, 0, 1, 96))
@@ -518,113 +563,71 @@ def rank_program(g, core, T, topo):
             nx.append(one(run, n - 1))
         return nx
 
-    def member(l, t, a, b, sx, sent):
-        out = R("xw", 720 * l + 4 * a + t, 720 * l + 4 * b, 4, p1=96)
-        if l and sent:
-            ts(out, R("cm", 66 + a, 66 + b, p1=96), sx[0], A.add, sx[1], A.is_lt)
-        elif l:
-            ts(out, R("cm", a, b, p1=96), sx[0], A.add, sx[1], A.is_ge)
-        elif sent:
-            ts(out, R("cm", a, b, p1=96), sx, A.is_gt)
-        else:
-            ts(out, R("cm", 66 + a, 66 + b, p1=96), sx, A.is_le)
+    def cell(t, j):
+        return R("xa", 384 * j + t, 384 * j + 384, 4, p1=96)
 
-    def cell(l, t, j):
-        return R("xb", 512 * j + t, 512 * j + 384, 4, p1=96) if l else R("xa", 384 * j + t, 384 * j + 384, 4, p1=96)
-
-    def candidates(l):
-        if l == 0:
-            quant(R("nw0", 0, 192), R("ht", 128, 896))
-            exchange([(R("nw0", 0, 192), R("nw0", 192, 384), PART[l])], "ar0")
-            quant(R("nwb", 0, 224), R("ht", 128, 1024))
-            wins = [[R("nwb", 0, 128), R("nwb", 96, 224)], [R("nw0", 192, 320), R("nw0", 288, 416)]]
-            cols = [R("nwb", 0, 192), R("nw0", 192, 384)]
-        else:
-            quant(R("nw1", 0, 128), R("ht", 0, 512))
-            exchange([(R("nw1", 32, 128), R("nw1", 128, 224), PART[l])], "ar1")
-            quant(R("nw1", 224, 352), R("ht", 128, 640))
-            wins = [[R("nw1", 224, 352)], [R("nw1", 128, 256)]]
-            cols = [wins[0][0], wins[1][0]]
-        K = 2 - l
+    def candidates():
+        quant(R("nw0", 0, 192), R("ht", 128, 896))
+        exchange([(R("nw0", 0, 192), R("nw0", 192, 384), PART[0])], "ar0")
+        quant(R("nwb", 0, 128), R("ht", 512, 1024))
+        wins = [[R("nw0", 0, 128), R("nwb", 0, 128)], [R("nw0", 192, 320), R("nw0", 288, 416)]]
+        cols = [R("nw0", 0, 192), R("nw0", 192, 384)]
         got = []
         for s in range(2):
             row, rows, d, bound = sizes(wins[s])
-            sx = scores(wins[s], cols[s], R("ur", 256 * s + 128 * l, 256 * s + 128 * l + 128))
+            sx = scores(wins[s], cols[s], R("ur", 256 * s, 256 * s + 128))
             got.append((row, rows, d))
-            if l == 0:
-                for k in range(2):
-                    member(l, 2 * s + k, 0, 66, sx[k], s == 1)
-                ts(cell(l, 2 * s, 2 * s + 1), rows[1], d[0], A.is_le)
-                ts(cell(l, 2 * s + 1, 2 * s), rows[0], d[1], A.is_lt)
-            else:
-                member(l, s, 0, 34, sx[0], s == 1)
-                member(l, s, 34, 66, sx[0], s == 0)
-                member(l, 3 - s, 32, 66, sx[0], s == 0)
-            for k in range(K):
-                tt(cell(l, K * s + k, K * s + k), rows[k], bound[k], A.is_le)
-        if l == 0:
-            for j in range(2):
-                sg = tb(192, 96)
-                act(sg, got[0][0], F.Sign, bias=got[1][2][j], scale=-1.0)
-                for k in range(2):
-                    act(cell(l, 2 + j, k), sub(sg, k, 192, 2), F.Relu)
-                    ts(cell(l, k, 2 + j), got[1][1][j], got[0][2][k], A.is_le)
-            quant(R("ca", 0, 192), R("xa", 0, 768))
-            quant(R("ca", 192, 416), R("xa", 768, 1664))
-            cw = [R("ca", 96 * k, 96 * k + 128) for k in range(4)]
-        else:
-            ts(cell(l, 1, 0), got[0][0], got[1][2][0], A.is_lt)
-            ts(cell(l, 2, 0), got[0][0], got[1][2][0], A.is_equal)
-            ts(cell(l, 0, 1), got[1][0], got[0][2][0], A.is_le)
-            ts(cell(l, 3, 1), got[1][0], got[0][2][0], A.is_equal, -1.0, A.mult)
             for k in range(2):
-                quant(R("cb", 128 * k, 128 * k + 128), R("xb", 512 * k, 512 * k + 512))
-            cw = [R("cb", 128 * k, 128 * k + 128) for k in (0, 1, 1, 0)]
-        quant(R("wv", 180 * l, 180 * l + 178), R("xw", 720 * l, 720 * l + 712))
+                out = R("xw", 2 * s + k, 264, 4, p1=96)
+                if s:
+                    ts(out, R("cm", 0, 66, p1=96), sx[k], A.is_gt)
+                else:
+                    ts(out, R("cm", 66, 132, p1=96), sx[k], A.is_le)
+                tt(cell(2 * s + k, 2 * s + k), rows[k], bound[k], A.is_le)
+            ts(cell(2 * s, 2 * s + 1), rows[1], d[0], A.is_le)
+            ts(cell(2 * s + 1, 2 * s), rows[0], d[1], A.is_lt)
+        for j in range(2):
+            sg = tb(192, 96)
+            act(sg, got[0][0], F.Sign, bias=got[1][2][j], scale=-1.0)
+            for k in range(2):
+                act(cell(2 + j, k), sub(sg, k, 192, 2), F.Relu)
+                ts(cell(k, 2 + j), got[1][1][j], got[0][2][k], A.is_le)
+        quant(R("ca", 0, 192), R("xa", 0, 768))
+        quant(R("ca", 192, 416), R("xa", 768, 1664))
+        quant(R("wv", 0, 178), R("xw", 0, 712))
         for k in range(4):
-            mm(2, cw[k], R("wv", 180 * l + WO[k], 180 * l + WO[k] + 128), k == 0, k == 3)
+            mm(2, R("ca", 96 * k, 96 * k + 128), R("wv", WO[k], WO[k] + 128), k == 0, k == 3)
         xp, thr, sq = take("xp", 32, 96), take("col", 16, 96), take("sq", 128)
         c0 = xp[3] // 4
-        flags = R("xw", 720 * l + 128, 720 * l + 132, p1=96)
+        flags = R("xw", 128, 132, p1=96)
         copy("a", sub(xp, 16, 32, 4), flags)
         for k in range(1, 4):
             copy("a", sub(xp, 17 + 4 * k, 17 + 5 * k), sub(flags, 0, k))
-        act(thr, sub(xp, 16, 32), F.Identity, bias=1000.0, scale=(96.5 if l == 0 else 48.5) - 1000.0)
+        act(thr, sub(xp, 16, 32), F.Identity, bias=1000.0, scale=96.5 - 1000.0)
         tt(sub(xp, 0, 16), bank(2, 0, 16, 96), thr, A.is_gt)
         quant(sq, R("xp", 0, 512))
         mm(1, CX, sq)
-        tile, q = "xm" if l == 0 else "xn", R("qrow", 192, 288, p1=96)
+        q = R("qrow", 192, 288, p1=96)
         for k in range(4):
-            ts(R(tile, k, 384, 4, p1=96), q, bank(1, c0 + k, c0 + k + 1, 96), A.is_ge)
-            ts(R(tile, 384 + k, 768, 4, p1=96), q, bank(1, c0 + k, c0 + k + 1, 96), A.add, bank(1, c0 + 4 + k, c0 + 5 + k, 96), A.is_ge)
+            ts(R("xm", k, 384, 4, p1=96), q, bank(1, c0 + k, c0 + k + 1, 96), A.is_ge)
+            ts(R("xm", 384 + k, 768, 4, p1=96), q, bank(1, c0 + k, c0 + k + 1, 96), A.add, bank(1, c0 + 4 + k, c0 + 5 + k, 96), A.is_ge)
         pa = take("col", 8, 96)
         copy("a", sub(pa, 4, 8), flags)
         copy("v", sub(pa, 0, 4), bank(1, c0 + 4, c0 + 8, 96))
-        out = take("off", 12)
-        L["q", l + 1] = listed(tile, 0, 192, 192, 0, out)
-        L["l", l + 1] = out
-        L["a", l + 1] = pa
-
-    def members(l):
-        pa = L["a", l]
+        L["l", 1] = take("off", 12)
+        lq = listed("xm", 0, 192, 192, 0, L["l", 1])
         for k in range(4):
-            act(R("xg", 512 * l - 512 + k, 512 * l, 4, p1=96), on(128, 96), F.Copy, scale=one(pa, 4 + k))
+            act(R("xg", k, 512, 4, p1=96), on(128, 96), F.Copy, scale=one(pa, 4 + k))
         sq = take("sq", 128)
-        quant(sq, R("xg", 512 * l - 512, 512 * l))
-        mm(3, sq, L["q", l])
-        L["z", l] = tf(192)
-        copy("a", L["z", l], bank(3, 0, 192))
-        if l == 1:
-            L["s", 0] = take("off", 12)
-            for k in range(2):
-                ts(R("xs", k, 384, 4, p1=96), R("qrow", 192, 288, p1=96), one(pa, k), A.add, cc(JB + k, 1, 96), A.is_ge)
-                ts(R("xs", 384 + k, 768, 4, p1=96), R("qrow", 192, 288, p1=96), one(pa, k), A.is_ge)
-            listed("xs", 0, 192, 192, 3, L["s", 0])
-        else:
-            L["m", 2] = take("off", 6)
-            for k in range(2):
-                ts(R("xk", k, 384, 4, p1=96), R("qrow", 192, 288, p1=96), one(pa, k), A.is_ge)
-            listed("xk", 0, 96, 128, 3, L["m", 2])
+        quant(sq, R("xg", 0, 512))
+        mm(3, sq, lq)
+        L["z"] = tf(192)
+        copy("a", L["z"], bank(3, 0, 192))
+        L["s"] = take("off", 12)
+        for k in range(2):
+            ts(R("xs", k, 384, 4, p1=96), q, one(pa, k), A.add, cc(JB + k, 1, 96), A.is_ge)
+            ts(R("xs", 384 + k, 768, 4, p1=96), q, one(pa, k), A.is_ge)
+        listed("xs", 0, 192, 192, 3, L["s"])
 
     def count(src, func, bias, scale, cnt, hi):
         n, pb = width(src), src[2]
@@ -653,9 +656,6 @@ def rank_program(g, core, T, topo):
 
     L = {}
 
-    def S(l, a, b):
-        return R("s1" if l else "s0", SO[l] + a, SO[l] + b)
-
     def casts(h, scale):
         for b in range(4):
             copy("va"[b & 1], R("ht", 128 + b, 128 + 4 * h, 4), bank(4 + b, 0, h), scale=scale)
@@ -674,148 +674,217 @@ def rank_program(g, core, T, topo):
         L["l", 0] = half(P, row, vals)
 
     def up(l):
-        n = NS[l]
+        n, s = NS[l], "s%d" % l
         h = n // 2
         m = max(h, 128)
-        lw, win = L["l", l], R(("f", "nw0", "nw1")[l], 0, UW[l])
+        lw, win = L["l", l], R(("f", "nw0")[l], 0, P)
         if l == 0:
-            pick(S(l, 0, h), win, sub(lw, 0, h // 16))
-            pick(S(l, h, n), win, sub(lw, h // 16, n // 16))
+            pick(R(s, 0, h), win, sub(lw, 0, h // 16))
+            pick(R(s, h, n), win, sub(lw, h // 16, n // 16))
         else:
-            pick(S(l, 0, n), win, lw)
-        K, pb, hp = [(2, 96, 192), (1, 96, 96), (2, 48, 48)][l]
+            pick(R(s, 0, n), win, lw)
+        K, pb = h // 96, 96
         par, hi = take("col", K, pb), take("col", K, pb)
         for k in range(K):
-            a = h + (hp * k if l == 2 else 0)
-            mm(k, S(l, pb * k, pb * k + 128), S(l, a, a + m))
-            pad = 64 if l == 2 and k else 16
-            rm = tf(pad + hp, pb)
-            fill(sub(rm, 0, pad), -1e29)
-            scan(sub(rm, pad, pad + hp), bank(k, 0, hp, pb), on(hp, pb), -1e29, A.max, A.mult)
-            count(rm, F.Sign, one(rm, pad + hp - 1), -1.0, one(par, k), one(hi, k))
-        L["par", l] = par
+            mm(k, R(s, pb * k, pb * k + 128), R(s, h, h + m))
+            rm = tf(16 + h, pb)
+            fill(sub(rm, 0, 16), -1e29)
+            scan(sub(rm, 16, 16 + h), bank(k, 0, h, pb), on(h, pb), -1e29, A.max, A.mult)
+            count(rm, F.Sign, one(rm, 15 + h), -1.0, one(par, k), one(hi, k))
         for b in range(4):
-            mm(4 + b, ET(b), S(l, 0, m), True, False)
+            mm(4 + b, ET(b), R(s, 0, m), True, False)
         pw = take("off", h // 16)
         L["p", l] = pw
         ts(pw, spread(par, hi, K, pb, "xp", 2), float(h - 16), A.add)
-        pick(R("pc", PPO[l], PPO[l] + h), S(l, 0, n), pw)
+        pick(R("pc", PPO[l], PPO[l] + h), R(s, 0, n), pw)
         for b in range(4):
             mm(4 + b, EH(b), R("pc", PPO[l], PPO[l] + m), False, True)
         casts(h, None)
-        if l == 2:
-            quant(S(l, BE[l], BE[l] + 128), R("ht", 128, 640))
+
+    def last_level():
+        quant(R("s1", 320, 448), R("ht", 0, 512))
+        exchange([(R("s1", 352, 448), R("s1", 448, 544), PART[1])], "ar1")
+        quant(R("s1", 544, 672), R("ht", 128, 640))
+        wins = [R("s1", 544, 672), R("s1", 448, 576)]
+        rows, ds, fl, ks = [], [], [], []
+
+        def at(t, j):
+            return R("xb", 384 * j + t, 384 * j + 384, 4, p1=96)
+        for s in range(2):
+            row, unused, d, bound = sizes([wins[s]])
+            y = scores([wins[s]], wins[s], R("ur", 256 * s + 128, 256 * s + 256))
+            rows.append(row)
+            ds.append(d[0])
+            tt(at(s, s), row, bound[0], A.is_le)
+            copy("a", at(s, 3 - s), at(s, s))
+            c = take("col", 6, 96)
+            for f in range(2):
+                ts(R("xv", 512 * f + s, 512 * f + 512, 2, p1=96), R("zr", 0, 256, p1=96), y, A.is_gt if f != s else A.is_le, -U, A.mult)
+                w = R("xv", 512 * f + s, 512 * f + s + 1, p1=96)
+                copy("a", one(c, f), w, scale=-2.0 ** -42 / U)
+                copy("a", one(c, 3 - f), w, scale=1e29 / U)
+            copy("a", one(c, 4), w, scale=-96.0 / U)
+            fl.append(c)
+        ts(at(0, 1), rows[1], ds[0], A.is_le)
+        ts(at(0, 2), rows[1], ds[0], A.is_lt)
+        ts(at(1, 0), rows[0], ds[1], A.is_lt)
+        ts(at(1, 3), rows[0], ds[1], A.is_le)
+        quant(R("cb", 0, 192), R("xb", 0, 768))
+        quant(R("cb", 192, 416), R("xb", 768, 1664))
+        for f in range(2):
+            quant(R("wm", 256 * f, 256 * f + 128), R("xv", 512 * f, 512 * f + 512))
+            mm((2, 7)[f], R("wm", 256 * f, 256 * f + 128), R("cb", 192 * f, 192 * f + 192))
+        par, hi = take("col", 2, 96), take("col", 2, 96)
+        for s in range(2):
+            mm(s, wins[s], R("s1", 352, 640))
+            ms, rm = [tf(192, 96), tf(192, 96)], tf(208, 96)
+            for f in range(2):
+                gs = tf(192, 96)
+                act(gs, bank(s, 96 * f, 96 * f + 192, 96), F.Identity, bias=one(fl[s], 2 + f), scale=one(fl[s], f))
+                tt(ms[f], bank((2, 7)[f], 0, 192, 96), gs, A.min)
+            fill(sub(rm, 0, 16), -1e29)
+            scan(sub(rm, 16, 208), ms[0], ms[1], -1e29, A.max, A.max)
+            count(rm, F.Sign, one(rm, 207), -1.0, one(par, s), one(hi, s))
+            mm(4 + s, R("cb", 96 * s, 96 * s + 128), R("wm", 126, 254), True, False)
+            mm(4 + s, R("cb", 288 - 96 * s, 416 - 96 * s), R("wm", 130, 258), False, True)
+            k = take("col", 2, 96)
+            for f in range(2):
+                ts(one(k, f), bank(4 + s, 126 * f, 126 * f + 1, 96), 0.0, A.max, one(fl[s], 2 + f), A.subtract)
+            ks.append(k)
+
+        def digits(xp, cnt, sixteens, shift):
+            act(sub(xp, 1, 24, 4), cc(OH, 6, 96), F.Copy, scale=shift)
+            act(sub(xp, 2, 24, 4), cc(OHM, 6, 96), F.Relu, bias=cnt, scale=sixteens)
+            ts(sub(xp, 3, 24, 4), cc(OHN, 6, 96), sixteens, A.mult)
+        xp, sq, pw = take("xp", 48, 96), take("sq", 128), take("off", 12)
+        for s in range(2):
+            digits(sub(xp, 24 * s, 24 * s + 24), one(par, s), one(hi, s), one(fl[s], 4))
+        quant(sq, R("xp", 0, 512))
+        mm(2, C2, sq)
+        ts(pw, bank(2, xp[3] // 4, xp[4] // 4), 336.0, A.add)
+        for b in range(4):
+            mm(4 + b, ET(b), R("s1", 352, 544), True, False)
+        pick(R("pc", 384, 576), R("s1", 0, 672), pw)
+        for b in range(4):
+            mm(4 + b, EH(b), R("pc", 384, 576), False, True)
+        casts(192, None)
+        quant(R("s1", 672, 864), R("ht", 128, 896))
+        quant(R("s1", 864, 992), R("ht", 128, 640))
+        for t, (s, f) in enumerate(((0, 0), (1, 0), (1, 1), (0, 1))):
+            ts(R("xc", t, 384, 4, p1=96), R("iot", 16 + 96 * f, 112 + 96 * f, p1=96), one(par, s), A.subtract, one(ks[s], f), A.is_equal)
+        sq, cnt, hi, kind = take("sq", 128), take("col", 1, 96), take("col", 1, 96), take("col", 2, 96)
+        quant(sq, R("xc", 0, 512))
+        mm(0, sq, TR)
+        count(bank(0, 0, 208, 96), F.Relu, 1.0, -1.0, cnt, hi)
+        xo, sq = take("xo", 48, 96), take("sq", 128)
+        digits(sub(xo, 0, 24), cnt, hi, one(fl[0], 4))
+        ts(one(kind, 0), one(ks[0], 0), one(ks[0], 1), A.min, 0.0, A.is_equal)
+        ts(sub(xo, 25, 48, 4), cc(OH, 6, 96), one(kind, 0), A.mult, 320.0, A.mult)
+        ts(sub(xo, 24, 48, 4), cc(OHL, 6, 96), cnt, A.is_gt, 640.0, A.mult)
+        copy("a", sub(xo, 26, 48, 4), cc(OHQ, 6, 96))
+        act(sub(xo, 27, 48, 4), cc(OH, 6, 96), F.Copy, scale=cc(NM, 1, 96))
+        quant(sq, R("xo", 0, 512))
+        mm(1, C2, sq)
+        c0, ends = xo[3] // 4, take("off", 6)
+        L["c", 2] = take("off", 6)
+        ts(L["c", 2], bank(1, c0, c0 + 6), 656.0, A.add)
+        copy("v", ends, bank(1, c0 + 6, c0 + 12))
+        xp, sq, pa, z = take("xp", 8, 96), take("sq", 128), take("col", 4, 96), tf(832)
+        for e, s in ((0, 0), (4, 1), (5, 0)):
+            copy("a", one(xp, e), one(fl[s], 0), scale=2.0 ** 42)
+        quant(sq, R("xp", 0, 512))
+        mm(3, CX, sq)
+        copy("v", sub(pa, 0, 2), bank(3, xp[3] // 4, xp[3] // 4 + 2, 96))
+        for s in range(2):
+            ts(one(pa, 2 + s), one(pa, s), one(ks[s], 0), A.add)
+            ts(R("xk", s, 384, 4, p1=96), R("qrow", 192, 288, p1=96), one(pa, s), A.is_ge)
+            ts(R("xk", 2 + s, 384, 4, p1=96), R("qrow", 193, 289, p1=96), one(pa, 2 + s), A.is_equal, 288.0, A.mult)
+        by = take("off", 6)
+        listed("xk", 0, 96, 128, 3, by)
+        mm(3, R("wm", 0, 128), TR)
+        act(sub(z, 352, 544), bank(3, 16, 208), F.Identity, bias=-1.0, scale=-0.5 / U)
+        fill(sub(z, 544, 640), 0.0)
+        act(sub(z, 640, 832), sub(z, 0, 640), F.Copy, off=pw)
+        act(R("pat", PAO[2], PAO[2] + 96), sub(z, 352, 832), F.Copy, off=by)
+        return ends
 
     def children(l):
         h = NS[l] // 2
         K, pb, k16 = h // 96, 96, h // 16
         prow, cnt, hi = tb(h), take("col", K, pb), take("col", K, pb)
-        if l == 2:
-            for k in range(2):
-                ts(R("xc", 192 * k, 192 * k + 192, 4, p1=48), R("qrow", 208 + 48 * k, 256 + 48 * k, p1=48), one(L["par", l], k), A.is_equal)
-            sq = take("sq", 128)
-            quant(sq, R("xc", 0, 512))
-            mm(0, sq, TR)
-            count(bank(0, 0, 64, pb), F.Relu, 1.0, -1.0, cnt, hi)
-        else:
-            act(prow, R("iot", 0, 2 * h), F.Identity, bias=-float(h), off=L["p", l])
-        for k in range(K if l < 2 else 0):
+        act(prow, R("iot", 0, 2 * h), F.Identity, bias=-float(h), off=L["p", l])
+        for k in range(K):
             ne, cp = tb(h, pb), tb(h + 16, pb)
             fill(sub(cp, 0, 16), 1.0)
             ts(ne, sub(prow, 0, h, 1, 0, pb), cc(Q96 + k, 1, pb), A.not_equal)
             scan(sub(cp, 16, h + 16), ne, ne, 1.0, A.mult, A.mult)
             count(cp, F.Copy, 0.0, 1.0, one(cnt, k), one(hi, k))
-        both = spread(cnt, hi, K, pb, "xo", 1 if l == 2 else 3, under=(h if l < 2 else 48) + 15.5, step=float(AV[l] - h))
-        res = sub(both, 0, k16)
+        both = spread(cnt, hi, K, pb, "xo", 3, under=h + 15.5, step=float(AV[l] - h))
         mw, ow, v = take("off", k16), take("off", k16), tf(2 * h)
         L["c", l] = mw
-        if l == 2:
-            for k in range(2):
-                ts(sub(mw, 3 * k, 3 * k + 3), sub(res, 3 * k, 3 * k + 3), float(BE[l] + 48 * k - 16), A.add)
-            copy("a", sub(v, 0, h), R("iot", BE[l], BE[l] + h))
-        else:
-            ts(mw, res, -16.0, A.add, float(h - 1), A.min)
+        ts(mw, sub(both, 0, k16), -16.0, A.add, float(h - 1), A.min)
         if l == 0:
             for a in range(0, h, 96):
-                scatter(sub(v, 0, h), sub(L["s", l], a // 16, a // 16 + 6), R("iot", BE[l] + a, BE[l] + a + 96))
+                scatter(sub(v, 0, h), sub(L["s"], a // 16, a // 16 + 6), R("iot", BE + a, BE + a + 96))
             L["c", l] = through(sub(v, 0, h), mw)
         ts(ow, sub(both, k16, 2 * k16), float(h), A.add)
-        act(sub(v, h, 2 * h), R("iot", 0, BE[l]), F.Copy, off=ow)
+        act(sub(v, h, 2 * h), R("iot", 0, BE), F.Copy, off=ow)
         return v
 
-    def through(row, off, bias=None):
+    def through(row, off):
         n = 16 * width(off)
         got, out = tf(n), take("off", n // 16)
-        if bias is None:
-            act(got, row, F.Copy, off=off)
-        else:
-            act(got, row, F.Identity, bias=bias, off=off)
+        act(got, row, F.Copy, off=off)
         wrap(got, out)
         return out
-
-    def inverse(off, w, full=False):
-        row = tf(w)
-        if not full:
-            fill(row, 0.0)
-        for a in range(0, width(off), 6):
-            scatter(row, sub(off, a, a + 6), R("iot", 16 * a, 16 * a + 96))
-        return row
 
     def parents(l, fw):
         n = NS[l]
         h = n // 2
         if l:
-            z, y = L["z", l], tf(n)
-            act(sub(y, 0, h), z, F.Copy, off=L["p", l])
-            copy("a", sub(y, h, n), sub(z, h, n))
-            z = y
+            z = tf(n)
+            act(sub(z, 0, h), L["z"], F.Copy, off=L["p", l])
+            copy("a", sub(z, h, n), sub(L["z"], h, n))
         else:
-            z, pr = tf(BE[l] + h), tf(h)
+            z, pr = tf(BE + h), tf(h)
             for a in range(0, n, 96):
                 act(sub(z, a, a + 96), R("iot", 0, n), F.Copy, off=sub(L["l", l], a // 16, a // 16 + 6))
             copy("a", sub(z, AV[l], AV[l] + h), sub(z, h, n))
             act(pr, sub(z, 0, n), F.Copy, off=L["p", l])
-            act(sub(z, BE[l], BE[l] + h), pr, F.Copy, off=L["s", l])
-        for a in range(0, P >> l, 96):
+            act(sub(z, BE, BE + h), pr, F.Copy, off=L["s"])
+        for a in range(0, n, 96):
             act(R("pat", PAO[l] + a, PAO[l] + a + 96), z, F.Copy, off=sub(fw, a // 16, a // 16 + 6))
 
     def down(l):
-        n = NS[l]
-        h = n // 2
+        h = (192, 96, 96)[l]
         m = max(h, 128)
+        name, piv, new = (("s0", 192, 384), ("s1", 96, 192), ("s1", 544, 992))[l]
         for b in range(4):
-            mm(4 + b, ET(b), S(l, h, h + m), True, False)
-        pick(R("pc", CO[l], CO[l] + h), S(l, 0, 448 if l == 2 else 768), L["c", l])
+            mm(4 + b, ET(b), R(name, piv, piv + m), True, False)
+        pick(R("pc", CO[l], CO[l] + h), R(name, 0, (768, 1120, 992)[l]), L["c", l])
         for b in range(4):
             mm(4 + b, ET(b), R("pc", CO[l], CO[l] + m), False, True)
         casts(h, 0.5)
-        quant(S(l, AV[l], AV[l] + m), R("ht", 128, 128 + 4 * m))
+        quant(R(name, new, new + m), R("ht", 128, 128 + 4 * m))
 
     first()
     up(0)
-    candidates(0)
-    members(1)
+    candidates()
     v0 = children(0)
     up(1)
     v1 = children(1)
-    z1, at1 = take("off", 12), take("off", 12)
-    wrap(L["z", 1], z1)
-    wrap(inverse(z1, 192, True), at1)
-    candidates(1)
-    members(2)
-    up(2)
-    inv, mine, own = inverse(L["l", 2], UW[2]), tf(96), take("off", 6)
-    tt(mine, sub(inv, 32, 128), sub(inv, 224, 320), A.add)
-    wrap(mine, own)
-    kid = through(mine, L["c", 1])
-    v2 = children(2)
-    L["c", 1] = through(v2, kid, float(SO[2]))
-    act(sub(v1, 0, 96), v2, F.Identity, bias=float(SO[2]), off=own)
+    z1, at1, inv = take("off", 12), take("off", 12), tf(192)
+    wrap(L["z"], z1)
+    for a in (0, 96):
+        scatter(inv, sub(z1, a // 16, a // 16 + 6), R("iot", a, a + 96))
+    wrap(inv, at1)
+    act(sub(v1, 0, 96), R("iot", 0, 768), F.Identity, bias=352.0, off=last_level())
+    L["c", 1] = through(sub(v1, 0, 96), L["c", 1])
     down(2)
     down(1)
-    pick(R("dn1", 0, 96), S(1, 0, 768), through(v1, sub(at1, 6, 12)))
-    exchange([(R("dn1", 0, 96), R("s0", BE[0], BE[0] + 96), PART[0])], "ar2")
-    pick(R("s0", BE[0] + 96, BE[0] + 192), S(1, 0, 768), through(v1, sub(at1, 0, 6)))
+    pick(R("dn1", 0, 96), R("s1", 0, 1120), through(v1, sub(at1, 6, 12)))
+    exchange([(R("dn1", 0, 96), R("s0", BE, BE + 96), PART[0])], "ar2")
+    pick(R("s0", BE + 96, BE + 192), R("s1", 0, 1120), through(v1, sub(at1, 0, 6)))
     fl0, fw = tf(P), take("off", 24)
     for a in range(0, P, 96):
         scatter(fl0, sub(L["l", 0], a // 16, a // 16 + 6), sub(v0, a, a + 96))
@@ -823,12 +892,11 @@ def rank_program(g, core, T, topo):
         wrap(sub(fl0, a, a + 192), sub(fw, a // 16, a // 16 + 12))
     parents(0, fw)
     parents(1, at1)
-    parents(2, through(inv, L["m", 2]))
     dma("g", T.pa[0:1, :], T.pat[0:1, :], [R("pat", 0, 672, p1=1)], [], "st3")
     down(0)
     for i, (a, b) in enumerate(((0, 256), (256, P))):
         fin = R("fin", a, b)
-        pick(fin, S(0, 0, 768), sub(fw, a // 16, b // 16))
+        pick(fin, R("s0", 0, 768), sub(fw, a // 16, b // 16))
         dma("g", T.oc[:, 4 * a:4 * b], T.fin[:, a:b].bitcast(dt.uint8), [fin], [], "st3")
         mm(i, R("wq", 0, 128), fin)
         copy("av"[i], R("yt", a, b), bank(i, 0, b - a))

@@ -1,5 +1,5 @@
 from concourse.bass import DstId, RemoteDMATransfer
-from concourse.mybir import dt, AluOpType, AxisListType, ActivationFunctionType
+from concourse.mybir import dt, AluOpType, ActivationFunctionType
 
 A = AluOpType
 F = ActivationFunctionType
@@ -8,7 +8,7 @@ PART = [2, 1]
 NS = [384, 192]
 AV = [384, 192]
 BE = 576
-PPO = [672, 576, 384]
+PPO = [672, 576]
 CO = [0, 192, 288]
 PAO = [0, 384, 576]
 WO = [0, 16, 34, 50]
@@ -16,27 +16,42 @@ U = 2.0 ** 28
 X4, U8, F32, BF, U16, I32 = "float8_e4m3fn_x4", "uint8", "float32", "bfloat16", "uint16", "int32"
 
 SCRATCH = {"ps": ("psum", [128, 4096], F32)}
-for _n, _w in (("f", 512), ("s0", 768), ("s1", 1120), ("pc", 864), ("wm", 384), ("tq", 208), ("nw0", 512), ("nwb", 128), ("cq", 1536),
+for _n, _w in (("f", 512), ("s0", 768), ("s1", 1120), ("pc", 864), ("wm", 640), ("tq", 208), ("nw0", 512), ("nwb", 128), ("cq", 1536),
                ("lq", 1280), ("sq", 1672), ("uq", 128), ("uv", 32), ("ur", 512), ("wq", 128), ("fin", 384), ("dn1", 96),
                ("ca", 416), ("cb", 416), ("wv", 180)):
     SCRATCH[_n] = ("sbuf", [128, _w], X4)
     SCRATCH[_n + "s"] = ("sbuf", [128, _w], U8)
 for _n, _w, _d in (("xt", 1536, BF), ("ut", 512, BF), ("wt", 512, BF), ("on", 512, BF), ("idn", 128, BF), ("cw", 512, BF),
-                   ("cx", 512, BF), ("tr", 832, BF), ("wkd", 160, BF), ("mt", 288, BF), ("tm", 96, BF), ("mz", 96, BF), ("cm", 132, BF),
+                   ("cx", 512, BF), ("tr", 832, BF), ("wkd", 160, BF), ("wke", 160, BF), ("mt", 288, BF), ("tm", 96, BF),
+                   ("mz", 96, BF), ("cm", 132, BF),
                    ("et", 520, BF), ("eh", 520, BF), ("xp", 528, BF), ("xo", 512, BF), ("xl", 1536, BF), ("xm", 768, BF),
                    ("xk", 512, BF), ("xc", 512, BF), ("xs", 768, BF), ("xa", 1664, BF), ("xb", 1664, BF), ("xv", 1024, BF),
-                   ("c2", 512, BF), ("xw", 720, BF), ("ht", 1024, BF), ("r16", 128, BF), ("qrow", 384, BF), ("iot", 768, F32),
-                   ("pi", 2, I32), ("cc", 120, F32), ("zr", 256, BF), ("c4", 512, BF), ("wk0", 192, BF), ("wk", 192, BF),
-                   ("xg", 512, BF), ("off", 384, U16), ("col", 384, F32), ("tf", 20480, F32), ("tb", 16384, BF), ("pat", 672, F32),
+                   ("c2", 512, BF), ("xw", 720, BF), ("ht", 1024, BF), ("r16", 128, BF), ("qrow", 400, BF), ("iot", 768, F32),
+                   ("pi", 2, I32), ("cc", 128, F32), ("zr", 256, BF), ("c4", 512, BF), ("tau", 130, BF), ("m3", 1152, BF),
+                   ("wk0", 192, BF), ("wk", 192, BF),
+                   ("xg", 512, BF), ("off", 384, U16), ("col", 384, F32), ("tf", 20480, F32), ("tb", 20480, BF), ("pat", 672, F32),
                    ("yt", 384, F32)):
     SCRATCH[_n] = ("sbuf", [128, _w], _d)
 
-SEMAPHORES = ["v", "a", "t", "g", "lx0", "lx1", "lx2", "lu", "lw", "lz", "sent", "aru", "ar0", "ar1", "ar2", "st1", "st3"]
+SEMAPHORES = ["v", "a", "t", "g", "lx0", "lx1", "lu", "lw", "lz", "sent", "aru", "ar0", "ar1", "ar2", "st1"]
 
-PM, FX, JA, JB, Q96, OH, OHM, QW, V16, NM, OHN, MK, OHQ, OHL = 0, 1, 2, 5, 8, 10, 16, 22, 44, 57, 58, 64, 34, 112
+PM, FX, JA, JB, Q96, OH, OHM, QW, V16, NM, OHN, MK, OHQ, OHL, OHF = 0, 1, 2, 5, 8, 10, 16, 22, 44, 57, 58, 64, 34, 112, 120
 CYC, HOP, FAR = 0.00095, 0.23, 0.9
 CASES = ((1.0, 0.23, 1.0), (0.87, 0.26, 0.85), (1.1, 0.21, 1.0), (1.3, 0.23, 1.5))
-PLANS, TRIES, MOVES = {}, 800, 14000
+PLANS, MOVES = {}, 6000
+START = (
+    "0002062i070b0g090c0a0q2o2j2k2v08352e010405102a116b6g3s2b2c2d29123x1w3w1315030e3t145a3z4o4r4u0f2w2p4a2l2h4p4s4v4q4t2f4w2z2g30595157"
+    "55534z4x0m1k4b4c0d1h0p1m1g191j1d0o1a0n1l1n1c160h402r2sbo283r2q2t1x50522m32544y56585k5c5f5b5j5g2n5d5h5l315e5i5m2x2u33343v3p5n0i0rcc"
+    "3m211y5o5p0j3yff5u5v5t5r5q5s3uar3k4d1o2yaw410y0u0s0t0x0z0v600w615w393b4f4h385x48625y63375z643l65676668424e6a6c696f6h44360k0l473q3n"
+    "6e6d6j6i6n6p3a6k6l6o6q204l1r4g6r466m6s3e6t454i6u496v433o4mf16waq1z3f6y6z6x70axas733d72741p71hf4nayat75b0az79avau274k7a7b7s7r7t7f7v"
+    "7ub776771826257c7g3g7h7z80b17wb2787k177x817i7d7lb37j7m7n7q7e7p7ob57y8e898r848f8a82868g8b8q8s8u8t878y8v8c8k8h8m8o838p8l8z8n8w858j9f"
+    "9c8i889h8d969e9d9g908x999b989a91949395929i9k979q9r9s9pj19ta54j9ladaeacabbaj31qb61t9j9m9n9o9ub99vb4b8af9wbbcm3cj4j5ci9ya1a2a0a69za4"
+    "9xa3aiajala7aka8ag1i3h3i3jama9ahaa23jdanblaocsapbmj2j6bnbcbpbsbtbubvbebdctbrbqbxbw22bycubzc0c1cvj7c2cbcdc3c6cac4c5c8jcc7cecfcgcjc9"
+    "1b1v24cyd2cwchbfdfdgbgczd01ud3dhbjdid4clckdjdkd5cndl1e1fd1d8d9dcddded6dadbcxjed7dve7e8dodwdygsfaeweae9dxepeoebe4ece6e2coe0e3e5e1dz"
+    "dpdmedemeeegendtjfgr1sdqdndsdrefejeqesfzeritekehexeifbezetf5fdeueveleyfcfofjgkfkf6frbkduf7flf0fef2fgf9fmcqf8bhfnf3f4fhfig0fxcpfqgc"
+    "geftgdgffpfsfufyggiugzgygxfvghfwh0gogjgig1h1gmgqgnh2gpbig2glg3g6h3gth4g5g4h7h6g7h5g9gugvh8gwcrgag8jhgbh9hihphnhmhohahqhrhjhkhvhuhs"
+    "hthyhwiohlhbhdi3hzhxi2i4i1i0ighcihi5i6i9i7iai8iviiidibieichehgiwifikhhjmjnjojlijiliziximinj0jbjaipiyj8iqirisjjjpjqjkjij9jrjujvjyjt"
+    "jsjxjwjzk5k0k2k3k4k8k1k7k9kakbjgk6kekfkgkdkckh")
 
 
 def R(name, c0, c1, step=1, p0=0, p1=128):
@@ -63,6 +78,7 @@ def meet(a, b, banks):
 
 def arrange(ops):
     seen = {}
+    laid = {i for i, o in enumerate(ops) if o["sem"] == "lz"}
     for i, o in enumerate(ops):
         pre = set(o["after"])
         for a, wr in [(r, False) for r in o["r"]] + [(r, True) for r in o["w"]]:
@@ -72,48 +88,12 @@ def arrange(ops):
                     pre.add(j)
         for a, wr in [(r, False) for r in o["r"]] + [(r, True) for r in o["w"]]:
             seen.setdefault(a[0], []).append((i, a, wr))
-        o["pre"] = pre
-    top = 0.0
-    for turn in range(2):
-        rank = [top - o["by"] if o["by"] else 0.0 for o in ops]
-        for i in range(len(ops) - 1, -1, -1):
-            rank[i] += ops[i]["c"] + ops[i]["lat"]
-            for j in ops[i]["pre"]:
-                rank[j] = max(rank[j], rank[i] + HOP)
-        top = max(rank)
+        o["pre"] = pre | laid if pre & laid else pre
     n = len(ops)
     post = [[] for o in ops]
     for i, o in enumerate(ops):
         for j in o["pre"]:
             post[j].append(i)
-    gap = [[(j, 0.001 if o["q"] == "t" == ops[j]["q"] else ops[j]["lat"] + HOP) for j in o["pre"]] for o in ops]
-
-    def plan(bonus):
-        left = [len(o["pre"]) for o in ops]
-        ready = [i for i in range(n) if not left[i]]
-        busy, start, end = {}, [0.0] * n, [0.0] * n
-        while ready:
-            i = max(ready, key=lambda k: rank[k] + bonus[k])
-            ready.remove(i)
-            o = ops[i]
-            t = max([end[j] + d for j, d in gap[i]] + [0.0])
-            slots = busy.setdefault(o["q"], [])
-            at = len(slots)
-            for k, (s, e) in enumerate(slots):
-                if e <= t:
-                    continue
-                if t + o["c"] <= s:
-                    at = k
-                    break
-                t = e
-            start[i], end[i] = t, t + o["c"]
-            if o["q"]:
-                slots.insert(at, (t, end[i]))
-            for j in post[i]:
-                left[j] -= 1
-                if not left[j]:
-                    ready.append(j)
-        return sorted(range(n), key=lambda k: (start[k], k))
 
     def span(order):
         tot, held = 0.0, []
@@ -129,7 +109,7 @@ def arrange(ops):
                 end[i] = t + ops[i]["c"] * slow
                 if q:
                     free[q], last[q] = end[i], i
-            i = max(order, key=lambda k: end[k] + ops[k]["lat"])
+            i = max(tail, key=lambda k: end[k] + ops[k]["lat"])
             tot += end[i] + ops[i]["lat"]
             while why[i] is not None:
                 j = why[i]
@@ -141,28 +121,18 @@ def arrange(ops):
 
     if n not in PLANS:
         queues = [o["q"] for o in ops]
+        tail = [i for i in range(n) if not post[i]]
         cases = [[[(j, 0.001 if o["q"] == "t" == ops[j]["q"] else ops[j]["lat"] * far + hop) for j in o["pre"]] for o in ops]
                  for slow, hop, far in CASES]
-        bonus, seed = [0.0] * n, 1
-        best = plan(bonus)
+        left, best, done = [int(START[k:k + 2], 36) for k in range(0, len(START), 2)], [], set()
+        assert sorted(left) == list(range(n))
+        while left:
+            i = next(k for k in left if ops[k]["pre"] <= done)
+            left.remove(i)
+            best.append(i)
+            done.add(i)
         least, held = span(best)
-        for turn in range(TRIES):
-            other = list(bonus)
-            for k in range(3):
-                seed = (seed * 1103515245 + 12345) % 2147483648
-                j, i = held[seed // 64 % len(held)]
-                step = (1 + seed // 65536 % 4) * (0.15 if seed // 1024 & 1 else 0.6)
-                if k == 2:
-                    other[seed // 64 % n] = (seed // 65536 % 9 - 4) * 0.5
-                elif seed // 4096 & 1:
-                    other[j] -= step
-                else:
-                    other[i] += step
-            order = plan(other)
-            t, now = span(order)
-            if t <= least:
-                bonus, best, least, held = other, order, t, now
-        now, cost = best, least
+        now, cost, seed = best, least, 1
         for turn in range(MOVES):
             seed = (seed * 1103515245 + 12345) % 2147483648
             j, i = held[seed // 64 % len(held)]
@@ -191,7 +161,7 @@ def arrange(ops):
                     continue
                 order = now[:a] + [x for x in now[a:b + 1] if x not in go] + [x for x in now[a:b + 1] if x in go] + now[b + 1:]
             t, got = span(order)
-            if t <= cost + 0.25 * (1 - turn / MOVES) * (seed // 16 % 4 == 0):
+            if t <= cost:
                 now, cost, held = order, t, got
                 if t < least:
                     best, least = order, t
@@ -216,7 +186,7 @@ def rank_program(g, core, T, topo):
 
     def op(q, fn, reads, writes, c, lat=0.0, sem=None, inc=1, after=()):
         ops.append({"q": q, "fn": fn, "r": [r for r in reads if isinstance(r, tuple)], "w": writes, "sem": sem, "inc": inc,
-                    "c": c, "lat": lat, "after": after, "by": 0.0})
+                    "c": c, "lat": lat, "after": after})
         return len(ops) - 1
 
     def sc(r):
@@ -250,10 +220,6 @@ def rank_program(g, core, T, topo):
 
     def turn(out, in_):
         op("v", lambda: g.vector.transpose(ap(out), ap(in_)), [in_], [out], cyc(width(out)))
-
-    def minus_abs_sum(out, in_):
-        op("v", lambda: g.vector.tensor_reduce(ap(out), ap(in_), AxisListType.X, A.add, negate=True, apply_absolute_value=True),
-           [in_], [out], cyc(width(in_)))
 
     def act(out, in_, func, bias=0.0, scale=1.0, acc=None, off=None):
         def fn():
@@ -294,6 +260,9 @@ def rank_program(g, core, T, topo):
     def select(out, in_, pattern, cmp, base, cm, other=0.0):
         op("g", lambda: g.affine_select(ap(out), ap(in_), pattern, cmp, other, base, cm), [in_], [out], 0.17 + 2 * CYC * width(out))
 
+    def hand_round(out, in_):
+        op("g", lambda: g.partition_broadcast(ap(out), ap(in_), out[2]), [in_], [out], 0.14 + 4 * CYC * width(out))
+
     def dma(q, out, in_, reads, writes, sem):
         op(q, lambda: queue[q].dma_start(out, in_), reads, writes, 0.06, FAR, sem=sem, inc=16)
 
@@ -315,7 +284,7 @@ def rank_program(g, core, T, topo):
                     return g.remote_dma(d, s, T.sem[sem], T.sem.sent, at[1], at[0], m)
                 return g.remote_dma_fused([RemoteDMATransfer(dst_ids=[DstId(rid=at[0], pnc=at[1])], dma_engine_mask=m, remote_sem=T.sem[sem], src=s, dst=d)
                                            for s, d, at, m in raw], local_sem=T.sem.sent)
-            calls.append(op("g", fn, [x[0] for x in sides], [], 0.2, FAR, sem="sent", inc=per * len(items)))
+            calls.append(op("g", fn, [x[0] for x in sides], [], 0.2, FAR * (1.15 - 0.3 * kind), sem="sent", inc=per * len(items)))
         op(None, None, [], [x[1] for x in items] + [sc(x[1]) for x in items], 0.0, sem=sem, inc=total, after=calls)
 
     used = {}
@@ -361,20 +330,21 @@ def rank_program(g, core, T, topo):
     def EH(b):
         return R("cq", 768 + 128 * b, 896 + 128 * b)
 
-    for k in range(3):
-        dma("yay"[k], T.xt[:, 512 * k:512 * k + 512], T.x[:, 512 * k:512 * k + 512], [], [R("xt", 512 * k, 512 * k + 512)], "lx%d" % k)
-        quant(R("f", 128 * k, 128 * k + 128), R("xt", 512 * k, 512 * k + 512))
+    for k, (a, b) in enumerate(((0, 160), (160, 384))):
+        dma("ya"[k], T.xt[:, 4 * a:4 * b], T.x[:, 4 * a:4 * b], [], [R("xt", 4 * a, 4 * b)], "lx%d" % k)
+        quant(R("f", a, b), R("xt", 4 * a, 4 * b))
     dma("y", T.ut[:], T.u[:], [], [R("ut", 0, 512)], "lu")
     dma("y", T.wt[:], T.w[:], [], [R("wt", 0, 512)], "lw")
-    memset(on(512), 1.0)
+    memset(on(160), 1.0)
+    memset(R("on", 160, 512), 1.0)
     quant(R("f", 384, 512), on(512))
-    select(R("wkd", 0, 160), on(160), [[1, 160]], A.is_ge, -2, -1)
-    select(R("wkd", 0, 160), R("wkd", 0, 160), [[1, 160]], A.not_equal, -1, -1, 2.0 ** 60)
+    select(R("wke", 0, 160), on(160), [[1, 160]], A.is_ge, -2, -1)
+    select(R("wkd", 0, 160), R("wke", 0, 160), [[1, 160]], A.not_equal, -1, -1, 2.0 ** 60)
     iota(R("pi", 0, 1), [[0, 1]], 0, 1, small=False)
     iota(R("r16", 0, 128), [[0, 8], [1, 16]], 0, 0)
     select(R("idn", 0, 128), on(128), [[-1, 128]], A.is_equal, 0, 1)
-    select(R("cw", 0, 512, 4), on(128), [[1, 128]], A.is_ge, 0, -1)
-    iota(R("qrow", 0, 384), [[1, 384]], -192, 0)
+    copy("a", R("cw", 0, 512, 4), R("wke", 2, 130))
+    iota(R("qrow", 0, 400), [[1, 400]], -192, 0)
     iota(cc(JA, 3), [[128, 3]], 1 - 192, 1)
     iota(cc(JB, 2), [[96, 2]], 1, 1)
     memset(R("et", 0, 520), 0.0)
@@ -387,7 +357,7 @@ def rank_program(g, core, T, topo):
     iota(R("iot", 0, 768), [[1, 768]], 0, 0)
     memset(R("xp", 0, 528), 0.0)
     memset(R("xm", 0, 768), 0.0)
-    for name, a, b, p in (("xa", 0, 768, 96), ("xa", 768, 1536, 96), ("xa", 1536, 1664, 0), ("xw", 0, 720, 0), ("xg", 0, 512, 96),
+    for name, a, b, p in (("xa", 0, 768, 96), ("xa", 768, 1536, 96), ("xw", 0, 512, 0), ("xg", 0, 512, 96),
                           ("xs", 0, 768, 96), ("ht", 0, 128, 0), ("ht", 896, 1024, 0), ("zr", 0, 256, 0)):
         lay(R(name, a, b, 1, p, 128), R("xm", 0, b - a, 1, p, 128))
     lay(R("mt", 0, 96), on(96))
@@ -395,24 +365,38 @@ def rank_program(g, core, T, topo):
     for name, a in (("nw0", 384), ("s1", 192)):
         lay(R(name, a, a + 128), ONES)
         lay(sc(R(name, a, a + 128)), sc(ONES))
-    for name, a, b in (("xo", 0, 512), ("xb", 0, 1664), ("xk", 0, 512), ("xc", 0, 512), ("tr", 0, 832)):
+    for name, a, b in (("xo", 0, 512), ("xb", 0, 1536), ("xk", 0, 512), ("xc", 0, 512), ("tr", 0, 832)):
         flat(name, a, b)
     flat("cx", 0, 512, 1)
     for t in (2, 3):
         fill(R("xs", t, 768, 4, p1=96), 0.0)
     for k, t in enumerate((2, 3, 3, 2)):
-        copy("a", R("xb", 384 * k + t, 384 * k + 384, 4, p1=96), R("idn", 0, 96, p1=96), scale=-64.0)
+        copy("a", R("xb", 384 * k + t, 384 * k + 384, 4, p1=96), R("idn", 0, 96, p1=96), scale=-64.0 if k < 2 else 64.0)
     for t in range(2):
         fill(R("xb", t, 1536, 4, 96, 128), 1.0)
     for t, c in enumerate((-U / 2, U / 64, 0.0, 0.0)):
-        fill(R("xv", t, 1024, 4, 96, 128), c)
-    quant(R("wm", 128, 256), R("xc", 0, 512))
+        fill(R("xv", t, 512, 4, 96, 128), c)
+    fill(R("xv", 512, 1024, p1=96), U)
+    fill(R("xv", 512, 1024, 1, 96, 128), 0.0)
+    for a in (0, 256):
+        quant(R("wm", a, a + 128), R("xc", 0, 512))
+    quant(R("wm", 384, 512), R("xv", 512, 1024))
+    quant(R("cb", 288, 416), R("xc", 0, 512))
+    quant(R("ca", 288, 416), R("xc", 0, 512))
+    quant(R("wv", 52, 180), R("xc", 0, 512))
     fill(R("xl", 3, 1536, 4), 0.0)
     fill(R("cw", 1, 512, 4), 1.0)
-    fill(cc(MK, 24), 8192.5 - P)
-    for a, b, st in ((1, 5, 1), (10, 12, 1), (13, 14, 1), (19, 23, 3)):
-        fill(R("cc", MK + a, MK + b, st), 0.5 - P)
-    act(cc(MK + 24, 24), cc(MK, 24), F.Identity, bias=1.0 - 2 * P, scale=-1.0)
+    fill(cc(MK, 24), 8192.0)
+    for a, b, st in ((1, 5, 1), (10, 14, 3), (22, 23, 1)):
+        fill(R("cc", MK + a, MK + b, st), 0.0)
+    ts(R("tau", 0, 129), R("wke", 1, 130), 2.0, A.mult, -1.0, A.add)
+    for a, e, src, c in ((3, P, 2, 1.0), (0, 1, 1, -1.0), (1, P, 1, 1.0), (2, P, None, 1.0), (P + 3, 2 * P, None, -1.0), (P, P + 1, None, 1.0),
+                         (P + 1, 2 * P, 1, -1.0), (P + 2, 2 * P, 1, 1.0), (2 * P, 3 * P, 0, -1.0), (2 * P + 1, 3 * P, None, 1.0), (2 * P + 2, 3 * P, 1, -1.0)):
+        out = R("m3", a, e, 3)
+        if src is None:
+            memset(out, c)
+        else:
+            copy("v", out, R("tau", src, src + width(out)), scale=c)
     for t in range(4):
         copy("a", R("c4", t, 512, 4), R("cw", 0, 512, 4))
     quant(C4, R("c4", 0, 512))
@@ -434,6 +418,7 @@ def rank_program(g, core, T, topo):
     ts(cc(OHM, 6), cc(OH, 6), 1008.0, A.mult, -1024.0, A.add)
     copy("a", cc(OHN, 6), cc(OH, 6), scale=-16.0)
     copy("a", cc(OHL, 6), cc(OH, 6), scale=207.5)
+    act(cc(OHF, 6), cc(OH, 6), F.Identity, bias=1024.0, scale=111.5 - 1024.0)
     tt(cc(OHQ, 6), cc(OH, 6), cc(QW, 6), A.mult)
     copy("a", R("cx", 0, 512, 4), R("cw", 0, 512, 4))
     quant(CX, R("cx", 0, 512))
@@ -452,12 +437,9 @@ def rank_program(g, core, T, topo):
     copy("a", R("cm", 66, 132), R("cm", 0, 66), scale=-1.0)
     for b in range(4):
         quant(ET(b), R("et", 3 - b, 515 - b))
-        ops[-1]["by"] = 3.0
         quant(EH(b), R("eh", 3 - b, 515 - b))
-        ops[-1]["by"] = 7.0
     quant(R("uq", 0, 128), R("ut", 0, 512))
     exchange([(R("uq", 0, 2), R("uv", 16 * l, 16 * l + 2), PART[l]) for l in range(2)], "aru")
-    ops[-2]["by"] = ops[-3]["by"] = 7.0
     for l in range(2):
         pick(R("ur", 128 * l, 128 * l + 128), R("uq", 0, 128), sub(o_u, 8 * l, 8 * l + 8))
         pick(R("ur", 256 + 128 * l, 384 + 128 * l), R("uv", 0, 32), sub(o_u, 16 * l, 16 * l + 8))
@@ -485,29 +467,21 @@ def rank_program(g, core, T, topo):
 
     def half(n, row, vals):
         h, K, pb = n // 2, 3, 128
-        s, cn = take("col", K, pb), take("col", K, pb)
-        run = tf(h + K, pb)
-        a = sub(run, h - 1, h - 1 + K)
-        xp = take("xp", 64, pb)
-        sq = take("sq", 132)
-        fill(sub(xp, 35, 44, 4), -h / pb)
+        s, xp, sq = take("col", K, pb), take("xp", 32, pb), take("sq", 132)
+        fill(sub(xp, 3, 12, 4), -h / pb)
         for k in range(K):
-            sg = tb(n, pb)
+            sg, eq, run = tb(n, pb), tb(n, pb), tb(n, pb)
             act(sg, row, F.Sign, bias=vals[k], scale=-1.0, acc=one(s, k))
-            if k == K - 1:
-                eq = tb(n, pb)
-                ts(eq, row, vals[k], A.is_equal)
-                scan(sub(run, 0, h), sub(eq, 0, h), sub(eq, h, n), -float(n), A.add, A.add)
+            if k != 1:
+                ts(eq, row, vals[k], A.is_equal, -1.0, A.mult)
             else:
-                minus_abs_sum(one(a, k + 1), sg)
-            ak = one(a, (k + 1) % K)
-            ts(sub(xp, k, 32, 4), cc(MK + 8 * k, 8), one(s, k), A.add, ak, A.is_lt)
-            ts(sub(xp, 32 + k, 64, 4), cc(MK + 24 + 8 * k, 8), one(s, k), A.subtract, ak, A.is_gt)
+                ts(eq, sg, 0.0, A.is_equal, -1.0, A.mult)
+            scan(run, R("m3", n * k, n * k + n), eq, one(s, k), A.mult, A.add)
+            ts(sub(xp, k, 32, 4), cc(MK + 8 * k, 8), one(run, n - 1), A.is_le)
         quant(sq, R("xp", 0, 528))
         mm(2, ONES, sub(sq, 0, 128), True, False)
         mm(2, C4, sub(sq, 4, 132), False, True)
-        for k in range(K):
-            ts(one(cn, k), bank(2, k, k + 1, pb), bank(2, K, K + 1, pb), A.subtract, bank(2, 8 + k, 9 + k, pb), A.max)
+        cn = bank(2, 0, K)
         out = take("off", n // 16)
         for side in range(2):
             for k in range(K):
@@ -521,7 +495,7 @@ def rank_program(g, core, T, topo):
             listed("xl", h * i, h * i + h, h, i, sub(out, h * i // 16, (h * i + h) // 16))
         return out
 
-    def sizes(wins):
+    def sizes(wins, by):
         K = len(wins)
         tmp, row, d, bound = tf(32 * K, 96), tf(96 * K, 96), [], []
         for k in range(K):
@@ -532,9 +506,10 @@ def rank_program(g, core, T, topo):
             act(e, d[k], F.Identity, bias=2.0 ** -30, scale=1.25 * 2.0 ** -24)
             bound.append(tf(96, 96))
             act(bound[k], R("tm", 0, 96, p1=96), F.Identity, bias=d[k], scale=e)
-        for i in range(9):
-            q, r = i // 3, i % 3
-            copy("av"[i & 1], sub(row, 32 * K * r, 32 * K * (r + 1), 1, 32 * q, 32 * q + 32), sub(tmp, 0, 32 * K, 1, 32 * r, 32 * r + 32))
+        hand_round(sub(row, 0, 32 * K), sub(tmp, 0, 32 * K, 1, 0, 1))
+        for q in range(3):
+            for r in (1, 2):
+                copy(by[r - 1], sub(row, 32 * K * r, 32 * K * (r + 1), 1, 32 * q, 32 * q + 32), sub(tmp, 0, 32 * K, 1, 32 * r, 32 * r + 32))
         return row, [sub(row, k, 96 * K, K) for k in range(K)], d, bound
 
     def scores(wins, cols, ur):
@@ -574,7 +549,7 @@ def rank_program(g, core, T, topo):
         cols = [R("nw0", 0, 192), R("nw0", 192, 384)]
         got = []
         for s in range(2):
-            row, rows, d, bound = sizes(wins[s])
+            row, rows, d, bound = sizes(wins[s], ("aa", "av")[s])
             sx = scores(wins[s], cols[s], R("ur", 256 * s, 256 * s + 128))
             got.append((row, rows, d))
             for k in range(2):
@@ -585,16 +560,20 @@ def rank_program(g, core, T, topo):
                     ts(out, R("cm", 66, 132, p1=96), sx[k], A.is_le)
                 tt(cell(2 * s + k, 2 * s + k), rows[k], bound[k], A.is_le)
             ts(cell(2 * s, 2 * s + 1), rows[1], d[0], A.is_le)
-            ts(cell(2 * s + 1, 2 * s), rows[0], d[1], A.is_lt)
+            sg = tb(96, 96)
+            act(sg, rows[0], F.Sign, bias=d[1], scale=-1.0)
+            act(cell(2 * s + 1, 2 * s), sg, F.Relu)
+        for j in range(2):
+            for k in range(2):
+                ts(cell(j, 2 + k), got[1][1][k], got[0][2][j], A.is_le)
         for j in range(2):
             sg = tb(192, 96)
             act(sg, got[0][0], F.Sign, bias=got[1][2][j], scale=-1.0)
             for k in range(2):
                 act(cell(2 + j, k), sub(sg, k, 192, 2), F.Relu)
-                ts(cell(k, 2 + j), got[1][1][j], got[0][2][k], A.is_le)
         quant(R("ca", 0, 192), R("xa", 0, 768))
-        quant(R("ca", 192, 416), R("xa", 768, 1664))
-        quant(R("wv", 0, 178), R("xw", 0, 712))
+        quant(R("ca", 192, 384), R("xa", 768, 1536))
+        quant(R("wv", 0, 128), R("xw", 0, 512))
         for k in range(4):
             mm(2, R("ca", 96 * k, 96 * k + 128), R("wv", WO[k], WO[k] + 128), k == 0, k == 3)
         xp, thr, sq = take("xp", 32, 96), take("col", 16, 96), take("sq", 128)
@@ -661,16 +640,15 @@ def rank_program(g, core, T, topo):
             copy("va"[b & 1], R("ht", 128 + b, 128 + 4 * h, 4), bank(4 + b, 0, h), scale=scale)
 
     def first():
-        row, vals = tf(P), []
+        row, tmp, vals = tf(P), tf(96), []
         for k in range(3):
             last = own_products(k, R("f", 128 * k, 128 * k + 128), 160, 128)
             vals.append(one(last, 159))
-            turn(sub(row, 32 * k, 32 * k + 32), sub(last, 128, 160))
-        w = 96
-        for q in range(4):
-            copy("va"[q & 1], sub(row, w, 2 * w, 1, 32 * q, 32 * q + 32), sub(row, 0, w, 1, 32 * (q ^ 1), 32 * (q ^ 1) + 32))
-        for q in range(2):
-            copy("va"[q], sub(row, 2 * w, 4 * w, 1, 64 * q, 64 * q + 64), sub(row, 0, 2 * w, 1, 64 - 64 * q, 128 - 64 * q))
+            turn(sub(tmp, k, 96, 3), sub(last, 128, 160))
+        hand_round(sub(row, 0, 96), sub(tmp, 0, 96, 1, 0, 1))
+        for i in range(12):
+            q, r = i // 3, 1 + i % 3
+            copy("av"[i & 1], sub(row, 96 * r, 96 * r + 96, 1, 32 * q, 32 * q + 32), sub(tmp, 0, 96, 1, 32 * r, 32 * r + 32))
         L["l", 0] = half(P, row, vals)
 
     def up(l):
@@ -679,8 +657,8 @@ def rank_program(g, core, T, topo):
         m = max(h, 128)
         lw, win = L["l", l], R(("f", "nw0")[l], 0, P)
         if l == 0:
-            pick(R(s, 0, h), win, sub(lw, 0, h // 16))
-            pick(R(s, h, n), win, sub(lw, h // 16, n // 16))
+            for a, b in ((h, n), (0, 128), (128, h)):
+                pick(R(s, a, b), win, sub(lw, a // 16, b // 16))
         else:
             pick(R(s, 0, n), win, lw)
         K, pb = h // 96, 96
@@ -711,29 +689,28 @@ def rank_program(g, core, T, topo):
         def at(t, j):
             return R("xb", 384 * j + t, 384 * j + 384, 4, p1=96)
         for s in range(2):
-            row, unused, d, bound = sizes([wins[s]])
+            row, unused, d, bound = sizes([wins[s]], ("aa", "av")[s])
             y = scores([wins[s]], wins[s], R("ur", 256 * s + 128, 256 * s + 256))
             rows.append(row)
             ds.append(d[0])
             tt(at(s, s), row, bound[0], A.is_le)
-            copy("a", at(s, 3 - s), at(s, s))
+            copy("a", at(s, 3 - s), at(s, s), scale=-1.0)
             c = take("col", 6, 96)
-            for f in range(2):
-                ts(R("xv", 512 * f + s, 512 * f + 512, 2, p1=96), R("zr", 0, 256, p1=96), y, A.is_gt if f != s else A.is_le, -U, A.mult)
-                w = R("xv", 512 * f + s, 512 * f + s + 1, p1=96)
-                copy("a", one(c, f), w, scale=-2.0 ** -42 / U)
-                copy("a", one(c, 3 - f), w, scale=1e29 / U)
-            copy("a", one(c, 4), w, scale=-96.0 / U)
+            ts(R("xv", s, 512, 2, p1=96), R("zr", 0, 256, p1=96), y, A.is_gt if s else A.is_le, -U, A.mult)
+            w = R("xv", s, s + 1, p1=96)
+            for k, (ca, cb) in enumerate(((2.0 ** -42, 0), (0, 2.0 ** -42), (0, -2.0 ** 96), (-2.0 ** 96, 0), (0, 96.0), (0, -192.0))[:6 - s]):
+                act(one(c, k), w, F.Identity, bias=float(cb), scale=(cb - ca) / U)
             fl.append(c)
         ts(at(0, 1), rows[1], ds[0], A.is_le)
-        ts(at(0, 2), rows[1], ds[0], A.is_lt)
+        ts(at(0, 2), rows[1], ds[0], A.is_lt, -1.0, A.mult)
         ts(at(1, 0), rows[0], ds[1], A.is_lt)
-        ts(at(1, 3), rows[0], ds[1], A.is_le)
+        ts(at(1, 3), rows[0], ds[1], A.is_le, -1.0, A.mult)
         quant(R("cb", 0, 192), R("xb", 0, 768))
-        quant(R("cb", 192, 416), R("xb", 768, 1664))
-        for f in range(2):
-            quant(R("wm", 256 * f, 256 * f + 128), R("xv", 512 * f, 512 * f + 512))
-            mm((2, 7)[f], R("wm", 256 * f, 256 * f + 128), R("cb", 192 * f, 192 * f + 192))
+        quant(R("cb", 192, 384), R("xb", 768, 1536))
+        quant(R("wm", 128, 256), R("xv", 0, 512))
+        mm(2, R("wm", 128, 256), R("cb", 0, 192))
+        mm(7, R("wm", 384, 512), R("cb", 192, 384), True, False)
+        mm(7, R("wm", 128, 256), R("cb", 192, 384), False, True)
         par, hi = take("col", 2, 96), take("col", 2, 96)
         for s in range(2):
             mm(s, wins[s], R("s1", 352, 640))
@@ -745,8 +722,9 @@ def rank_program(g, core, T, topo):
             fill(sub(rm, 0, 16), -1e29)
             scan(sub(rm, 16, 208), ms[0], ms[1], -1e29, A.max, A.max)
             count(rm, F.Sign, one(rm, 207), -1.0, one(par, s), one(hi, s))
-            mm(4 + s, R("cb", 96 * s, 96 * s + 128), R("wm", 126, 254), True, False)
-            mm(4 + s, R("cb", 288 - 96 * s, 416 - 96 * s), R("wm", 130, 258), False, True)
+            mm(4 + s, R("cb", 96 * s, 96 * s + 128), R("wm", 254, 382), True, False)
+            mm(4 + s, R("cb", 288 - 96 * s, 416 - 96 * s), R("wm", 258, 386), False, False)
+            mm(4 + s, R("cb", 288 - 96 * s, 416 - 96 * s), R("wm", 2, 130), False, True)
             k = take("col", 2, 96)
             for f in range(2):
                 ts(one(k, f), bank(4 + s, 126 * f, 126 * f + 1, 96), 0.0, A.max, one(fl[s], 2 + f), A.subtract)
@@ -769,15 +747,15 @@ def rank_program(g, core, T, topo):
             mm(4 + b, EH(b), R("pc", 384, 576), False, True)
         casts(192, None)
         quant(R("s1", 672, 864), R("ht", 128, 896))
-        quant(R("s1", 864, 992), R("ht", 128, 640))
         for t, (s, f) in enumerate(((0, 0), (1, 0), (1, 1), (0, 1))):
-            ts(R("xc", t, 384, 4, p1=96), R("iot", 16 + 96 * f, 112 + 96 * f, p1=96), one(par, s), A.subtract, one(ks[s], f), A.is_equal)
+            ts(R("xc", t, 384, 4, p1=96), R("qrow", 208 + 96 * f, 304 + 96 * f, p1=96), one(par, s), A.subtract, one(ks[s], f), A.is_equal)
         sq, cnt, hi, kind = take("sq", 128), take("col", 1, 96), take("col", 1, 96), take("col", 2, 96)
         quant(sq, R("xc", 0, 512))
         mm(0, sq, TR)
         count(bank(0, 0, 208, 96), F.Relu, 1.0, -1.0, cnt, hi)
         xo, sq = take("xo", 48, 96), take("sq", 128)
         digits(sub(xo, 0, 24), cnt, hi, one(fl[0], 4))
+        ts(sub(xo, 0, 24, 4), cc(OHF, 6, 96), cnt, A.is_lt, one(fl[0], 5), A.mult)
         ts(one(kind, 0), one(ks[0], 0), one(ks[0], 1), A.min, 0.0, A.is_equal)
         ts(sub(xo, 25, 48, 4), cc(OH, 6, 96), one(kind, 0), A.mult, 320.0, A.mult)
         ts(sub(xo, 24, 48, 4), cc(OHL, 6, 96), cnt, A.is_gt, 640.0, A.mult)
@@ -787,7 +765,7 @@ def rank_program(g, core, T, topo):
         mm(1, C2, sq)
         c0, ends = xo[3] // 4, take("off", 6)
         L["c", 2] = take("off", 6)
-        ts(L["c", 2], bank(1, c0, c0 + 6), 656.0, A.add)
+        ts(L["c", 2], bank(1, c0, c0 + 6), 656.0, A.add, 863.0, A.min)
         copy("v", ends, bank(1, c0 + 6, c0 + 12))
         xp, sq, pa, z = take("xp", 8, 96), take("sq", 128), take("col", 4, 96), tf(832)
         for e, s in ((0, 0), (4, 1), (5, 0)):
@@ -801,7 +779,7 @@ def rank_program(g, core, T, topo):
             ts(R("xk", 2 + s, 384, 4, p1=96), R("qrow", 193, 289, p1=96), one(pa, 2 + s), A.is_equal, 288.0, A.mult)
         by = take("off", 6)
         listed("xk", 0, 96, 128, 3, by)
-        mm(3, R("wm", 0, 128), TR)
+        mm(3, R("wm", 128, 256), TR)
         act(sub(z, 352, 544), bank(3, 16, 208), F.Identity, bias=-1.0, scale=-0.5 / U)
         fill(sub(z, 544, 640), 0.0)
         act(sub(z, 640, 832), sub(z, 0, 640), F.Copy, off=pw)
@@ -892,18 +870,26 @@ def rank_program(g, core, T, topo):
         wrap(sub(fl0, a, a + 192), sub(fw, a // 16, a // 16 + 12))
     parents(0, fw)
     parents(1, at1)
-    dma("g", T.pa[0:1, :], T.pat[0:1, :], [R("pat", 0, 672, p1=1)], [], "st3")
+    dma("y", T.pa[0:1, :], T.pat[0:1, :], [R("pat", 0, 672, p1=1)], [], "st1")
+    yw = tf(768)
+    for i, a in enumerate((192, BE)):
+        mm(i, R("wq", 0, 128), R("s0", a, a + 192))
+        copy("a", sub(yw, a, a + 192), bank(i, 0, 192))
     down(0)
-    for i, (a, b) in enumerate(((0, 256), (256, P))):
+    for i, a in enumerate((384, 448)):
+        mm(i, R("wq", 0, 128), R("s0", a, a + 128))
+        copy("va"[i], sub(yw, 384 + 96 * i, 480 + 96 * i), bank(i, 32 * i, 32 * i + 96))
+    for a, b in ((0, 256), (256, P)):
         fin = R("fin", a, b)
         pick(fin, R("s0", 0, 768), sub(fw, a // 16, b // 16))
-        dma("g", T.oc[:, 4 * a:4 * b], T.fin[:, a:b].bitcast(dt.uint8), [fin], [], "st3")
-        mm(i, R("wq", 0, 128), fin)
-        copy("av"[i], R("yt", a, b), bank(i, 0, b - a))
-        dma("y", T.y[:, a:b], T.yt[:, a:b], [R("yt", a, b)], [], "st1")
+        dma("y", T.oc[:, 4 * a:4 * b], T.fin[:, a:b].bitcast(dt.uint8), [fin], [], "st1")
+    act(R("yt", 0, 192), yw, F.Copy, off=sub(fw, 0, 12))
+    op("v", lambda: g.vector.tensor_copy(T.yt[:, 192:P], ap(yw).indirect(ap(sub(fw, 12, 24)))), [yw, fw], [R("yt", 192, P)], 0.05 + 1.5 * CYC * 192)
+    for a in (0, 192):
+        dma("y", T.y[:, a:a + 192], T.yt[:, a:a + 192], [R("yt", a, a + 192)], [], "st1")
     fin = R("fin", 0, P)
     for k in range(4):
-        dma("ayag"[k], T.osc[4 * k:4 * k + 4, :], T.fins[32 * k:32 * k + 4, 0:P], [sc(fin)], [], "st3" if k == 3 else "st1")
+        dma("yaya"[k], T.osc[4 * k:4 * k + 4, :], T.fins[32 * k:32 * k + 4, 0:P], [sc(fin)], [], "st1")
 
     order = arrange(ops)
     place = {j: i for i, j in enumerate(order)}
@@ -951,5 +937,5 @@ def rank_program(g, core, T, topo):
             count_of[q] += 1
             o["n"] = count_of[q]
             ins.then_inc(T.sem[q], 1)
-    for s in ("sent", "st1", "st3"):
+    for s in ("sent", "st1"):
         g.wait_ge(T.sem[s], total[s])

@@ -6,52 +6,39 @@ F = ActivationFunctionType
 P = 384
 PART = [2, 1]
 NS = [384, 192]
-AV = [384, 192]
-BE = 576
+AV = [608, 192]
+BE = 384
 PPO = [672, 576]
-CO = [0, 192, 288]
 PAO = [0, 384, 576]
-WO = [0, 16, 34, 50]
 U = 2.0 ** 28
 X4, U8, F32, BF, U16, I32 = "float8_e4m3fn_x4", "uint8", "float32", "bfloat16", "uint16", "int32"
 
 SCRATCH = {"ps": ("psum", [128, 4096], F32)}
-for _n, _w in (("f", 512), ("s0", 768), ("s1", 1120), ("pc", 864), ("wm", 640), ("tq", 208), ("nw0", 512), ("nwb", 128), ("cq", 1536),
-               ("lq", 1280), ("sq", 1672), ("uq", 128), ("uv", 32), ("ur", 512), ("wq", 128), ("fin", 384), ("dn1", 96),
-               ("ca", 416), ("cb", 416), ("wv", 180)):
+for _n, _w in (("f", 512), ("s0", 832), ("s1", 1120), ("pc", 896), ("pd", 224), ("wm", 640), ("tq", 208), ("nw0", 512), ("nwb", 128),
+               ("cq", 1536), ("lq", 1280), ("sq", 1928), ("uq", 128), ("uv", 32), ("ur", 512), ("wq", 128), ("fin", 384), ("dn1", 96),
+               ("ca", 416), ("cb", 416), ("wv", 144), ("wr", 144), ("wo", 128)):
     SCRATCH[_n] = ("sbuf", [128, _w], X4)
     SCRATCH[_n + "s"] = ("sbuf", [128, _w], U8)
 for _n, _w, _d in (("xt", 1536, BF), ("ut", 512, BF), ("wt", 512, BF), ("on", 512, BF), ("idn", 128, BF), ("cw", 512, BF),
                    ("cx", 512, BF), ("tr", 832, BF), ("wkd", 160, BF), ("wke", 160, BF), ("mt", 288, BF), ("tm", 96, BF),
-                   ("mz", 96, BF), ("cm", 132, BF),
-                   ("et", 520, BF), ("eh", 520, BF), ("xp", 528, BF), ("xo", 512, BF), ("xl", 1536, BF), ("xm", 768, BF),
+                   ("mz", 96, BF), ("cm", 32, BF), ("et", 520, BF), ("eh", 520, BF), ("xp", 512, BF), ("xo", 544, BF),
+                   ("xq", 512, BF), ("xi", 512, BF), ("xl", 1536, BF), ("xm", 896, BF),
                    ("xk", 512, BF), ("xc", 512, BF), ("xs", 768, BF), ("xa", 1664, BF), ("xb", 1664, BF), ("xv", 1024, BF),
-                   ("c2", 512, BF), ("xw", 720, BF), ("ht", 1024, BF), ("r16", 128, BF), ("qrow", 400, BF), ("iot", 768, F32),
-                   ("pi", 2, I32), ("cc", 128, F32), ("zr", 256, BF), ("c4", 512, BF), ("tau", 130, BF), ("m3", 1152, BF),
+                   ("c2", 512, BF), ("xw", 512, BF), ("xr", 512, BF), ("ht", 1024, BF), ("r16", 128, BF), ("qrow", 400, BF),
+                   ("iot", 768, F32), ("pi", 2, I32), ("cc", 128, F32), ("zr", 256, BF), ("tau", 130, BF), ("m3", 384, BF), ("sg", 130, BF),
                    ("wk0", 192, BF), ("wk", 192, BF),
-                   ("xg", 512, BF), ("off", 384, U16), ("col", 384, F32), ("tf", 20480, F32), ("tb", 20480, BF), ("pat", 672, F32),
+                   ("xg", 512, BF), ("off", 448, U16), ("col", 448, F32), ("tf", 20480, F32), ("tb", 20480, BF), ("pat", 672, F32),
                    ("yt", 384, F32)):
     SCRATCH[_n] = ("sbuf", [128, _w], _d)
 
-SEMAPHORES = ["v", "a", "t", "g", "lx0", "lx1", "lu", "lw", "lz", "sent", "aru", "ar0", "ar1", "ar2", "st1"]
+SEMAPHORES = ["v", "a", "t", "g", "lx0", "lx1", "lx2", "lu", "lw", "lz", "lz2", "sent", "aru", "ar0", "arf", "ar1", "ar2", "st1"]
 
-PM, FX, JA, JB, Q96, OH, OHM, QW, V16, NM, OHN, MK, OHQ, OHL, OHF = 0, 1, 2, 5, 8, 10, 16, 22, 44, 57, 58, 64, 34, 112, 120
-CYC, HOP, FAR = 0.00095, 0.23, 0.9
-CASES = ((1.0, 0.23, 1.0), (0.87, 0.26, 0.85), (1.1, 0.21, 1.0), (1.3, 0.23, 1.5))
-PLANS, MOVES = {}, 6000
+PM, FX, JA, JB, Q96, OH, OHM, V16, OHN, MK, OHQ, OHF, PH, PJ, OH8 = 0, 1, 2, 5, 8, 10, 16, 44, 58, 64, 34, 120, 100, 104, 88
+CYC, FAR = 0.00095, 0.9
 START = (
-    "0002062i070b0g090c0a0q2o2j2k2v08352e010405102a116b6g3s2b2c2d29123x1w3w1315030e3t145a3z4o4r4u0f2w2p4a2l2h4p4s4v4q4t2f4w2z2g30595157"
-    "55534z4x0m1k4b4c0d1h0p1m1g191j1d0o1a0n1l1n1c160h402r2sbo283r2q2t1x50522m32544y56585k5c5f5b5j5g2n5d5h5l315e5i5m2x2u33343v3p5n0i0rcc"
-    "3m211y5o5p0j3yff5u5v5t5r5q5s3uar3k4d1o2yaw410y0u0s0t0x0z0v600w615w393b4f4h385x48625y63375z643l65676668424e6a6c696f6h44360k0l473q3n"
-    "6e6d6j6i6n6p3a6k6l6o6q204l1r4g6r466m6s3e6t454i6u496v433o4mf16waq1z3f6y6z6x70axas733d72741p71hf4nayat75b0az79avau274k7a7b7s7r7t7f7v"
-    "7ub776771826257c7g3g7h7z80b17wb2787k177x817i7d7lb37j7m7n7q7e7p7ob57y8e898r848f8a82868g8b8q8s8u8t878y8v8c8k8h8m8o838p8l8z8n8w858j9f"
-    "9c8i889h8d969e9d9g908x999b989a91949395929i9k979q9r9s9pj19ta54j9ladaeacabbaj31qb61t9j9m9n9o9ub99vb4b8af9wbbcm3cj4j5ci9ya1a2a0a69za4"
-    "9xa3aiajala7aka8ag1i3h3i3jama9ahaa23jdanblaocsapbmj2j6bnbcbpbsbtbubvbebdctbrbqbxbw22bycubzc0c1cvj7c2cbcdc3c6cac4c5c8jcc7cecfcgcjc9"
-    "1b1v24cyd2cwchbfdfdgbgczd01ud3dhbjdid4clckdjdkd5cndl1e1fd1d8d9dcddded6dadbcxjed7dve7e8dodwdygsfaeweae9dxepeoebe4ece6e2coe0e3e5e1dz"
-    "dpdmedemeeegendtjfgr1sdqdndsdrefejeqesfzeritekehexeifbezetf5fdeueveleyfcfofjgkfkf6frbkduf7flf0fef2fgf9fmcqf8bhfnf3f4fhfig0fxcpfqgc"
-    "geftgdgffpfsfufyggiugzgygxfvghfwh0gogjgig1h1gmgqgnh2gpbig2glg3g6h3gth4g5g4h7h6g7h5g9gugvh8gwcrgag8jhgbh9hihphnhmhohahqhrhjhkhvhuhs"
-    "hthyhwiohlhbhdi3hzhxi2i4i1i0ighcihi5i6i9i7iai8iviiidibieichehgiwifikhhjmjnjojlijiliziximinj0jbjaipiyj8iqirisjjjpjqjkjij9jrjujvjyjt"
-    "jsjxjwjzk5k0k2k3k4k8k1k7k9kakbjgk6kekfkgkdkckh")
+    "0002080i04090k33370b34390a2r3d130d3536382y0c3a1v3c2x2s012z300331320e1l055i1m550g1n2t1o2u1w521p3e1q0s0h1r4z1s0m561t1u063f073z502v0t53570n513j0f540o40595a0l5g5b585h101b5d5c1a0j5e5f1k160z3b171x1f6u1g1j5x3k1i60185q1c5z5s1y3i5y5j5u5l5r5n5t5k6z42615m0p5v0v5o3r140u5w15621d1e5p190q3l2c1h6349642d3n3m4l0r653u274n2e2f3v2i4a2h672n0x2o682k280y662m692j3t6a2p4b6b2g4e2l6c296m6hckdago3g6d4f4m852a863s8c6i4c8b453h6e892b4d446j8d476f87463p6k6p6q116n6o6r6s4k6l236t486g6y4g7d880w6v7c24217a708a224h6x6w8e264j7t724i718i744o738g7b3o8l7u7n7m8h754q4v8j7o4p4t76204s128fh2cf7p3wkb778k1zdy7q7w78797v7r7s4u7h2w7glg7f3q8m7z7x7l7e2q4r7y7j80253x837k7i8182844x8n8tce8p4w9c8zd39b8q4y9d9f8o8r8u90cg9ecl9j8v9g91ch928w8x9kcj9h94953y999l979a9i9893968y9o9pcq9m8sa09n9ya59wci9q9za1a6cp9r9xa2a39sa7a8av9v41a4abafaaauaeadaiahatacasaga99uamajlhb6apb7akanlfal9tb8arb9aqaoaxbabbawlkaycmbnazcrljcsb043b1b2bxb3libzb4b5byc0cnbccoc1llbdctcvcucwbecxbmbkbibgblbhbfbjbpbobtbqc4c6c7buc8c2brc5c9bvc3bslnbwd5d6d7d8ebcad9dodnecdmdldbcbeddddcccdfdecdcydgeid0dhdidjdkeedxlmdrdsczdpdzdqdvdwdtdue0efe1eje2ene5eke6e3ege4eoehelf0f1epf2e7eqerf3lpe8eyeteuf4ese9evewezexf5eaemfffuf6loftgjfgf7fvfhfigxfwgafxfnfkfmfqhtfyfofpflfrfsf8fjgcfzgbg8g9f9g1fbfafcg2fdgyg0h0geg3gfg5g4j8g6gdg7ghgkgigmgghbhjh6h1j2h7feh8gngsgtglgugzhuidgph3h9grhagvgqgwh4hrhdj6hshci5i6h5j7i7hehki4hlhfi8hmhgi9jtjuhn"
+    "hhhiifjviahoibhvhwhphqhxhyicj3hziei0jai1j4igi2j9iij5ihjbijiri3ikipimiqilisinjcjdjwiwiuiojgivd1itj0jfiyjejijhizjjixjkjqjmjrjlkijnkhjoj1kjd2lujsjxjpkkkelrlvkfkgjykulsl2klk3kmjzknk2k0kokvltkpk1kqk4krkskwmad4k5mcmbktmdl3k6kxkyl4l7k7l8kzl6l5k9l0lalbl9lxkalylzlck8m1ldlwm2m0m3m6lem4m7kcl1mhm5mgmfmemlm8mkmnmjmim9mokdmmmpmumslqmrmqmvmwmxmymtn1n3n2n4mzn0")
+FLIP = "0s1v202t2u2z30313237393d454c58595a5e5f5h6m7k7l818384878j8k96aaacadagbocqcudfdye4fkfqfrfshlikilimj4jujvkekpl8l9lilplsm1m3mxmy"
 
 
 def R(name, c0, c1, step=1, p0=0, p1=128):
@@ -76,9 +63,15 @@ def meet(a, b, banks):
     return bool(set(range(a[3], a[4], a[5])) & set(range(b[3], b[4], b[5])))
 
 
+def numbers(s):
+    return [int(s[k:k + 2], 36) for k in range(0, len(s), 2)]
+
+
 def arrange(ops):
+    for i in numbers(FLIP):
+        ops[i]["q"], ops[i]["fn"], ops[i]["c"] = ops[i]["alt"]
     seen = {}
-    laid = {i for i, o in enumerate(ops) if o["sem"] == "lz"}
+    laid = [{i for i, o in enumerate(ops) if o["sem"] == s} for s in ("lz", "lz2")]
     for i, o in enumerate(ops):
         pre = set(o["after"])
         for a, wr in [(r, False) for r in o["r"]] + [(r, True) for r in o["w"]]:
@@ -88,85 +81,16 @@ def arrange(ops):
                     pre.add(j)
         for a, wr in [(r, False) for r in o["r"]] + [(r, True) for r in o["w"]]:
             seen.setdefault(a[0], []).append((i, a, wr))
-        o["pre"] = pre | laid if pre & laid else pre
-    n = len(ops)
-    post = [[] for o in ops]
-    for i, o in enumerate(ops):
-        for j in o["pre"]:
-            post[j].append(i)
-
-    def span(order):
-        tot, held = 0.0, []
-        for (slow, hop, far), gaps in zip(CASES, cases):
-            free, last, end, why = {}, {}, [0.0] * n, [None] * n
-            for i in order:
-                q, t = queues[i], 0.0
-                for j, d in gaps[i]:
-                    if end[j] + d > t:
-                        t, why[i] = end[j] + d, j
-                if free.get(q, 0.0) > t:
-                    t, why[i] = free[q], -1 - last[q]
-                end[i] = t + ops[i]["c"] * slow
-                if q:
-                    free[q], last[q] = end[i], i
-            i = max(tail, key=lambda k: end[k] + ops[k]["lat"])
-            tot += end[i] + ops[i]["lat"]
-            while why[i] is not None:
-                j = why[i]
-                if j < 0:
-                    j = -1 - j
-                    held.append((j, i))
-                i = j
-        return tot, held
-
-    if n not in PLANS:
-        queues = [o["q"] for o in ops]
-        tail = [i for i in range(n) if not post[i]]
-        cases = [[[(j, 0.001 if o["q"] == "t" == ops[j]["q"] else ops[j]["lat"] * far + hop) for j in o["pre"]] for o in ops]
-                 for slow, hop, far in CASES]
-        left, best, done = [int(START[k:k + 2], 36) for k in range(0, len(START), 2)], [], set()
-        assert sorted(left) == list(range(n))
-        while left:
-            i = next(k for k in left if ops[k]["pre"] <= done)
-            left.remove(i)
-            best.append(i)
-            done.add(i)
-        least, held = span(best)
-        now, cost, seed = best, least, 1
-        for turn in range(MOVES):
-            seed = (seed * 1103515245 + 12345) % 2147483648
-            j, i = held[seed // 64 % len(held)]
-            a, b = now.index(j), now.index(i)
-            if seed // 4096 & 1:
-                for k in range(seed // 8192 % 3):
-                    a = max([x for x in range(max(a - 40, 0), a) if queues[now[x]] == queues[i]] + [-1])
-                    if a < 0:
-                        a = now.index(j)
-                        break
-                go = {i}
-                for x in now[b - 1:a - 1 if a else None:-1]:
-                    if go.intersection(post[x]):
-                        go.add(x)
-                if now[a] in go:
-                    continue
-                order = now[:a] + [x for x in now[a:b + 1] if x in go] + [x for x in now[a:b + 1] if x not in go] + now[b + 1:]
-            else:
-                for k in range(seed // 8192 % 4):
-                    b = min([x for x in range(b + 1, min(b + 40, n)) if queues[now[x]] == queues[i]] + [n - 1])
-                go = {j}
-                for x in now[a + 1:b + 1]:
-                    if go.intersection(ops[x]["pre"]):
-                        go.add(x)
-                if i in go:
-                    continue
-                order = now[:a] + [x for x in now[a:b + 1] if x not in go] + [x for x in now[a:b + 1] if x in go] + now[b + 1:]
-            t, got = span(order)
-            if t <= cost:
-                now, cost, held = order, t, got
-                if t < least:
-                    best, least = order, t
-        PLANS[n] = best
-    return PLANS[n]
+        o["pre"] = pre.union(*[s for s in laid if pre & s])
+    left, order, done = numbers(START), [], set()
+    if sorted(left) != list(range(len(ops))):
+        left = list(range(len(ops)))
+    while left:
+        i = next(k for k in left if ops[k]["pre"] <= done)
+        left.remove(i)
+        order.append(i)
+        done.add(i)
+    return order
 
 
 def rank_program(g, core, T, topo):
@@ -184,9 +108,9 @@ def rank_program(g, core, T, topo):
             return T[r[0]][r[1]:r[2], r[3]:r[4]]
         return T[r[0]][r[1]:r[2], r[3]:r[4]:r[5]]
 
-    def op(q, fn, reads, writes, c, lat=0.0, sem=None, inc=1, after=()):
+    def op(q, fn, reads, writes, c, lat=0.0, sem=None, inc=1, after=(), alt=None):
         ops.append({"q": q, "fn": fn, "r": [r for r in reads if isinstance(r, tuple)], "w": writes, "sem": sem, "inc": inc,
-                    "c": c, "lat": lat, "after": after})
+                    "c": c, "lat": lat, "after": after, "alt": alt})
         return len(ops) - 1
 
     def sc(r):
@@ -198,13 +122,35 @@ def rank_program(g, core, T, topo):
     def memset(out, c):
         op("v", lambda: g.vector.memset(ap(out), c), [], [out], cyc(width(out), out))
 
+    def both(q, out, in_, bias=None, scale=None, off=None, relu=False):
+        def src():
+            return ap(in_) if off is None else ap(in_).indirect(ap(off))
+
+        def on_v():
+            steps = ([(scale, A.mult)] if scale is not None else []) + ([(bias, A.add)] if bias is not None else []) + ([(0.0, A.max)] if relu else [])
+            if not steps:
+                return g.vector.tensor_copy(ap(out), src())
+            if len(steps) == 1:
+                return g.vector.tensor_scalar(ap(out), src(), ap(steps[0][0]), None, steps[0][1])
+            return g.vector.tensor_scalar(ap(out), src(), ap(steps[0][0]), ap(steps[1][0]), steps[0][1], steps[1][1])
+
+        def on_a():
+            if relu:
+                return g.scalar.activation(ap(out), src(), F.Relu, scale=1.0 if scale is None else scale)
+            if bias is not None:
+                return g.scalar.activation(ap(out), src(), F.Identity, bias=ap(bias), scale=1.0 if scale is None else ap(scale))
+            if scale is not None:
+                return g.scalar.activation(ap(out), src(), F.Copy, scale=ap(scale))
+            return g.scalar.activation(ap(out), src(), F.Copy)
+        n = width(out)
+        ways = {"v": ("v", on_v, cyc(n, out, in_) if off is None else 0.05 + 1.5 * CYC * n), "a": ("a", on_a, cyc(n) if off is None else 0.065 + 1.5 * CYC * n)}
+        op(q, ways[q][1], [in_, bias, scale, off], [out], ways[q][2], alt=ways["va"[q == "v"]])
+
     def copy(q, out, in_, scale=None):
-        if q == "a":
-            act(out, in_, F.Copy, scale=1.0 if scale is None else scale)
-        elif scale is None:
-            op("v", lambda: g.vector.tensor_copy(ap(out), ap(in_)), [in_], [out], cyc(width(out), out, in_))
+        if size[out[0]] in (F32, BF) and size[in_[0]] in (F32, BF):
+            both(q, out, in_, scale=scale)
         else:
-            ts(out, in_, scale, A.mult)
+            op("v", lambda: g.vector.tensor_copy(ap(out), ap(in_)), [in_], [out], cyc(width(out), out, in_))
 
     def ts(out, in0, s1, op0, s2=None, op1=None):
         if op1 is None:
@@ -222,18 +168,19 @@ def rank_program(g, core, T, topo):
         op("v", lambda: g.vector.transpose(ap(out), ap(in_)), [in_], [out], cyc(width(out)))
 
     def act(out, in_, func, bias=0.0, scale=1.0, acc=None, off=None):
+        if acc is None and (func in (F.Copy, F.Identity) or func == F.Relu and bias == 0.0):
+            return both("a", out, in_, None if bias == 0.0 else bias, None if scale == 1.0 else scale, off, func == F.Relu)
+
         def fn():
-            src = ap(in_) if off is None else ap(in_).indirect(ap(off))
-            if func == F.Copy and scale == 1.0 and acc is None:
-                return g.scalar.activation(ap(out), src, func)
             if func == F.Copy:
-                return g.scalar.activation(ap(out), src, func, scale=ap(scale), accum_out=ap(acc))
-            return g.scalar.activation(ap(out), src, func, bias=ap(bias), scale=ap(scale), accum_out=ap(acc))
-        c = cyc(width(out)) if off is None else 0.065 + 1.5 * CYC * width(out)
-        op("a", fn, [in_, bias, scale, off], [out] + ([acc] if acc else []), c + (0.02 if acc else 0.0))
+                return g.scalar.activation(ap(out), ap(in_), func, scale=ap(scale), accum_out=ap(acc))
+            return g.scalar.activation(ap(out), ap(in_), func, bias=ap(bias), scale=ap(scale), accum_out=ap(acc))
+        op("a", fn, [in_, bias, scale], [out] + ([acc] if acc else []), cyc(width(out)) + (0.02 if acc else 0.0))
 
     def fill(out, c):
-        copy("a", out, R("on", 0, width(out), 1, out[1], out[2]), scale=c)
+        ones = R("on", 0, width(out), 1, out[1], out[2])
+        op("a", lambda: g.scalar.activation(ap(out), ap(ones), F.Copy, scale=c), [ones], [out], cyc(width(out)),
+           alt=("v", lambda: g.vector.memset(ap(out), c), cyc(width(out), out)))
 
     def quant(out, in_):
         op("v", lambda: g.vector.quantize_mx(ap(out), ap(sc(out)), ap(in_)), [in_], [out, sc(out)], 0.015 + 0.26 * CYC * width(in_))
@@ -263,29 +210,19 @@ def rank_program(g, core, T, topo):
     def hand_round(out, in_):
         op("g", lambda: g.partition_broadcast(ap(out), ap(in_), out[2]), [in_], [out], 0.14 + 4 * CYC * width(out))
 
-    def dma(q, out, in_, reads, writes, sem):
-        op(q, lambda: queue[q].dma_start(out, in_), reads, writes, 0.06, FAR, sem=sem, inc=16)
+    def dma(q, out, in_, reads, writes, sem, after=()):
+        return op(q, lambda: queue[q].dma_start(out, in_), reads, writes, 0.06, FAR, sem=sem, inc=16, after=after)
 
-    def exchange(items, sem):
-        calls, total = [], 0
+    def exchange(src, dst, part, sem):
+        other = T.cores[rank ^ part]
+        at, mask, per = topo.addr(other), topo.mask(core, other), len(topo.engines(core, other))
+        calls = []
         for kind in range(2):
-            sides = []
-            for i, (s, d, part) in enumerate(items):
-                other = T.cores[rank ^ part]
-                eng = topo.engines(core, other)
-                per = len(eng) // len(items)
-                total += per
-                sides.append(((s, d) if kind == 0 else (sc(s), sc(d))) + (topo.addr(other)[:2], sum(1 << e for e in eng[per * i:][:per])))
-
-            def fn(kind=kind, sides=sides):
-                raw = [(ap(s).bitcast(dt.uint8), ap(d).bitcast(dt.uint8), at, m) if kind == 0 else (ap(s), ap(d), at, m) for s, d, at, m in sides]
-                if len(raw) == 1:
-                    s, d, at, m = raw[0]
-                    return g.remote_dma(d, s, T.sem[sem], T.sem.sent, at[1], at[0], m)
-                return g.remote_dma_fused([RemoteDMATransfer(dst_ids=[DstId(rid=at[0], pnc=at[1])], dma_engine_mask=m, remote_sem=T.sem[sem], src=s, dst=d)
-                                           for s, d, at, m in raw], local_sem=T.sem.sent)
-            calls.append(op("g", fn, [x[0] for x in sides], [], 0.2, FAR * (1.15 - 0.3 * kind), sem="sent", inc=per * len(items)))
-        op(None, None, [], [x[1] for x in items] + [sc(x[1]) for x in items], 0.0, sem=sem, inc=total, after=calls)
+            def fn(kind=kind):
+                s, d = (ap(src).bitcast(dt.uint8), ap(dst).bitcast(dt.uint8)) if kind == 0 else (ap(sc(src)), ap(sc(dst)))
+                return g.remote_dma(d, s, T.sem[sem], T.sem.sent, at[1], at[0], mask)
+            calls.append(op("g", fn, [sc(src) if kind else src], [], 0.2, FAR * (1.15 - 0.3 * kind), sem="sent", inc=per))
+        op(None, None, [], [dst, sc(dst)], 0.0, sem=sem, inc=2 * per, after=calls)
 
     used = {}
 
@@ -312,17 +249,12 @@ def rank_program(g, core, T, topo):
     def on(k, pb=128):
         return R("on", 0, k, p1=pb)
 
-    def flat(name, a, b, c=0):
-        for k in range(a, b, 256):
-            iota(R(name, k, min(b, k + 256)), [[0, min(b, k + 256) - k]], c, 0)
-
-    def lay(out, in_):
+    def lay(out, in_, sem="lz2"):
         raw = size[out[0]] == X4
-        dma("y", ap(out).bitcast(dt.uint8) if raw else ap(out), ap(in_).bitcast(dt.uint8) if raw else ap(in_), [in_], [out], "lz")
-        ops[-1]["lat"] = 3 * FAR
+        dma("y", ap(out).bitcast(dt.uint8) if raw else ap(out), ap(in_).bitcast(dt.uint8) if raw else ap(in_), [in_], [out], sem,
+            loads + [u_load] * (sem == "lz2"))
 
-    CW, ONES, CX, C2, TR = R("cq", 0, 128), R("f", 384, 512), R("cq", 1280, 1408), R("cq", 1408, 1536), R("tq", 0, 208)
-    C4 = R("cq", 128, 256)
+    ONES, CX, C2, TR = R("f", 384, 512), R("cq", 1280, 1408), R("cq", 1408, 1536), R("tq", 0, 208)
 
     def ET(b):
         return R("cq", 256 + 128 * b, 384 + 128 * b)
@@ -330,11 +262,12 @@ def rank_program(g, core, T, topo):
     def EH(b):
         return R("cq", 768 + 128 * b, 896 + 128 * b)
 
-    for k, (a, b) in enumerate(((0, 160), (160, 384))):
-        dma("ya"[k], T.xt[:, 4 * a:4 * b], T.x[:, 4 * a:4 * b], [], [R("xt", 4 * a, 4 * b)], "lx%d" % k)
+    loads = []
+    for k, (a, b) in enumerate(((256, 384), (128, 256), (0, 128))):
+        loads.append(dma("yay"[k], T.xt[:, 4 * a:4 * b], T.x[:, 4 * a:4 * b], [], [R("xt", 4 * a, 4 * b)], "lx%d" % k))
         quant(R("f", a, b), R("xt", 4 * a, 4 * b))
-    dma("y", T.ut[:], T.u[:], [], [R("ut", 0, 512)], "lu")
-    dma("y", T.wt[:], T.w[:], [], [R("wt", 0, 512)], "lw")
+    u_load = dma("y", T.ut[:], T.u[:], [], [R("ut", 0, 512)], "lu", loads)
+    dma("y", T.wt[:], T.w[:], [], [R("wt", 0, 512)], "lw", loads)
     memset(on(160), 1.0)
     memset(R("on", 160, 512), 1.0)
     quant(R("f", 384, 512), on(512))
@@ -347,59 +280,61 @@ def rank_program(g, core, T, topo):
     iota(R("qrow", 0, 400), [[1, 400]], -192, 0)
     iota(cc(JA, 3), [[128, 3]], 1 - 192, 1)
     iota(cc(JB, 2), [[96, 2]], 1, 1)
-    memset(R("et", 0, 520), 0.0)
+    iota(cc(PJ, 3), [[-128, 3]], 191, -1)
+    iota(cc(PJ + 3, 3), [[128, 3]], 0, 1)
+    for a in range(0, 896, 224):
+        fill(R("xm", a, a + 224), 0.0)
+    for name, a, b in (("et", 0, 520), ("eh", 0, 520), ("xq", 0, 512), ("ht", 0, 128), ("ht", 896, 1024)):
+        for k in range(a, b, 260):
+            fill(R(name, k, min(b, k + 260)), 0.0)
     copy("a", R("et", 3, 512, 4), R("idn", 0, 128))
-    for a in (0, 260):
-        copy("a", R("eh", a, a + 260), R("et", a, a + 260), scale=-0.5)
+    copy("a", R("eh", 3, 512, 4), R("idn", 0, 128), scale=-0.5)
     iota(cc(V16, 12), [[16, 12]], 0, -1)
     iota(cc(Q96, 2), [[96, 2]], 0, 1)
-    iota(cc(QW, 12), [[16, 12]], 0, 0)
     iota(R("iot", 0, 768), [[1, 768]], 0, 0)
-    memset(R("xp", 0, 528), 0.0)
-    memset(R("xm", 0, 768), 0.0)
-    for name, a, b, p in (("xa", 0, 768, 96), ("xa", 768, 1536, 96), ("xw", 0, 512, 0), ("xg", 0, 512, 96),
-                          ("xs", 0, 768, 96), ("ht", 0, 128, 0), ("ht", 896, 1024, 0), ("zr", 0, 256, 0)):
+    memset(R("xp", 0, 512), 0.0)
+    for name, a, b, p in (("xa", 0, 768, 96), ("xa", 768, 1536, 96), ("xw", 0, 512, 0), ("xr", 0, 512, 0), ("xg", 0, 512, 96),
+                          ("xs", 0, 768, 96), ("zr", 0, 256, 0), ("xo", 0, 544, 0), ("xi", 0, 512, 0), ("xb", 0, 768, 0), ("xb", 768, 1536, 0),
+                          ("xk", 0, 512, 0), ("xc", 0, 512, 0), ("tr", 0, 832, 96), ("xv", 512, 1024, 96)):
         lay(R(name, a, b, 1, p, 128), R("xm", 0, b - a, 1, p, 128))
     lay(R("mt", 0, 96), on(96))
     lay(R("mt", 192, 288), on(96))
-    for name, a in (("nw0", 384), ("s1", 192)):
-        lay(R(name, a, a + 128), ONES)
-        lay(sc(R(name, a, a + 128)), sc(ONES))
-    for name, a, b in (("xo", 0, 512), ("xb", 0, 1536), ("xk", 0, 512), ("xc", 0, 512), ("tr", 0, 832)):
-        flat(name, a, b)
-    flat("cx", 0, 512, 1)
+    for name, a, k in (("nw0", 384, 32), ("s1", 192, 32), ("pc", 864, 32), ("pc", 352, 32), ("pd", 0, 32)):
+        lay(R(name, a, a + k), sub(ONES, 0, k), "lz")
+        lay(sc(R(name, a, a + k)), sc(sub(ONES, 0, k)), "lz")
+    for a in (0, 256):
+        fill(R("cx", a, a + 256), 1.0)
     for t in (2, 3):
-        fill(R("xs", t, 768, 4, p1=96), 0.0)
+        iota(R("xs", t, 768, 4, p1=96), [[0, 192]], 0, 0)
     for k, t in enumerate((2, 3, 3, 2)):
         copy("a", R("xb", 384 * k + t, 384 * k + 384, 4, p1=96), R("idn", 0, 96, p1=96), scale=-64.0 if k < 2 else 64.0)
     for t in range(2):
-        fill(R("xb", t, 1536, 4, 96, 128), 1.0)
+        for a in (0, 768):
+            iota(R("xb", a + t, a + 768, 4), [[0, 192]], 1 + 3 * (a > 0 == t), 0)
     for t, c in enumerate((-U / 2, U / 64, 0.0, 0.0)):
-        fill(R("xv", t, 512, 4, 96, 128), c)
-    fill(R("xv", 512, 1024, p1=96), U)
-    fill(R("xv", 512, 1024, 1, 96, 128), 0.0)
-    for a in (0, 256):
-        quant(R("wm", a, a + 128), R("xc", 0, 512))
+        select(R("xv", t, 512, 4), on(128), [[0, 128]], A.is_gt, 0, 0, c)
+    for a in (512, 768):
+        select(R("xv", a, a + 256, p1=96), on(256, 96), [[0, 256]], A.is_gt, 0, 0, U)
+    quant(R("wm", 0, 128), R("xm", 0, 512))
+    for name, a, k in (("wm", 256, 128), ("cb", 384, 32), ("ca", 384, 32), ("wv", 128, 16), ("wr", 0, 16), ("wr", 32, 112)):
+        lay(R(name, a, a + k), R("wm", 0, k))
+        lay(sc(R(name, a, a + k)), sc(R("wm", 0, k)))
     quant(R("wm", 384, 512), R("xv", 512, 1024))
-    quant(R("cb", 288, 416), R("xc", 0, 512))
-    quant(R("ca", 288, 416), R("xc", 0, 512))
-    quant(R("wv", 52, 180), R("xc", 0, 512))
     fill(R("xl", 3, 1536, 4), 0.0)
+    for e in (0, 768):
+        fill(R("xl", e + 512, e + 768, 4), 1.0)
+        fill(R("xl", e + 2, e + 256, 4), 0.0)
     fill(R("cw", 1, 512, 4), 1.0)
-    fill(cc(MK, 24), 8192.0)
-    for a, b, st in ((1, 5, 1), (10, 14, 3), (22, 23, 1)):
-        fill(R("cc", MK + a, MK + b, st), 0.0)
+    fill(cc(MK, 4), 258.0)
     ts(R("tau", 0, 129), R("wke", 1, 130), 2.0, A.mult, -1.0, A.add)
-    for a, e, src, c in ((3, P, 2, 1.0), (0, 1, 1, -1.0), (1, P, 1, 1.0), (2, P, None, 1.0), (P + 3, 2 * P, None, -1.0), (P, P + 1, None, 1.0),
-                         (P + 1, 2 * P, 1, -1.0), (P + 2, 2 * P, 1, 1.0), (2 * P, 3 * P, 0, -1.0), (2 * P + 1, 3 * P, None, 1.0), (2 * P + 2, 3 * P, 1, -1.0)):
-        out = R("m3", a, e, 3)
-        if src is None:
-            memset(out, c)
-        else:
-            copy("v", out, R("tau", src, src + width(out)), scale=c)
-    for t in range(4):
-        copy("a", R("c4", t, 512, 4), R("cw", 0, 512, 4))
-    quant(C4, R("c4", 0, 512))
+    for q in range(4):
+        copy("v", R("sg", 0, 32, 1, 32 * q, 32 * q + 32), R("tau", 32 * q, 32 * q + 32, 1, 32 * q, 32 * q + 32), scale=-1.0)
+    for a, b, p0, p1, c in ((32, 96, 0, 64, -1.0), (32, 96, 64, 128, 1.0), (96, 128, 0, 32, -1.0), (96, 128, 64, 96, -1.0),
+                            (96, 130, 32, 64, 1.0), (96, 130, 96, 128, 1.0), (128, 130, 0, 32, 1.0), (128, 130, 64, 96, 1.0)):
+        fill(R("sg", a, b, 1, p0, p1), c)
+    tt(R("m3", 1, 129), R("sg", 0, 128), R("sg", 1, 129), A.mult)
+    fill(R("m3", 0, 1), -1.0)
+    fill(R("m3", 129, P), 1.0)
     ts(R("pi", 1, 2), R("pi", 0, 1), 15, A.bitwise_and)
     copy("v", cc(PM), R("pi", 1, 2))
     ts(R("cw", 2, 512, 4), R("r16", 0, 128), cc(PM), A.is_equal)
@@ -413,13 +348,14 @@ def rank_program(g, core, T, topo):
         copy("a", R("wk", a, a + 96), R("wk0", 0, 96), scale=2048.0)
     for k, c in enumerate((0, 1, 17)):
         memset(sub(o_u, 8 * k, 8 * k + 8), c)
-    quant(CW, R("cw", 0, 512))
     ts(cc(OH, 6), cc(V16, 6), cc(PM), A.add, 0.0, A.is_equal)
     ts(cc(OHM, 6), cc(OH, 6), 1008.0, A.mult, -1024.0, A.add)
     copy("a", cc(OHN, 6), cc(OH, 6), scale=-16.0)
-    copy("a", cc(OHL, 6), cc(OH, 6), scale=207.5)
+    ts(cc(OH8, 8), cc(V16, 8), cc(PM), A.add, 0.0, A.is_equal)
     act(cc(OHF, 6), cc(OH, 6), F.Identity, bias=1024.0, scale=111.5 - 1024.0)
-    tt(cc(OHQ, 6), cc(OH, 6), cc(QW, 6), A.mult)
+    act(cc(OHQ, 6), cc(OH, 6), F.Identity, bias=1024.0, scale=207.5 - 1024.0)
+    ts(cc(PH, 2), cc(Q96, 2), cc(PM), A.subtract)
+    ts(cc(PH + 2), cc(Q96), cc(PM), A.subtract, -192.0, A.add)
     copy("a", R("cx", 0, 512, 4), R("cw", 0, 512, 4))
     quant(CX, R("cx", 0, 512))
     for t in range(2):
@@ -431,20 +367,18 @@ def rank_program(g, core, T, topo):
     act(R("mt", 96, 192), R("idn", 0, 96), F.Identity, bias=1.0, scale=-2.0)
     act(R("mz", 0, 96), R("idn", 0, 96), F.Identity, bias=1.0, scale=-1.0)
     act(R("tm", 0, 96), R("cw", 0, 384, 4), F.Identity, bias=-1.0)
-    fill(R("cm", 0, 66), -1024.0)
-    for a, b in ((0, 1), (5, 14), (20, 21), (26, 31), (32, 33), (42, 43), (49, 50), (62, 63)):
-        fill(R("cm", a, b, 4), 0.0)
-    copy("a", R("cm", 66, 132), R("cm", 0, 66), scale=-1.0)
+    for a, c in ((0, -1024.0), (16, 1024.0)):
+        fill(R("cm", a, a + 16), c)
+        fill(R("cm", a, a + 16, 5), 0.0)
     for b in range(4):
         quant(ET(b), R("et", 3 - b, 515 - b))
         quant(EH(b), R("eh", 3 - b, 515 - b))
     quant(R("uq", 0, 128), R("ut", 0, 512))
-    exchange([(R("uq", 0, 2), R("uv", 16 * l, 16 * l + 2), PART[l]) for l in range(2)], "aru")
+    exchange(R("uq", 0, 2), R("uv", 16, 18), PART[1], "aru")
     for l in range(2):
-        pick(R("ur", 128 * l, 128 * l + 128), R("uq", 0, 128), sub(o_u, 8 * l, 8 * l + 8))
-        pick(R("ur", 256 + 128 * l, 384 + 128 * l), R("uv", 0, 32), sub(o_u, 16 * l, 16 * l + 8))
+        pick(R("ur", 96 * l, 96 * l + 96), R("uq", 0, 128), sub(o_u, 8 * l, 8 * l + 6))
+    pick(R("ur", 192, 320), R("uv", 0, 32), sub(o_u, 16, 24))
     quant(R("wq", 0, 128), R("wt", 0, 512))
-    copy("a", cc(NM), cc(PM), scale=-1.0)
 
     def wrap(src, out):
         n = width(src)
@@ -467,33 +401,59 @@ def rank_program(g, core, T, topo):
 
     def half(n, row, vals):
         h, K, pb = n // 2, 3, 128
-        s, xp, sq = take("col", K, pb), take("xp", 32, pb), take("sq", 132)
+        s, xp, sq = take("col", K, pb), take("xp", 12, pb), take("sq", 128)
         fill(sub(xp, 3, 12, 4), -h / pb)
         for k in range(K):
-            sg, eq, run = tb(n, pb), tb(n, pb), tb(n, pb)
-            act(sg, row, F.Sign, bias=vals[k], scale=-1.0, acc=one(s, k))
-            if k != 1:
-                ts(eq, row, vals[k], A.is_equal, -1.0, A.mult)
-            else:
-                ts(eq, sg, 0.0, A.is_equal, -1.0, A.mult)
-            scan(run, R("m3", n * k, n * k + n), eq, one(s, k), A.mult, A.add)
-            ts(sub(xp, k, 32, 4), cc(MK + 8 * k, 8), one(run, n - 1), A.is_le)
-        quant(sq, R("xp", 0, 528))
-        mm(2, ONES, sub(sq, 0, 128), True, False)
-        mm(2, C4, sub(sq, 4, 132), False, True)
+            sg, eq, run = tb(128), tb(n), tb(n)
+            act(sg, sub(row, k, n, 3), F.Sign, bias=vals[k], scale=-1.0, acc=one(s, k))
+            ts(sub(eq, 0, 128), sg, 0.0, A.is_equal)
+            for i, j in enumerate(((1, 2), (2, 0), (0, 1))[k]):
+                out = sub(eq, 128 + 128 * i, 256 + 128 * i)
+                if j == k + 1:
+                    sg = tb(128)
+                    act(sg, sub(row, j, n, 3), F.Sign, bias=vals[k], scale=-1.0)
+                    act(out, sg, F.Relu, scale=-2.0)
+                else:
+                    ts(out, sub(row, j, n, 3), vals[k], A.is_gt if j > k else A.is_ge, 2.0, A.mult)
+            scan(run, R("m3", 0, n), eq, one(s, k), A.mult, A.add)
+            ts(sub(xp, 4 * k, 12, 5), cc(MK, 3 - k), one(run, n - 1), A.is_le)
+        quant(sq, R("xp", 0, 512))
+        lower, L["z0"], L["at0"] = take("col", 4), tf(P), take("off", 24)
+        copy("a", sub(lower, 0, 3), sub(xp, 0, 12, 4))
+        mm(2, CX, sq)
         cn = bank(2, 0, K)
         out = take("off", n // 16)
         for side in range(2):
             for k in range(K):
-                e = 4 * side * h + k
-                x = R("xl", e, e + 4 * h - k, 4, p1=pb)
+                e, a, b = 4 * side * h + k, (0, 0, 64)[k], (128, h, h)[k]
+                x = R("xl", e + 4 * a, e + 4 * b - k, 4, p1=pb)
                 if side == 0:
-                    ts(x, R("qrow", 0, h), one(cn, k), A.is_ge)
+                    ts(x, R("qrow", a, b), one(cn, k), A.is_ge)
                 else:
-                    ts(x, R("qrow", h, n), one(cn, k), A.add, cc(JA + k), A.is_ge)
+                    ts(x, R("qrow", h + a, h + b), one(cn, k), A.add, cc(JA + k), A.is_ge)
         for i in range(2):
-            listed("xl", h * i, h * i + h, h, i, sub(out, h * i // 16, (h * i + h) // 16))
+            listed("xl", h * i, h * i + h, h, 4 + i, sub(out, h * i // 16, (h * i + h) // 16))
+            copy("a", sub(L["z0"], h * i, h * i + h), bank(4 + i, 0, h))
+        at = take("col", 16)
+        copy("v", sub(at, 0, 3), cn)
+        L["at"] = at, lower
         return out
+
+    def where():
+        (at, lower), xi, sq, K = L["at"], take("xi", 96), take("sq", 128), 3
+        for k in range(K):
+            act(one(at, 3 + k), one(at, k), F.Identity, bias=cc(PJ + k), scale=2.0)
+            act(one(at, 6 + k), one(at, k), F.Identity, bias=cc(PJ + 3 + k), scale=-1.0)
+            act(one(at, 9 + k), one(at, 3 + k), F.Identity, bias=one(at, 6 + k), scale=one(lower, k))
+        ts(sub(at, 12, 15), sub(at, 9, 12), 1.5 * 2.0 ** 28, A.add, 1.5 * 2.0 ** 28, A.subtract)
+        for k in range(K):
+            copy("a", sub(xi, 32 * k, 32 * k + 32, 4), cc(OH8, 8), scale=one(at, 12 + k))
+        tt(sub(at, 0, 3), sub(at, 9, 12), sub(at, 12, 15), A.subtract)
+        for k in range(K):
+            copy("a", sub(xi, 32 * k + 1, 32 * k + 32, 4), cc(OH8, 8), scale=one(at, k))
+        quant(sq, R("xi", 0, 512))
+        mm(4, C2, sq)
+        copy("v", L["at0"], bank(4, 0, 24))
 
     def sizes(wins, by):
         K = len(wins)
@@ -506,19 +466,20 @@ def rank_program(g, core, T, topo):
             act(e, d[k], F.Identity, bias=2.0 ** -30, scale=1.25 * 2.0 ** -24)
             bound.append(tf(96, 96))
             act(bound[k], R("tm", 0, 96, p1=96), F.Identity, bias=d[k], scale=e)
-        hand_round(sub(row, 0, 32 * K), sub(tmp, 0, 32 * K, 1, 0, 1))
+        if by == "aa":
+            hand_round(sub(row, 0, 32 * K), sub(tmp, 0, 32 * K, 1, 0, 1))
         for q in range(3):
-            for r in (1, 2):
+            for r in (1, 2) if by == "aa" else (0, 1, 2):
                 copy(by[r - 1], sub(row, 32 * K * r, 32 * K * (r + 1), 1, 32 * q, 32 * q + 32), sub(tmp, 0, 32 * K, 1, 32 * r, 32 * r + 32))
         return row, [sub(row, k, 96 * K, K) for k in range(K)], d, bound
 
-    def scores(wins, cols, ur):
+    def scores(wins, cols, ur, short=False):
         K = len(wins)
         n = 96 * K
         for k in range(K):
             mm(6 + k, wins[k], ur)
         mm(5, ur, cols)
-        if K == 1:
+        if short:
             ge, eq, above, later = tb(n, 96), tb(n, 96), tb(n // 2, 96), tb(n, 96)
             ts(ge, bank(5, 0, n, 96), bank(6, 0, 1, 96), A.is_ge)
             ts(eq, bank(5, 0, n, 96), bank(6, 0, 1, 96), A.is_equal)
@@ -526,7 +487,7 @@ def rank_program(g, core, T, topo):
             scan(later, R("mz", 0, n, p1=96), eq, 0.0, A.mult, A.add)
             y = take("col", 1, 96)
             ts(y, one(above, n // 2 - 1), one(later, n - 1), A.subtract)
-            return y
+            return [y]
         sv, s, nx = take("col", K, 96), take("col", K, 96), []
         for k in range(K):
             copy("a", one(sv, k), bank(6 + k, 0, 1, 96))
@@ -539,25 +500,26 @@ def rank_program(g, core, T, topo):
         return nx
 
     def cell(t, j):
-        return R("xa", 384 * j + t, 384 * j + 384, 4, p1=96)
+        return R("xa", 384 * (j ^ 2) + t, 384 * (j ^ 2) + 384, 4, p1=96)
 
     def candidates():
         quant(R("nw0", 0, 192), R("ht", 128, 896))
-        exchange([(R("nw0", 0, 192), R("nw0", 192, 384), PART[0])], "ar0")
+        exchange(R("nw0", 0, 192), R("nw0", 192, 384), PART[0], "ar0")
         quant(R("nwb", 0, 128), R("ht", 512, 1024))
         wins = [[R("nw0", 0, 128), R("nwb", 0, 128)], [R("nw0", 192, 320), R("nw0", 288, 416)]]
-        cols = [R("nw0", 0, 192), R("nw0", 192, 384)]
         got = []
         for s in range(2):
             row, rows, d, bound = sizes(wins[s], ("aa", "av")[s])
-            sx = scores(wins[s], cols[s], R("ur", 256 * s, 256 * s + 128))
             got.append((row, rows, d))
+            if s == 0:
+                sx = scores(wins[0], R("nw0", 0, 192), R("ur", 0, 128))
+                for k in range(2):
+                    ts(R("xr", 2 + k, 64, 4, p1=96), R("cm", 0, 16, p1=96), sx[k], A.is_gt)
+                    ts(R("xw", 64 + k, 128, 4, p1=96), R("cm", 16, 32, p1=96), sx[k], A.is_le)
+                quant(R("wo", 0, 128), R("xr", 0, 512))
+                exchange(R("wo", 0, 16), R("wr", 16, 32), PART[0], "arf")
+                quant(R("wv", 0, 128), R("xw", 0, 512))
             for k in range(2):
-                out = R("xw", 2 * s + k, 264, 4, p1=96)
-                if s:
-                    ts(out, R("cm", 0, 66, p1=96), sx[k], A.is_gt)
-                else:
-                    ts(out, R("cm", 66, 132, p1=96), sx[k], A.is_le)
                 tt(cell(2 * s + k, 2 * s + k), rows[k], bound[k], A.is_le)
             ts(cell(2 * s, 2 * s + 1), rows[1], d[0], A.is_le)
             sg = tb(96, 96)
@@ -567,22 +529,20 @@ def rank_program(g, core, T, topo):
             for k in range(2):
                 ts(cell(j, 2 + k), got[1][1][k], got[0][2][j], A.is_le)
         for j in range(2):
-            sg = tb(192, 96)
-            act(sg, got[0][0], F.Sign, bias=got[1][2][j], scale=-1.0)
             for k in range(2):
-                act(cell(2 + j, k), sub(sg, k, 192, 2), F.Relu)
+                ts(cell(2 + j, k), got[0][1][k], got[1][2][j], A.is_lt)
         quant(R("ca", 0, 192), R("xa", 0, 768))
         quant(R("ca", 192, 384), R("xa", 768, 1536))
-        quant(R("wv", 0, 128), R("xw", 0, 512))
         for k in range(4):
-            mm(2, R("ca", 96 * k, 96 * k + 128), R("wv", WO[k], WO[k] + 128), k == 0, k == 3)
+            for name in ("wv", "wr"):
+                mm(2, R("ca", 96 * (k ^ 2), 96 * (k ^ 2) + 128), R(name, 16 - 4 * k, 144 - 4 * k), (k, name) == (0, "wv"), (k, name) == (3, "wr"))
+        for k in range(4):
+            mm(7, ET(k), R(("wv", "wr")[k // 2], 16 - 4 * k, 144 - 4 * k), k == 0, k == 3)
         xp, thr, sq = take("xp", 32, 96), take("col", 16, 96), take("sq", 128)
         c0 = xp[3] // 4
-        flags = R("xw", 128, 132, p1=96)
-        copy("a", sub(xp, 16, 32, 4), flags)
-        for k in range(1, 4):
-            copy("a", sub(xp, 17 + 4 * k, 17 + 5 * k), sub(flags, 0, k))
-        act(thr, sub(xp, 16, 32), F.Identity, bias=1000.0, scale=96.5 - 1000.0)
+        flags = sub(xp, 16, 32, 4)
+        act(thr, bank(7, 0, 16, 96), F.Identity, bias=1000.0, scale=96.5 - 1000.0)
+        copy("a", sub(xp, 16, 32), bank(7, 0, 16, 96))
         tt(sub(xp, 0, 16), bank(2, 0, 16, 96), thr, A.is_gt)
         quant(sq, R("xp", 0, 512))
         mm(1, CX, sq)
@@ -594,18 +554,19 @@ def rank_program(g, core, T, topo):
         copy("a", sub(pa, 4, 8), flags)
         copy("v", sub(pa, 0, 4), bank(1, c0 + 4, c0 + 8, 96))
         L["l", 1] = take("off", 12)
-        lq = listed("xm", 0, 192, 192, 0, L["l", 1])
+        lq = [listed("xm", 96 * k, 96 * k + 96, 128, 2 * k, sub(L["l", 1], 6 * k, 6 * k + 6)) for k in (1, 0)]
         for k in range(4):
             act(R("xg", k, 512, 4, p1=96), on(128, 96), F.Copy, scale=one(pa, 4 + k))
         sq = take("sq", 128)
         quant(sq, R("xg", 0, 512))
-        mm(3, sq, lq)
         L["z"] = tf(192)
-        copy("a", L["z"], bank(3, 0, 192))
+        for k in range(2):
+            mm(5 + k, sq, lq[1 - k])
+            copy("a", sub(L["z"], 96 * k, 96 * k + 96), bank(5 + k, 0, 96))
         L["s"] = take("off", 12)
         for k in range(2):
-            ts(R("xs", k, 384, 4, p1=96), q, one(pa, k), A.add, cc(JB + k, 1, 96), A.is_ge)
-            ts(R("xs", 384 + k, 768, 4, p1=96), q, one(pa, k), A.is_ge)
+            ts(R("xs", 384 + k, 768, 4, p1=96), q, one(pa, k), A.add, cc(JB + k, 1, 96), A.is_ge)
+            ts(R("xs", k, 384, 4, p1=96), q, one(pa, k), A.is_ge)
         listed("xs", 0, 192, 192, 3, L["s"])
 
     def count(src, func, bias, scale, cnt, hi):
@@ -613,42 +574,43 @@ def rank_program(g, core, T, topo):
         act(tb(n, pb), src, func, bias=bias, scale=scale, acc=cnt)
         act(tb(n // 16, pb), sub(src, 15, n, 16), func, bias=bias, scale=scale, acc=hi)
 
-    def spread(cnt, hi, K, pb, tile, b, under=None, step=0.0):
-        has = take("col", K, pb)
+    def spread(cnt, hi, K, pb, tile, b, under=None, step=0):
         G = pb // 16
-        xp = take(tile, 4 * K * G * (2 if under else 1), pb)
-        if under:
-            ts(has, cnt, under, A.is_lt, step, A.mult)
-            act(sub(xp, 4 * K * G + 1, 8 * K * G, 4, 0, 32), cc(QW, K * G, 32), F.Copy, scale=1 / 32)
+        xp = take(tile, 4 * K * G, pb)
         for k in range(K):
             e = 4 * G * k
             act(sub(xp, e + 2, e + 4 * G, 4), cc(OHM, G, pb), F.Relu, bias=one(cnt, k), scale=one(hi, k))
-            ts(sub(xp, e + 3, e + 4 * G, 4), cc(OHN, G, pb), one(hi, k), A.mult)
+            copy("v", sub(xp, e + 3, e + 4 * G, 4), cc(OHN, G, pb), scale=one(hi, k))
             if under:
-                e += 4 * K * G
-                ts(sub(xp, e + 2, e + 4 * G, 4), cc(OH, G, pb), one(has, k), A.mult)
-                act(sub(xp, e + 3, e + 4 * G, 4), cc(OH, G, pb), F.Copy, scale=cc(NM, 1, pb))
+                ts(sub(xp, e, e + 4 * G, 4), cc(under, G, pb), one(cnt, k), A.is_lt, cc(step + k, 1, pb), A.mult)
+                ts(sub(xp, e + 1, e + 4 * G, 4), cc(under, G, pb), one(cnt, k), A.is_lt, cc(PM, 1, pb), A.mult)
         sq = take("sq", 128)
         quant(sq, R(tile, 0, 512))
-        mm(b, CW, sq)
+        mm(b, C2, sq)
         return bank(b, xp[3] // 4, xp[4] // 4)
 
     L = {}
 
-    def casts(h, scale):
+    def joined(one_, other, x, y, h, scale, b0=4, at=0, c0=0):
         for b in range(4):
-            copy("va"[b & 1], R("ht", 128 + b, 128 + 4 * h, 4), bank(4 + b, 0, h), scale=scale)
+            mm(b0 + b, one_(b), x, True, False)
+        for b in range(4):
+            mm(b0 + b, other(b), y, False, True)
+        for b in range(4):
+            copy("va"[b & 1], R("ht", 128 + 4 * at + b, 128 + 4 * (at + h), 4), bank(b0 + b, c0, c0 + h), scale=scale)
 
     def first():
-        row, tmp, vals = tf(P), tf(96), []
+        row, vals = tf(P), []
         for k in range(3):
             last = own_products(k, R("f", 128 * k, 128 * k + 128), 160, 128)
             vals.append(one(last, 159))
-            turn(sub(tmp, k, 96, 3), sub(last, 128, 160))
-        hand_round(sub(row, 0, 96), sub(tmp, 0, 96, 1, 0, 1))
-        for i in range(12):
-            q, r = i // 3, 1 + i % 3
-            copy("av"[i & 1], sub(row, 96 * r, 96 * r + 96, 1, 32 * q, 32 * q + 32), sub(tmp, 0, 96, 1, 32 * r, 32 * r + 32))
+            turn(sub(row, k, 96, 3), sub(last, 128, 160))
+        for i in range(2):
+            copy("av"[i], sub(row, 96, 192, 1, 64 * i, 64 * i + 64), sub(row, 0, 96, 1, 64 - 64 * i, 128 - 64 * i))
+        for i in range(8):
+            q, r = i // 2, i % 2
+            o = q ^ (3 - 2 * r)
+            copy("av"[i & 1], sub(row, 192 + 96 * r, 288 + 96 * r, 1, 32 * q, 32 * q + 32), sub(row, 0, 96, 1, 32 * o, 32 * o + 32))
         L["l", 0] = half(P, row, vals)
 
     def up(l):
@@ -656,32 +618,27 @@ def rank_program(g, core, T, topo):
         h = n // 2
         m = max(h, 128)
         lw, win = L["l", l], R(("f", "nw0")[l], 0, P)
-        if l == 0:
-            for a, b in ((h, n), (0, 128), (128, h)):
-                pick(R(s, a, b), win, sub(lw, a // 16, b // 16))
-        else:
-            pick(R(s, 0, n), win, lw)
+        for a, b in ((h, n), (96, h), (0, 96)) if l == 0 else ((h, n), (0, h)):
+            pick(R(s, a, b), win, sub(lw, a // 16, b // 16))
         K, pb = h // 96, 96
         par, hi = take("col", K, pb), take("col", K, pb)
-        for k in range(K):
+        pw = take("off", h // 16)
+        L["p", l] = pw
+        for k in range(K)[::-1]:
             mm(k, R(s, pb * k, pb * k + 128), R(s, h, h + m))
             rm = tf(16 + h, pb)
             fill(sub(rm, 0, 16), -1e29)
             scan(sub(rm, 16, 16 + h), bank(k, 0, h, pb), on(h, pb), -1e29, A.max, A.mult)
             count(rm, F.Sign, one(rm, 15 + h), -1.0, one(par, k), one(hi, k))
-        for b in range(4):
-            mm(4 + b, ET(b), R(s, 0, m), True, False)
-        pw = take("off", h // 16)
-        L["p", l] = pw
-        ts(pw, spread(par, hi, K, pb, "xp", 2), float(h - 16), A.add)
-        pick(R("pc", PPO[l], PPO[l] + h), R(s, 0, n), pw)
-        for b in range(4):
-            mm(4 + b, EH(b), R("pc", PPO[l], PPO[l] + m), False, True)
-        casts(h, None)
+        for k in range(K)[::-1]:
+            a = PPO[l] + pb * k
+            ts(sub(pw, 6 * k, 6 * k + 6), spread(one(par, k), one(hi, k), 1, pb, ("xp", "xq")[k], 2 + k), float(h - 16), A.add)
+            pick(R("pc", a, a + pb), R(s, 0, n), sub(pw, 6 * k, 6 * k + 6))
+            joined(ET, EH, R(s, pb * k, pb * k + 128), R("pc", a, a + 128), pb, None, 4 * (k == K - 1), pb * k)
 
     def last_level():
         quant(R("s1", 320, 448), R("ht", 0, 512))
-        exchange([(R("s1", 352, 448), R("s1", 448, 544), PART[1])], "ar1")
+        exchange(R("s1", 352, 448), R("s1", 448, 544), PART[1], "ar1")
         quant(R("s1", 544, 672), R("ht", 128, 640))
         wins = [R("s1", 544, 672), R("s1", 448, 576)]
         rows, ds, fl, ks = [], [], [], []
@@ -690,11 +647,14 @@ def rank_program(g, core, T, topo):
             return R("xb", 384 * j + t, 384 * j + 384, 4, p1=96)
         for s in range(2):
             row, unused, d, bound = sizes([wins[s]], ("aa", "av")[s])
-            y = scores([wins[s]], wins[s], R("ur", 256 * s + 128, 256 * s + 256))
+            y = scores([wins[s]], wins[s], R("ur", 96 * s + 96, 96 * s + 224), s == 1)[0]
             rows.append(row)
             ds.append(d[0])
             tt(at(s, s), row, bound[0], A.is_le)
-            copy("a", at(s, 3 - s), at(s, s), scale=-1.0)
+            if s:
+                tt(at(1, 2), row, bound[0], A.is_gt)
+            else:
+                copy("a", at(0, 3), at(0, 0), scale=-1.0)
             c = take("col", 6, 96)
             ts(R("xv", s, 512, 2, p1=96), R("zr", 0, 256, p1=96), y, A.is_gt if s else A.is_le, -U, A.mult)
             w = R("xv", s, s + 1, p1=96)
@@ -703,8 +663,10 @@ def rank_program(g, core, T, topo):
             fl.append(c)
         ts(at(0, 1), rows[1], ds[0], A.is_le)
         ts(at(0, 2), rows[1], ds[0], A.is_lt, -1.0, A.mult)
-        ts(at(1, 0), rows[0], ds[1], A.is_lt)
-        ts(at(1, 3), rows[0], ds[1], A.is_le, -1.0, A.mult)
+        sg = tb(96, 96)
+        act(sg, rows[0], F.Sign, bias=ds[1], scale=-1.0)
+        act(at(1, 0), sg, F.Relu)
+        act(at(1, 3), sg, F.Relu, scale=-1.0)
         quant(R("cb", 0, 192), R("xb", 0, 768))
         quant(R("cb", 192, 384), R("xb", 768, 1536))
         quant(R("wm", 128, 256), R("xv", 0, 512))
@@ -712,7 +674,7 @@ def rank_program(g, core, T, topo):
         mm(7, R("wm", 384, 512), R("cb", 192, 384), True, False)
         mm(7, R("wm", 128, 256), R("cb", 192, 384), False, True)
         par, hi = take("col", 2, 96), take("col", 2, 96)
-        for s in range(2):
+        for s in (1, 0):
             mm(s, wins[s], R("s1", 352, 640))
             ms, rm = [tf(192, 96), tf(192, 96)], tf(208, 96)
             for f in range(2):
@@ -728,45 +690,51 @@ def rank_program(g, core, T, topo):
             k = take("col", 2, 96)
             for f in range(2):
                 ts(one(k, f), bank(4 + s, 126 * f, 126 * f + 1, 96), 0.0, A.max, one(fl[s], 2 + f), A.subtract)
-            ks.append(k)
+            ks.insert(0, k)
 
         def digits(xp, cnt, sixteens, shift):
             act(sub(xp, 1, 24, 4), cc(OH, 6, 96), F.Copy, scale=shift)
             act(sub(xp, 2, 24, 4), cc(OHM, 6, 96), F.Relu, bias=cnt, scale=sixteens)
-            ts(sub(xp, 3, 24, 4), cc(OHN, 6, 96), sixteens, A.mult)
-        xp, sq, pw = take("xp", 48, 96), take("sq", 128), take("off", 12)
-        for s in range(2):
-            digits(sub(xp, 24 * s, 24 * s + 24), one(par, s), one(hi, s), one(fl[s], 4))
-        quant(sq, R("xp", 0, 512))
-        mm(2, C2, sq)
-        ts(pw, bank(2, xp[3] // 4, xp[4] // 4), 336.0, A.add)
-        for b in range(4):
-            mm(4 + b, ET(b), R("s1", 352, 544), True, False)
-        pick(R("pc", 384, 576), R("s1", 0, 672), pw)
-        for b in range(4):
-            mm(4 + b, EH(b), R("pc", 384, 576), False, True)
-        casts(192, None)
-        quant(R("s1", 672, 864), R("ht", 128, 896))
+            copy("v", sub(xp, 3, 24, 4), cc(OHN, 6, 96), scale=sixteens)
+        pw = take("off", 12)
+        for s in (1, 0):
+            xp, sq = take(("xp", "xq")[s], 24, 96), take("sq", 128)
+            digits(xp, one(par, s), one(hi, s), one(fl[s], 4))
+            quant(sq, R(xp[0], 0, 512))
+            mm(2 + s, C2, sq)
+            ts(sub(pw, 6 * s, 6 * s + 6), bank(2 + s, xp[3] // 4, xp[4] // 4), 336.0, A.add)
+            pick(R("pc", 384 + 96 * s, 480 + 96 * s), R("s1", 0, 672), sub(pw, 6 * s, 6 * s + 6))
+
+        def stage(s, k):
+            pc, done = R("pc", 352 + 128 * s, 480 + 128 * s), R("s1", 640 + 128 * s, 768 + 128 * s)
+            if k:
+                joined(ET, ET, pc, done, 96, 0.5, 4 * s, 96 * s, 32 - 32 * s)
+            else:
+                joined(ET, EH, R("s1", 320 + 128 * s, 448 + 128 * s), pc, 96, None, 4 * s, 96 * s, 32 - 32 * s)
+            quant(sub(done, 224 * k, 224 * k + 128), R("ht", 512 * s, 512 * s + 512))
+        stage(1, 0)
         for t, (s, f) in enumerate(((0, 0), (1, 0), (1, 1), (0, 1))):
             ts(R("xc", t, 384, 4, p1=96), R("qrow", 208 + 96 * f, 304 + 96 * f, p1=96), one(par, s), A.subtract, one(ks[s], f), A.is_equal)
         sq, cnt, hi, kind = take("sq", 128), take("col", 1, 96), take("col", 1, 96), take("col", 2, 96)
         quant(sq, R("xc", 0, 512))
         mm(0, sq, TR)
         count(bank(0, 0, 208, 96), F.Relu, 1.0, -1.0, cnt, hi)
-        xo, sq = take("xo", 48, 96), take("sq", 128)
+        stage(0, 0)
+        stage(1, 1)
+        xo, sq = take("xo", 48, 96), take("sq", 134)
         digits(sub(xo, 0, 24), cnt, hi, one(fl[0], 4))
         ts(sub(xo, 0, 24, 4), cc(OHF, 6, 96), cnt, A.is_lt, one(fl[0], 5), A.mult)
         ts(one(kind, 0), one(ks[0], 0), one(ks[0], 1), A.min, 0.0, A.is_equal)
-        ts(sub(xo, 25, 48, 4), cc(OH, 6, 96), one(kind, 0), A.mult, 320.0, A.mult)
-        ts(sub(xo, 24, 48, 4), cc(OHL, 6, 96), cnt, A.is_gt, 640.0, A.mult)
-        copy("a", sub(xo, 26, 48, 4), cc(OHQ, 6, 96))
-        act(sub(xo, 27, 48, 4), cc(OH, 6, 96), F.Copy, scale=cc(NM, 1, 96))
-        quant(sq, R("xo", 0, 512))
-        mm(1, C2, sq)
+        ts(sub(xo, 26, 48, 4), cc(OH, 6, 96), one(kind, 0), A.mult, 320.0, A.mult)
+        ts(one(kind, 1), one(fl[0], 4), cc(PH, 1, 96), A.add, -32.0, A.add)
+        for t, c in ((0, cc(PM, 1, 96)), (1, one(kind, 1)), (3, 704.0)):
+            ts(sub(xo, 24 + t, 48, 4), cc(OHQ, 6, 96), cnt, A.is_lt, c, A.mult)
+        quant(sq, R("xo", 0, 536))
+        stage(0, 1)
+        mm(7, C2, sub(sq, 0, 128), True, False)
+        mm(7, C2, sub(sq, 6, 134), False, True)
         c0, ends = xo[3] // 4, take("off", 6)
-        L["c", 2] = take("off", 6)
-        ts(L["c", 2], bank(1, c0, c0 + 6), 656.0, A.add, 863.0, A.min)
-        copy("v", ends, bank(1, c0 + 6, c0 + 12))
+        ts(ends, bank(7, c0, c0 + 6), 528.0, A.add)
         xp, sq, pa, z = take("xp", 8, 96), take("sq", 128), take("col", 4, 96), tf(832)
         for e, s in ((0, 0), (4, 1), (5, 0)):
             copy("a", one(xp, e), one(fl[s], 0), scale=2.0 ** 42)
@@ -797,16 +765,15 @@ def rank_program(g, core, T, topo):
             ts(ne, sub(prow, 0, h, 1, 0, pb), cc(Q96 + k, 1, pb), A.not_equal)
             scan(sub(cp, 16, h + 16), ne, ne, 1.0, A.mult, A.mult)
             count(cp, F.Copy, 0.0, 1.0, one(cnt, k), one(hi, k))
-        both = spread(cnt, hi, K, pb, "xo", 3, under=h + 15.5, step=float(AV[l] - h))
-        mw, ow, v = take("off", k16), take("off", k16), tf(2 * h)
-        L["c", l] = mw
-        ts(mw, sub(both, 0, k16), -16.0, A.add, float(h - 1), A.min)
+        ow, v, win = take("off", k16), tf(2 * h), R("iot", 0, P)
+        ts(ow, spread(cnt, hi, K, pb, "xo", 3, under=(OHQ, OHF)[l], step=PH + 2 * l), (-16.0, AV[1] - 16.0)[l], A.add)
         if l == 0:
+            win = tf(P)
             for a in range(0, h, 96):
                 scatter(sub(v, 0, h), sub(L["s"], a // 16, a // 16 + 6), R("iot", BE + a, BE + a + 96))
-            L["c", l] = through(sub(v, 0, h), mw)
-        ts(ow, sub(both, k16, 2 * k16), float(h), A.add)
-        act(sub(v, h, 2 * h), R("iot", 0, BE), F.Copy, off=ow)
+            act(sub(win, 0, h), sub(v, 0, h), F.Identity, bias=float(AV[0] - BE))
+            copy("a", sub(win, h, P), R("iot", h, P))
+        act(sub(v, h, 2 * h), win, F.Copy, off=ow)
         return v
 
     def through(row, off):
@@ -816,37 +783,19 @@ def rank_program(g, core, T, topo):
         wrap(got, out)
         return out
 
-    def parents(l, fw):
+    def parents(l, at):
         n = NS[l]
         h = n // 2
-        if l:
-            z = tf(n)
-            act(sub(z, 0, h), L["z"], F.Copy, off=L["p", l])
-            copy("a", sub(z, h, n), sub(L["z"], h, n))
-        else:
-            z, pr = tf(BE + h), tf(h)
-            for a in range(0, n, 96):
-                act(sub(z, a, a + 96), R("iot", 0, n), F.Copy, off=sub(L["l", l], a // 16, a // 16 + 6))
-            copy("a", sub(z, AV[l], AV[l] + h), sub(z, h, n))
-            act(pr, sub(z, 0, n), F.Copy, off=L["p", l])
-            act(sub(z, BE, BE + h), pr, F.Copy, off=L["s"])
+        z, places = tf(n), L[("z0", "z")[l]]
+        for a in range(0, h, 96):
+            act(sub(z, a, a + 96), places, F.Copy, off=sub(L["p", l], a // 16, a // 16 + 6))
+        copy("a", sub(z, h, n), sub(places, h, n))
         for a in range(0, n, 96):
-            act(R("pat", PAO[l] + a, PAO[l] + a + 96), z, F.Copy, off=sub(fw, a // 16, a // 16 + 6))
-
-    def down(l):
-        h = (192, 96, 96)[l]
-        m = max(h, 128)
-        name, piv, new = (("s0", 192, 384), ("s1", 96, 192), ("s1", 544, 992))[l]
-        for b in range(4):
-            mm(4 + b, ET(b), R(name, piv, piv + m), True, False)
-        pick(R("pc", CO[l], CO[l] + h), R(name, 0, (768, 1120, 992)[l]), L["c", l])
-        for b in range(4):
-            mm(4 + b, ET(b), R("pc", CO[l], CO[l] + m), False, True)
-        casts(h, 0.5)
-        quant(R(name, new, new + m), R("ht", 128, 128 + 4 * m))
+            act(R("pat", PAO[l] + a, PAO[l] + a + 96), z, F.Copy, off=sub(at, a // 16, a // 16 + 6))
 
     first()
     up(0)
+    where()
     candidates()
     v0 = children(0)
     up(1)
@@ -856,35 +805,40 @@ def rank_program(g, core, T, topo):
     for a in (0, 96):
         scatter(inv, sub(z1, a // 16, a // 16 + 6), R("iot", a, a + 96))
     wrap(inv, at1)
-    act(sub(v1, 0, 96), R("iot", 0, 768), F.Identity, bias=352.0, off=last_level())
-    L["c", 1] = through(sub(v1, 0, 96), L["c", 1])
-    down(2)
-    down(1)
-    pick(R("dn1", 0, 96), R("s1", 0, 1120), through(v1, sub(at1, 6, 12)))
-    exchange([(R("dn1", 0, 96), R("s0", BE, BE + 96), PART[0])], "ar2")
-    pick(R("s0", BE + 96, BE + 192), R("s1", 0, 1120), through(v1, sub(at1, 0, 6)))
+    pick(R("pd", 32, 224), R("pc", PPO[0], PPO[0] + 192), L["s"])
+    ends = last_level()
+    act(sub(v1, 0, 96), R("iot", 0, 768), F.Identity, bias=352.0, off=ends)
+    pick(R("pc", 288, 384), R("s1", 352, 1088), ends)
+    joined(ET, ET, R("pc", PPO[1], PPO[1] + 128), R("pc", 288, 416), 96, 0.5)
+    quant(R("s1", AV[1], AV[1] + 128), R("ht", 128, 640))
+    pick(R("dn1", 0, 96), R("s1", 0, 1088), through(v1, sub(at1, 6, 12)))
+    exchange(R("dn1", 0, 96), R("s0", BE + 96, BE + 192), PART[0], "ar2")
+    pick(R("s0", BE, BE + 96), R("s1", 0, 1088), through(v1, sub(at1, 0, 6)))
     fl0, fw = tf(P), take("off", 24)
     for a in range(0, P, 96):
-        scatter(fl0, sub(L["l", 0], a // 16, a // 16 + 6), sub(v0, a, a + 96))
+        act(sub(fl0, a, a + 96), v0, F.Copy, off=sub(L["at0"], a // 16, a // 16 + 6))
     for a in (0, 192):
         wrap(sub(fl0, a, a + 192), sub(fw, a // 16, a // 16 + 12))
-    parents(0, fw)
+    parents(0, L["at0"])
     parents(1, at1)
     dma("y", T.pa[0:1, :], T.pat[0:1, :], [R("pat", 0, 672, p1=1)], [], "st1")
-    yw = tf(768)
-    for i, a in enumerate((192, BE)):
-        mm(i, R("wq", 0, 128), R("s0", a, a + 192))
-        copy("a", sub(yw, a, a + 192), bank(i, 0, 192))
-    down(0)
-    for i, a in enumerate((384, 448)):
-        mm(i, R("wq", 0, 128), R("s0", a, a + 128))
-        copy("va"[i], sub(yw, 384 + 96 * i, 480 + 96 * i), bank(i, 32 * i, 32 * i + 96))
-    for a, b in ((0, 256), (256, P)):
+    yw = tf(832)
+    mm(0, R("wq", 0, 128), R("s0", 192, P))
+    copy("a", sub(yw, 192, P), bank(0, 0, 192))
+    for k in range(2):
+        a, c = BE + 96 * k, AV[0] + 96 * k
+        joined(ET, ET, R("pd", 96 * k, 96 * k + 128), R("s0", a - 32, a + 96), 96, 0.5, 4 * k, 96 * k, 32)
+        quant(R("s0", c - 32 + 32 * k, c + 96 + 32 * k), R("ht", 512 * k, 512 * k + 512))
+        mm(0, R("wq", 0, 128), R("s0", a - 32, a + 96))
+        copy("a", sub(yw, a, a + 96), bank(0, 32, 128))
+        mm(1, R("wq", 0, 128), R("s0", c - 32 + 32 * k, c + 96 + 32 * k))
+        copy("a", sub(yw, c, c + 96), bank(1, 32 - 32 * k, 128 - 32 * k))
+    for a, b in ((0, 192), (192, P)):
         fin = R("fin", a, b)
-        pick(fin, R("s0", 0, 768), sub(fw, a // 16, b // 16))
+        pick(fin, R("s0", 0, 832), sub(fw, a // 16, b // 16))
         dma("y", T.oc[:, 4 * a:4 * b], T.fin[:, a:b].bitcast(dt.uint8), [fin], [], "st1")
-    act(R("yt", 0, 192), yw, F.Copy, off=sub(fw, 0, 12))
-    op("v", lambda: g.vector.tensor_copy(T.yt[:, 192:P], ap(yw).indirect(ap(sub(fw, 12, 24)))), [yw, fw], [R("yt", 192, P)], 0.05 + 1.5 * CYC * 192)
+    for k in range(2):
+        both("av"[k], R("yt", 192 * k, 192 * k + 192), yw, off=sub(fw, 12 * k, 12 * k + 12))
     for a in (0, 192):
         dma("y", T.y[:, a:a + 192], T.yt[:, a:a + 192], [R("yt", a, a + 192)], [], "st1")
     fin = R("fin", 0, P)

from concourse.bass import DstId, RemoteDMATransfer
from concourse.mybir import dt, AluOpType, ActivationFunctionType

A = AluOpType
F = ActivationFunctionType
P = 384
PART = [2, 1]
NS = [384, 192]
AV = [608, 192]
BE = 384
PPO = [672, 576]
PAO = [0, 384, 576]
U = 2.0 ** 28
X4, U8, F32, BF, U16, I32 = "float8_e4m3fn_x4", "uint8", "float32", "bfloat16", "uint16", "int32"

SCRATCH = {"ps": ("psum", [128, 4096], F32)}
for _n, _w in (("f", 512), ("s0", 832), ("s1", 1120), ("pc", 896), ("pd", 224), ("wm", 640), ("tq", 208), ("nw0", 512), ("nwb", 128),
               ("cq", 1536), ("lq", 1280), ("sq", 1928), ("uq", 128), ("uv", 32), ("ur", 512), ("wq", 128), ("fin", 384), ("dn1", 96),
               ("ca", 416), ("cb", 416), ("wv", 144), ("wr", 144), ("wo", 128)):
    SCRATCH[_n] = ("sbuf", [128, _w], X4)
    SCRATCH[_n + "s"] = ("sbuf", [128, _w], U8)
for _n, _w, _d in (("xt", 1536, BF), ("ut", 512, BF), ("wt", 512, BF), ("on", 512, BF), ("idn", 128, BF), ("cw", 512, BF),
                   ("cx", 512, BF), ("tr", 832, BF), ("wkd", 160, BF), ("wke", 160, BF), ("mt", 288, BF), ("tm", 96, BF),
                   ("mz", 96, BF), ("cm", 32, BF), ("et", 520, BF), ("eh", 520, BF), ("xp", 512, BF), ("xo", 544, BF),
                   ("xq", 512, BF), ("xi", 512, BF), ("xl", 1536, BF), ("xm", 896, BF),
                   ("xk", 512, BF), ("xc", 512, BF), ("xs", 768, BF), ("xa", 1664, BF), ("xb", 1664, BF), ("xv", 1024, BF),
                   ("c2", 512, BF), ("xw", 512, BF), ("xr", 512, BF), ("ht", 1024, BF), ("r16", 128, BF), ("qrow", 400, BF),
                   ("iot", 768, F32), ("pi", 2, I32), ("cc", 128, F32), ("zr", 256, BF), ("tau", 130, BF), ("m3", 384, BF), ("sg", 130, BF),
                   ("wk0", 192, BF), ("wk", 192, BF),
                   ("xg", 512, BF), ("off", 448, U16), ("col", 448, F32), ("tf", 20480, F32), ("tb", 20480, BF), ("pat", 672, F32),
                   ("yt", 384, F32)):
    SCRATCH[_n] = ("sbuf", [128, _w], _d)

SEMAPHORES = ["v", "a", "t", "g", "lx0", "lx1", "lx2", "lu", "lw", "lz", "lz2", "sent", "aru", "ar0", "arf", "ar1", "ar2", "st1"]

PM, FX, JA, JB, Q96, OH, OHM, V16, OHN, MK, OHQ, OHF, PH, PJ, OH8 = 0, 1, 2, 5, 8, 10, 16, 44, 58, 64, 34, 120, 100, 104, 88
CYC, FAR = 0.00095, 0.9
START = (
    "0002080i04090k33370b34390a2r3d130d3536382y0c3a1v3c2x2s012z300331320e1l055i1m550g1n2t1o2u1w521p3e1q0s0h1r4z1s0m561t1u063f073z502v0t53570n513j0f540o40595a0l5g5b585h101b5d5c1a0j5e5f1k160z3b171x1f6u1g1j5x3k1i60185q1c5z5s1y3i5y5j5u5l5r5n5t5k6z42615m0p5v0v5o3r140u5w15621d1e5p190q3l2c1h6349642d3n3m4l0r653u274n2e2f3v2i4a2h672n0x2o682k280y662m692j3t6a2p4b6b2g4e2l6c296m6hckdago3g6d4f4m852a863s8c6i4c8b453h6e892b4d446j8d476f87463p6k6p6q116n6o6r6s4k6l236t486g6y4g7d880w6v7c24217a708a224h6x6w8e264j7t724i718i744o738g7b3o8l7u7n7m8h754q4v8j7o4p4t76204s128fh2cf7p3wkb778k1zdy7q7w78797v7r7s4u7h2w7glg7f3q8m7z7x7l7e2q4r7y7j80253x837k7i8182844x8n8tce8p4w9c8zd39b8q4y9d9f8o8r8u90cg9ecl9j8v9g91ch928w8x9kcj9h94953y999l979a9i9893968y9o9pcq9m8sa09n9ya59wci9q9za1a6cp9r9xa2a39sa7a8av9v41a4abafaaauaeadaiahatacasaga99uamajlhb6apb7akanlfal9tb8arb9aqaoaxbabbawlkaycmbnazcrljcsb043b1b2bxb3libzb4b5byc0cnbccoc1llbdctcvcucwbecxbmbkbibgblbhbfbjbpbobtbqc4c6c7buc8c2brc5c9bvc3bslnbwd5d6d7d8ebcad9dodnecdmdldbcbeddddcccdfdecdcydgeid0dhdidjdkeedxlmdrdsczdpdzdqdvdwdtdue0efe1eje2ene5eke6e3ege4eoehelf0f1epf2e7eqerf3lpe8eyeteuf4ese9evewezexf5eaemfffuf6loftgjfgf7fvfhfigxfwgafxfnfkfmfqhtfyfofpflfrfsf8fjgcfzgbg8g9f9g1fbfafcg2fdgyg0h0geg3gfg5g4j8g6gdg7ghgkgigmgghbhjh6h1j2h7feh8gngsgtglgugzhuidgph3h9grhagvgqgwh4hrhdj6hshci5i6h5j7i7hehki4hlhfi8hmhgi9jtjuhn"
    "hhhiifjviahoibhvhwhphqhxhyicj3hziei0jai1j4igi2j9iij5ihjbijiri3ikipimiqilisinjcjdjwiwiuiojgivd1itj0jfiyjejijhizjjixjkjqjmjrjlkijnkhjoj1kjd2lujsjxjpkkkelrlvkfkgjykulsl2klk3kmjzknk2k0kokvltkpk1kqk4krkskwmad4k5mcmbktmdl3k6kxkyl4l7k7l8kzl6l5k9l0lalbl9lxkalylzlck8m1ldlwm2m0m3m6lem4m7kcl1mhm5mgmfmemlm8mkmnmjmim9mokdmmmpmumslqmrmqmvmwmxmymtn1n3n2n4mzn0")
FLIP = "0s1v202t2u2z30313237393d454c58595a5e5f5h6m7k7l818384878j8k96aaacadagbocqcudfdye4fkfqfrfshlikilimj4jujvkekpl8l9lilplsm1m3mxmy"


def R(name, c0, c1, step=1, p0=0, p1=128):
    return (name, p0, p1, c0, c1, step)


def sub(r, a, b, step=1, p0=0, p1=None):
    return (r[0], p0, r[2] if p1 is None else p1, r[3] + a, r[3] + b, step)


def width(r):
    return len(range(r[3], r[4], r[5]))


def meet(a, b, banks):
    if banks:
        return a[3] // 512 <= (b[4] - 1) // 512 and b[3] // 512 <= (a[4] - 1) // 512
    if a[2] <= b[1] or b[2] <= a[1] or a[4] <= b[3] or b[4] <= a[3]:
        return False
    if a[5] == 1 and b[5] == 1:
        return True
    return bool(set(range(a[3], a[4], a[5])) & set(range(b[3], b[4], b[5])))


def numbers(s):
    return [int(s[k:k + 2], 36) for k in range(0, len(s), 2)]


def arrange(ops):
    for i in numbers(FLIP):
        ops[i]["q"], ops[i]["fn"], ops[i]["c"] = ops[i]["alt"]
    seen = {}
    laid = [{i for i, o in enumerate(ops) if o["sem"] == s} for s in ("lz", "lz2")]
    for i, o in enumerate(ops):
        pre = set(o["after"])
        for a, wr in [(r, False) for r in o["r"]] + [(r, True) for r in o["w"]]:
            for j, b, w2 in seen.get(a[0], []):
                bk = a[0] == "ps" and ops[j]["q"] != o["q"]
                if (wr or w2 or bk) and meet(a, b, bk):
                    pre.add(j)
        for a, wr in [(r, False) for r in o["r"]] + [(r, True) for r in o["w"]]:
            seen.setdefault(a[0], []).append((i, a, wr))
        o["pre"] = pre.union(*[s for s in laid if pre & s])
    left, order, done = numbers(START), [], set()
    if sorted(left) != list(range(len(ops))):
        left = list(range(len(ops)))
    while left:
        i = next(k for k in left if ops[k]["pre"] <= done)
        left.remove(i)
        order.append(i)
        done.add(i)
    return order


def rank_program(g, core, T, topo):
    rank = T.rank_of(core)
    if rank is None:
        return
    ops = []
    queue = {"v": g.vector, "a": g.scalar, "t": g.tensor, "g": g, "y": g.sync}
    size = {n: v[2] for n, v in SCRATCH.items()}

    def ap(r):
        if not isinstance(r, tuple):
            return r
        if r[5] == 1:
            return T[r[0]][r[1]:r[2], r[3]:r[4]]
        return T[r[0]][r[1]:r[2], r[3]:r[4]:r[5]]

    def op(q, fn, reads, writes, c, lat=0.0, sem=None, inc=1, after=(), alt=None):
        ops.append({"q": q, "fn": fn, "r": [r for r in reads if isinstance(r, tuple)], "w": writes, "sem": sem, "inc": inc,
                    "c": c, "lat": lat, "after": after, "alt": alt})
        return len(ops) - 1

    def sc(r):
        return (r[0] + "s",) + r[1:]

    def cyc(n, *sides):
        return CYC * max(64, n / 2 if sides and all(size[s[0]] in (BF, U16) for s in sides) else n)

    def memset(out, c):
        op("v", lambda: g.vector.memset(ap(out), c), [], [out], cyc(width(out), out))

    def both(q, out, in_, bias=None, scale=None, off=None, relu=False):
        def src():
            return ap(in_) if off is None else ap(in_).indirect(ap(off))

        def on_v():
            steps = ([(scale, A.mult)] if scale is not None else []) + ([(bias, A.add)] if bias is not None else []) + ([(0.0, A.max)] if relu else [])
            if not steps:
                return g.vector.tensor_copy(ap(out), src())
            if len(steps) == 1:
                return g.vector.tensor_scalar(ap(out), src(), ap(steps[0][0]), None, steps[0][1])
            return g.vector.tensor_scalar(ap(out), src(), ap(steps[0][0]), ap(steps[1][0]), steps[0][1], steps[1][1])

        def on_a():
            if relu:
                return g.scalar.activation(ap(out), src(), F.Relu, scale=1.0 if scale is None else scale)
            if bias is not None:
                return g.scalar.activation(ap(out), src(), F.Identity, bias=ap(bias), scale=1.0 if scale is None else ap(scale))
            if scale is not None:
                return g.scalar.activation(ap(out), src(), F.Copy, scale=ap(scale))
            return g.scalar.activation(ap(out), src(), F.Copy)
        n = width(out)
        ways = {"v": ("v", on_v, cyc(n, out, in_) if off is None else 0.05 + 1.5 * CYC * n), "a": ("a", on_a, cyc(n) if off is None else 0.065 + 1.5 * CYC * n)}
        op(q, ways[q][1], [in_, bias, scale, off], [out], ways[q][2], alt=ways["va"[q == "v"]])

    def copy(q, out, in_, scale=None):
        if size[out[0]] in (F32, BF) and size[in_[0]] in (F32, BF):
            both(q, out, in_, scale=scale)
        else:
            op("v", lambda: g.vector.tensor_copy(ap(out), ap(in_)), [in_], [out], cyc(width(out), out, in_))

    def ts(out, in0, s1, op0, s2=None, op1=None):
        if op1 is None:
            op("v", lambda: g.vector.tensor_scalar(ap(out), ap(in0), ap(s1), None, op0), [in0, s1], [out], cyc(width(out), out, in0))
        else:
            op("v", lambda: g.vector.tensor_scalar(ap(out), ap(in0), ap(s1), ap(s2), op0, op1), [in0, s1, s2], [out], cyc(width(out), out, in0))

    def tt(out, a, b, o):
        op("v", lambda: g.vector.tensor_tensor(ap(out), ap(a), ap(b), o), [a, b], [out], cyc(width(out) * (1 if a[0] == "ps" else 2)))

    def scan(out, d0, d1, init, o0, o1):
        op("v", lambda: g.vector.tensor_tensor_scan(ap(out), ap(d0), ap(d1), ap(init), o0, o1), [d0, d1, init], [out], cyc(width(out), out, d0, d1))

    def turn(out, in_):
        op("v", lambda: g.vector.transpose(ap(out), ap(in_)), [in_], [out], cyc(width(out)))

    def act(out, in_, func, bias=0.0, scale=1.0, acc=None, off=None):
        if acc is None and (func in (F.Copy, F.Identity) or func == F.Relu and bias == 0.0):
            return both("a", out, in_, None if bias == 0.0 else bias, None if scale == 1.0 else scale, off, func == F.Relu)

        def fn():
            if func == F.Copy:
                return g.scalar.activation(ap(out), ap(in_), func, scale=ap(scale), accum_out=ap(acc))
            return g.scalar.activation(ap(out), ap(in_), func, bias=ap(bias), scale=ap(scale), accum_out=ap(acc))
        op("a", fn, [in_, bias, scale], [out] + ([acc] if acc else []), cyc(width(out)) + (0.02 if acc else 0.0))

    def fill(out, c):
        ones = R("on", 0, width(out), 1, out[1], out[2])
        op("a", lambda: g.scalar.activation(ap(out), ap(ones), F.Copy, scale=c), [ones], [out], cyc(width(out)),
           alt=("v", lambda: g.vector.memset(ap(out), c), cyc(width(out), out)))

    def quant(out, in_):
        op("v", lambda: g.vector.quantize_mx(ap(out), ap(sc(out)), ap(in_)), [in_], [out, sc(out)], 0.015 + 0.26 * CYC * width(in_))

    def mm(bank, w, x, start=True, stop=True):
        out = R("ps", 512 * bank, 512 * bank + x[4] - x[3])
        op("t", lambda: g.tensor.matmul_mx(ap(out), ap(w), ap(sc(w)), ap(x), ap(sc(x)), start, stop), [w, sc(w), x, sc(x)], [out],
           0.6 * CYC * (width(x) + 16), 0.05)

    def pick(out, win, off):
        op("v", lambda: g.vector.tensor_copy(ap(out).bitcast(dt.uint32), ap(win).bitcast(dt.uint32).indirect(ap(off))), [win, off], [out],
           0.05 + 1.5 * CYC * width(out))
        act(sc(out), sc(win), F.Copy, off=off)

    def scatter(win, off, in_):
        op("v", lambda: g.vector.tensor_copy(ap(win).indirect(ap(off)), ap(in_)), [in_, off], [win], 0.05 + 3.8 * CYC * width(in_))

    def iota(out, pattern, base, cm, small=True):
        if small:
            op("g", lambda: g.iota(ap(out), pattern, base, cm, allow_small_or_imprecise_dtypes=True), [], [out], 0.13 + 2 * CYC * width(out))
        else:
            op("g", lambda: g.iota(ap(out), pattern, base, cm), [], [out], 0.13 + 2 * CYC * width(out))

    def select(out, in_, pattern, cmp, base, cm, other=0.0):
        op("g", lambda: g.affine_select(ap(out), ap(in_), pattern, cmp, other, base, cm), [in_], [out], 0.17 + 2 * CYC * width(out))

    def hand_round(out, in_):
        op("g", lambda: g.partition_broadcast(ap(out), ap(in_), out[2]), [in_], [out], 0.14 + 4 * CYC * width(out))

    def dma(q, out, in_, reads, writes, sem, after=()):
        return op(q, lambda: queue[q].dma_start(out, in_), reads, writes, 0.06, FAR, sem=sem, inc=16, after=after)

    def exchange(src, dst, part, sem):
        other = T.cores[rank ^ part]
        at, mask, per = topo.addr(other), topo.mask(core, other), len(topo.engines(core, other))
        calls = []
        for kind in range(2):
            def fn(kind=kind):
                s, d = (ap(src).bitcast(dt.uint8), ap(dst).bitcast(dt.uint8)) if kind == 0 else (ap(sc(src)), ap(sc(dst)))
                return g.remote_dma(d, s, T.sem[sem], T.sem.sent, at[1], at[0], mask)
            calls.append(op("g", fn, [sc(src) if kind else src], [], 0.2, FAR * (1.15 - 0.3 * kind), sem="sent", inc=per))
        op(None, None, [], [dst, sc(dst)], 0.0, sem=sem, inc=2 * per, after=calls)

    used = {}

    def take(name, k, p1=128, unit=2):
        a = used.get(name, 0)
        used[name] = a + -(-k // unit) * unit
        return R(name, a, a + k, p1=p1)

    def tf(k, p1=128):
        return take("tf", k, p1, 16)

    def tb(k, p1=128):
        return take("tb", k, p1, 16)

    def cc(c, k=1, pb=128):
        return R("cc", c, c + k, p1=pb)

    def one(r, k):
        return sub(r, k, k + 1)

    def bank(b, c0, c1, pb=128):
        return R("ps", 512 * b + c0, 512 * b + c1, p1=pb)

    def on(k, pb=128):
        return R("on", 0, k, p1=pb)

    def lay(out, in_, sem="lz2"):
        raw = size[out[0]] == X4
        dma("y", ap(out).bitcast(dt.uint8) if raw else ap(out), ap(in_).bitcast(dt.uint8) if raw else ap(in_), [in_], [out], sem,
            loads + [u_load] * (sem == "lz2"))

    ONES, CX, C2, TR = R("f", 384, 512), R("cq", 1280, 1408), R("cq", 1408, 1536), R("tq", 0, 208)

    def ET(b):
        return R("cq", 256 + 128 * b, 384 + 128 * b)

    def EH(b):
        return R("cq", 768 + 128 * b, 896 + 128 * b)

    loads = []
    for k, (a, b) in enumerate(((256, 384), (128, 256), (0, 128))):
        loads.append(dma("yay"[k], T.xt[:, 4 * a:4 * b], T.x[:, 4 * a:4 * b], [], [R("xt", 4 * a, 4 * b)], "lx%d" % k))
        quant(R("f", a, b), R("xt", 4 * a, 4 * b))
    u_load = dma("y", T.ut[:], T.u[:], [], [R("ut", 0, 512)], "lu", loads)
    dma("y", T.wt[:], T.w[:], [], [R("wt", 0, 512)], "lw", loads)
    memset(on(160), 1.0)
    memset(R("on", 160, 512), 1.0)
    quant(R("f", 384, 512), on(512))
    select(R("wke", 0, 160), on(160), [[1, 160]], A.is_ge, -2, -1)
    select(R("wkd", 0, 160), R("wke", 0, 160), [[1, 160]], A.not_equal, -1, -1, 2.0 ** 60)
    iota(R("pi", 0, 1), [[0, 1]], 0, 1, small=False)
    iota(R("r16", 0, 128), [[0, 8], [1, 16]], 0, 0)
    select(R("idn", 0, 128), on(128), [[-1, 128]], A.is_equal, 0, 1)
    copy("a", R("cw", 0, 512, 4), R("wke", 2, 130))
    iota(R("qrow", 0, 400), [[1, 400]], -192, 0)
    iota(cc(JA, 3), [[128, 3]], 1 - 192, 1)
    iota(cc(JB, 2), [[96, 2]], 1, 1)
    iota(cc(PJ, 3), [[-128, 3]], 191, -1)
    iota(cc(PJ + 3, 3), [[128, 3]], 0, 1)
    for a in range(0, 896, 224):
        fill(R("xm", a, a + 224), 0.0)
    for name, a, b in (("et", 0, 520), ("eh", 0, 520), ("xq", 0, 512), ("ht", 0, 128), ("ht", 896, 1024)):
        for k in range(a, b, 260):
            fill(R(name, k, min(b, k + 260)), 0.0)
    copy("a", R("et", 3, 512, 4), R("idn", 0, 128))
    copy("a", R("eh", 3, 512, 4), R("idn", 0, 128), scale=-0.5)
    iota(cc(V16, 12), [[16, 12]], 0, -1)
    iota(cc(Q96, 2), [[96, 2]], 0, 1)
    iota(R("iot", 0, 768), [[1, 768]], 0, 0)
    memset(R("xp", 0, 512), 0.0)
    for name, a, b, p in (("xa", 0, 768, 96), ("xa", 768, 1536, 96), ("xw", 0, 512, 0), ("xr", 0, 512, 0), ("xg", 0, 512, 96),
                          ("xs", 0, 768, 96), ("zr", 0, 256, 0), ("xo", 0, 544, 0), ("xi", 0, 512, 0), ("xb", 0, 768, 0), ("xb", 768, 1536, 0),
                          ("xk", 0, 512, 0), ("xc", 0, 512, 0), ("tr", 0, 832, 96), ("xv", 512, 1024, 96)):
        lay(R(name, a, b, 1, p, 128), R("xm", 0, b - a, 1, p, 128))
    lay(R("mt", 0, 96), on(96))
    lay(R("mt", 192, 288), on(96))
    for name, a, k in (("nw0", 384, 32), ("s1", 192, 32), ("pc", 864, 32), ("pc", 352, 32), ("pd", 0, 32)):
        lay(R(name, a, a + k), sub(ONES, 0, k), "lz")
        lay(sc(R(name, a, a + k)), sc(sub(ONES, 0, k)), "lz")
    for a in (0, 256):
        fill(R("cx", a, a + 256), 1.0)
    for t in (2, 3):
        iota(R("xs", t, 768, 4, p1=96), [[0, 192]], 0, 0)
    for k, t in enumerate((2, 3, 3, 2)):
        copy("a", R("xb", 384 * k + t, 384 * k + 384, 4, p1=96), R("idn", 0, 96, p1=96), scale=-64.0 if k < 2 else 64.0)
    for t in range(2):
        for a in (0, 768):
            iota(R("xb", a + t, a + 768, 4), [[0, 192]], 1 + 3 * (a > 0 == t), 0)
    for t, c in enumerate((-U / 2, U / 64, 0.0, 0.0)):
        select(R("xv", t, 512, 4), on(128), [[0, 128]], A.is_gt, 0, 0, c)
    for a in (512, 768):
        select(R("xv", a, a + 256, p1=96), on(256, 96), [[0, 256]], A.is_gt, 0, 0, U)
    quant(R("wm", 0, 128), R("xm", 0, 512))
    for name, a, k in (("wm", 256, 128), ("cb", 384, 32), ("ca", 384, 32), ("wv", 128, 16), ("wr", 0, 16), ("wr", 32, 112)):
        lay(R(name, a, a + k), R("wm", 0, k))
        lay(sc(R(name, a, a + k)), sc(R("wm", 0, k)))
    quant(R("wm", 384, 512), R("xv", 512, 1024))
    fill(R("xl", 3, 1536, 4), 0.0)
    for e in (0, 768):
        fill(R("xl", e + 512, e + 768, 4), 1.0)
        fill(R("xl", e + 2, e + 256, 4), 0.0)
    fill(R("cw", 1, 512, 4), 1.0)
    fill(cc(MK, 4), 258.0)
    ts(R("tau", 0, 129), R("wke", 1, 130), 2.0, A.mult, -1.0, A.add)
    for q in range(4):
        copy("v", R("sg", 0, 32, 1, 32 * q, 32 * q + 32), R("tau", 32 * q, 32 * q + 32, 1, 32 * q, 32 * q + 32), scale=-1.0)
    for a, b, p0, p1, c in ((32, 96, 0, 64, -1.0), (32, 96, 64, 128, 1.0), (96, 128, 0, 32, -1.0), (96, 128, 64, 96, -1.0),
                            (96, 130, 32, 64, 1.0), (96, 130, 96, 128, 1.0), (128, 130, 0, 32, 1.0), (128, 130, 64, 96, 1.0)):
        fill(R("sg", a, b, 1, p0, p1), c)
    tt(R("m3", 1, 129), R("sg", 0, 128), R("sg", 1, 129), A.mult)
    fill(R("m3", 0, 1), -1.0)
    fill(R("m3", 129, P), 1.0)
    ts(R("pi", 1, 2), R("pi", 0, 1), 15, A.bitwise_and)
    copy("v", cc(PM), R("pi", 1, 2))
    ts(R("cw", 2, 512, 4), R("r16", 0, 128), cc(PM), A.is_equal)
    copy("a", R("cw", 3, 512, 4), R("cw", 2, 512, 4), scale=-1.0)
    o_u = take("off", 24)
    ts(R("wk0", 0, 96), R("r16", 0, 96), cc(PM), A.is_le, -2.0, A.mult)
    ts(R("wk0", 96, 192), R("r16", 0, 96), cc(PM), A.subtract, 1.0, A.is_equal)
    ts(cc(FX), cc(PM), 14.5, A.is_lt, 2048.0, A.mult)
    tt(R("wk0", 0, 96), R("wk0", 0, 96), R("wk0", 96, 192), A.add)
    for a in (0, 96):
        copy("a", R("wk", a, a + 96), R("wk0", 0, 96), scale=2048.0)
    for k, c in enumerate((0, 1, 17)):
        memset(sub(o_u, 8 * k, 8 * k + 8), c)
    ts(cc(OH, 6), cc(V16, 6), cc(PM), A.add, 0.0, A.is_equal)
    ts(cc(OHM, 6), cc(OH, 6), 1008.0, A.mult, -1024.0, A.add)
    copy("a", cc(OHN, 6), cc(OH, 6), scale=-16.0)
    ts(cc(OH8, 8), cc(V16, 8), cc(PM), A.add, 0.0, A.is_equal)
    act(cc(OHF, 6), cc(OH, 6), F.Identity, bias=1024.0, scale=111.5 - 1024.0)
    act(cc(OHQ, 6), cc(OH, 6), F.Identity, bias=1024.0, scale=207.5 - 1024.0)
    ts(cc(PH, 2), cc(Q96, 2), cc(PM), A.subtract)
    ts(cc(PH + 2), cc(Q96), cc(PM), A.subtract, -192.0, A.add)
    copy("a", R("cx", 0, 512, 4), R("cw", 0, 512, 4))
    quant(CX, R("cx", 0, 512))
    for t in range(2):
        select(R("tr", t, 832, 2, p1=96), on(416, 96), [[1, 208], [0, 2]], A.is_ge, -16 - 96 * t, -1)
    quant(TR, R("tr", 0, 832))
    for t in range(4):
        copy("a", R("c2", t, 512, 4), R("cw", max(t, 2), 512, 4))
    quant(C2, R("c2", 0, 512))
    act(R("mt", 96, 192), R("idn", 0, 96), F.Identity, bias=1.0, scale=-2.0)
    act(R("mz", 0, 96), R("idn", 0, 96), F.Identity, bias=1.0, scale=-1.0)
    act(R("tm", 0, 96), R("cw", 0, 384, 4), F.Identity, bias=-1.0)
    for a, c in ((0, -1024.0), (16, 1024.0)):
        fill(R("cm", a, a + 16), c)
        fill(R("cm", a, a + 16, 5), 0.0)
    for b in range(4):
        quant(ET(b), R("et", 3 - b, 515 - b))
        quant(EH(b), R("eh", 3 - b, 515 - b))
    quant(R("uq", 0, 128), R("ut", 0, 512))
    exchange(R("uq", 0, 2), R("uv", 16, 18), PART[1], "aru")
    for l in range(2):
        pick(R("ur", 96 * l, 96 * l + 96), R("uq", 0, 128), sub(o_u, 8 * l, 8 * l + 6))
    pick(R("ur", 192, 320), R("uv", 0, 32), sub(o_u, 16, 24))
    quant(R("wq", 0, 128), R("wt", 0, 512))

    def wrap(src, out):
        n = width(src)
        ws = tf(n)
        scan(ws, R("wk", 0, n), src, 0.0, A.add, A.max)
        ts(out, sub(ws, 15, n, 16), cc(FX), A.subtract)

    def listed(tile, a0, a1, m, b, out):
        lq = take("lq", m)
        quant(lq, R(tile, 4 * a0, 4 * (a0 + m)))
        mm(b, ONES, lq)
        wrap(bank(b, 0, a1 - a0), out)
        return lq

    def own_products(b, win, wide, pb):
        mm(b, win, sub(win, 0, wide))
        last = tf(wide, pb)
        scan(last, R("wkd", 0, wide, p1=pb), bank(b, 0, wide, pb), 0.0, A.mult, A.max)
        return last

    def half(n, row, vals):
        h, K, pb = n // 2, 3, 128
        s, xp, sq = take("col", K, pb), take("xp", 12, pb), take("sq", 128)
        fill(sub(xp, 3, 12, 4), -h / pb)
        for k in range(K):
            sg, eq, run = tb(128), tb(n), tb(n)
            act(sg, sub(row, k, n, 3), F.Sign, bias=vals[k], scale=-1.0, acc=one(s, k))
            ts(sub(eq, 0, 128), sg, 0.0, A.is_equal)
            for i, j in enumerate(((1, 2), (2, 0), (0, 1))[k]):
                out = sub(eq, 128 + 128 * i, 256 + 128 * i)
                if j == k + 1:
                    sg = tb(128)
                    act(sg, sub(row, j, n, 3), F.Sign, bias=vals[k], scale=-1.0)
                    act(out, sg, F.Relu, scale=-2.0)
                else:
                    ts(out, sub(row, j, n, 3), vals[k], A.is_gt if j > k else A.is_ge, 2.0, A.mult)
            scan(run, R("m3", 0, n), eq, one(s, k), A.mult, A.add)
            ts(sub(xp, 4 * k, 12, 5), cc(MK, 3 - k), one(run, n - 1), A.is_le)
        quant(sq, R("xp", 0, 512))
        lower, L["z0"], L["at0"] = take("col", 4), tf(P), take("off", 24)
        copy("a", sub(lower, 0, 3), sub(xp, 0, 12, 4))
        mm(2, CX, sq)
        cn = bank(2, 0, K)
        out = take("off", n // 16)
        for side in range(2):
            for k in range(K):
                e, a, b = 4 * side * h + k, (0, 0, 64)[k], (128, h, h)[k]
                x = R("xl", e + 4 * a, e + 4 * b - k, 4, p1=pb)
                if side == 0:
                    ts(x, R("qrow", a, b), one(cn, k), A.is_ge)
                else:
                    ts(x, R("qrow", h + a, h + b), one(cn, k), A.add, cc(JA + k), A.is_ge)
        for i in range(2):
            listed("xl", h * i, h * i + h, h, 4 + i, sub(out, h * i // 16, (h * i + h) // 16))
            copy("a", sub(L["z0"], h * i, h * i + h), bank(4 + i, 0, h))
        at = take("col", 16)
        copy("v", sub(at, 0, 3), cn)
        L["at"] = at, lower
        return out

    def where():
        (at, lower), xi, sq, K = L["at"], take("xi", 96), take("sq", 128), 3
        for k in range(K):
            act(one(at, 3 + k), one(at, k), F.Identity, bias=cc(PJ + k), scale=2.0)
            act(one(at, 6 + k), one(at, k), F.Identity, bias=cc(PJ + 3 + k), scale=-1.0)
            act(one(at, 9 + k), one(at, 3 + k), F.Identity, bias=one(at, 6 + k), scale=one(lower, k))
        ts(sub(at, 12, 15), sub(at, 9, 12), 1.5 * 2.0 ** 28, A.add, 1.5 * 2.0 ** 28, A.subtract)
        for k in range(K):
            copy("a", sub(xi, 32 * k, 32 * k + 32, 4), cc(OH8, 8), scale=one(at, 12 + k))
        tt(sub(at, 0, 3), sub(at, 9, 12), sub(at, 12, 15), A.subtract)
        for k in range(K):
            copy("a", sub(xi, 32 * k + 1, 32 * k + 32, 4), cc(OH8, 8), scale=one(at, k))
        quant(sq, R("xi", 0, 512))
        mm(4, C2, sq)
        copy("v", L["at0"], bank(4, 0, 24))

    def sizes(wins, by):
        K = len(wins)
        tmp, row, d, bound = tf(32 * K, 96), tf(96 * K, 96), [], []
        for k in range(K):
            last = own_products(k, wins[k], 128, 96)
            d.append(one(last, 127))
            turn(sub(tmp, k, 32 * K, K), sub(last, 96, 128))
            e = take("col", 1, 96)
            act(e, d[k], F.Identity, bias=2.0 ** -30, scale=1.25 * 2.0 ** -24)
            bound.append(tf(96, 96))
            act(bound[k], R("tm", 0, 96, p1=96), F.Identity, bias=d[k], scale=e)
        if by == "aa":
            hand_round(sub(row, 0, 32 * K), sub(tmp, 0, 32 * K, 1, 0, 1))
        for q in range(3):
            for r in (1, 2) if by == "aa" else (0, 1, 2):
                copy(by[r - 1], sub(row, 32 * K * r, 32 * K * (r + 1), 1, 32 * q, 32 * q + 32), sub(tmp, 0, 32 * K, 1, 32 * r, 32 * r + 32))
        return row, [sub(row, k, 96 * K, K) for k in range(K)], d, bound

    def scores(wins, cols, ur, short=False):
        K = len(wins)
        n = 96 * K
        for k in range(K):
            mm(6 + k, wins[k], ur)
        mm(5, ur, cols)
        if short:
            ge, eq, above, later = tb(n, 96), tb(n, 96), tb(n // 2, 96), tb(n, 96)
            ts(ge, bank(5, 0, n, 96), bank(6, 0, 1, 96), A.is_ge)
            ts(eq, bank(5, 0, n, 96), bank(6, 0, 1, 96), A.is_equal)
            scan(above, sub(ge, 0, n // 2), sub(ge, n // 2, n), -n / 2, A.add, A.add)
            scan(later, R("mz", 0, n, p1=96), eq, 0.0, A.mult, A.add)
            y = take("col", 1, 96)
            ts(y, one(above, n // 2 - 1), one(later, n - 1), A.subtract)
            return [y]
        sv, s, nx = take("col", K, 96), take("col", K, 96), []
        for k in range(K):
            copy("a", one(sv, k), bank(6 + k, 0, 1, 96))
        for k in range(K):
            sg, eq, run = tb(n, 96), tb(n, 96), tb(n, 96)
            act(sg, bank(5, 0, n, 96), F.Sign, bias=one(sv, k), scale=-1.0, acc=one(s, k))
            ts(eq, sg, 0.0, A.is_equal, -1.0, A.mult)
            scan(run, R("mt", 96 - 96 * k, 96 - 96 * k + n, p1=96), eq, one(s, k), A.mult, A.add)
            nx.append(one(run, n - 1))
        return nx

    def cell(t, j):
        return R("xa", 384 * (j ^ 2) + t, 384 * (j ^ 2) + 384, 4, p1=96)

    def candidates():
        quant(R("nw0", 0, 192), R("ht", 128, 896))
        exchange(R("nw0", 0, 192), R("nw0", 192, 384), PART[0], "ar0")
        quant(R("nwb", 0, 128), R("ht", 512, 1024))
        wins = [[R("nw0", 0, 128), R("nwb", 0, 128)], [R("nw0", 192, 320), R("nw0", 288, 416)]]
        got = []
        for s in range(2):
            row, rows, d, bound = sizes(wins[s], ("aa", "av")[s])
            got.append((row, rows, d))
            if s == 0:
                sx = scores(wins[0], R("nw0", 0, 192), R("ur", 0, 128))
                for k in range(2):
                    ts(R("xr", 2 + k, 64, 4, p1=96), R("cm", 0, 16, p1=96), sx[k], A.is_gt)
                    ts(R("xw", 64 + k, 128, 4, p1=96), R("cm", 16, 32, p1=96), sx[k], A.is_le)
                quant(R("wo", 0, 128), R("xr", 0, 512))
                exchange(R("wo", 0, 16), R("wr", 16, 32), PART[0], "arf")
                quant(R("wv", 0, 128), R("xw", 0, 512))
            for k in range(2):
                tt(cell(2 * s + k, 2 * s + k), rows[k], bound[k], A.is_le)
            ts(cell(2 * s, 2 * s + 1), rows[1], d[0], A.is_le)
            sg = tb(96, 96)
            act(sg, rows[0], F.Sign, bias=d[1], scale=-1.0)
            act(cell(2 * s + 1, 2 * s), sg, F.Relu)
        for j in range(2):
            for k in range(2):
                ts(cell(j, 2 + k), got[1][1][k], got[0][2][j], A.is_le)
        for j in range(2):
            for k in range(2):
                ts(cell(2 + j, k), got[0][1][k], got[1][2][j], A.is_lt)
        quant(R("ca", 0, 192), R("xa", 0, 768))
        quant(R("ca", 192, 384), R("xa", 768, 1536))
        for k in range(4):
            for name in ("wv", "wr"):
                mm(2, R("ca", 96 * (k ^ 2), 96 * (k ^ 2) + 128), R(name, 16 - 4 * k, 144 - 4 * k), (k, name) == (0, "wv"), (k, name) == (3, "wr"))
        for k in range(4):
            mm(7, ET(k), R(("wv", "wr")[k // 2], 16 - 4 * k, 144 - 4 * k), k == 0, k == 3)
        xp, thr, sq = take("xp", 32, 96), take("col", 16, 96), take("sq", 128)
        c0 = xp[3] // 4
        flags = sub(xp, 16, 32, 4)
        act(thr, bank(7, 0, 16, 96), F.Identity, bias=1000.0, scale=96.5 - 1000.0)
        copy("a", sub(xp, 16, 32), bank(7, 0, 16, 96))
        tt(sub(xp, 0, 16), bank(2, 0, 16, 96), thr, A.is_gt)
        quant(sq, R("xp", 0, 512))
        mm(1, CX, sq)
        q = R("qrow", 192, 288, p1=96)
        for k in range(4):
            ts(R("xm", k, 384, 4, p1=96), q, bank(1, c0 + k, c0 + k + 1, 96), A.is_ge)
            ts(R("xm", 384 + k, 768, 4, p1=96), q, bank(1, c0 + k, c0 + k + 1, 96), A.add, bank(1, c0 + 4 + k, c0 + 5 + k, 96), A.is_ge)
        pa = take("col", 8, 96)
        copy("a", sub(pa, 4, 8), flags)
        copy("v", sub(pa, 0, 4), bank(1, c0 + 4, c0 + 8, 96))
        L["l", 1] = take("off", 12)
        lq = [listed("xm", 96 * k, 96 * k + 96, 128, 2 * k, sub(L["l", 1], 6 * k, 6 * k + 6)) for k in (1, 0)]
        for k in range(4):
            act(R("xg", k, 512, 4, p1=96), on(128, 96), F.Copy, scale=one(pa, 4 + k))
        sq = take("sq", 128)
        quant(sq, R("xg", 0, 512))
        L["z"] = tf(192)
        for k in range(2):
            mm(5 + k, sq, lq[1 - k])
            copy("a", sub(L["z"], 96 * k, 96 * k + 96), bank(5 + k, 0, 96))
        L["s"] = take("off", 12)
        for k in range(2):
            ts(R("xs", 384 + k, 768, 4, p1=96), q, one(pa, k), A.add, cc(JB + k, 1, 96), A.is_ge)
            ts(R("xs", k, 384, 4, p1=96), q, one(pa, k), A.is_ge)
        listed("xs", 0, 192, 192, 3, L["s"])

    def count(src, func, bias, scale, cnt, hi):
        n, pb = width(src), src[2]
        act(tb(n, pb), src, func, bias=bias, scale=scale, acc=cnt)
        act(tb(n // 16, pb), sub(src, 15, n, 16), func, bias=bias, scale=scale, acc=hi)

    def spread(cnt, hi, K, pb, tile, b, under=None, step=0):
        G = pb // 16
        xp = take(tile, 4 * K * G, pb)
        for k in range(K):
            e = 4 * G * k
            act(sub(xp, e + 2, e + 4 * G, 4), cc(OHM, G, pb), F.Relu, bias=one(cnt, k), scale=one(hi, k))
            copy("v", sub(xp, e + 3, e + 4 * G, 4), cc(OHN, G, pb), scale=one(hi, k))
            if under:
                ts(sub(xp, e, e + 4 * G, 4), cc(under, G, pb), one(cnt, k), A.is_lt, cc(step + k, 1, pb), A.mult)
                ts(sub(xp, e + 1, e + 4 * G, 4), cc(under, G, pb), one(cnt, k), A.is_lt, cc(PM, 1, pb), A.mult)
        sq = take("sq", 128)
        quant(sq, R(tile, 0, 512))
        mm(b, C2, sq)
        return bank(b, xp[3] // 4, xp[4] // 4)

    L = {}

    def joined(one_, other, x, y, h, scale, b0=4, at=0, c0=0):
        for b in range(4):
            mm(b0 + b, one_(b), x, True, False)
        for b in range(4):
            mm(b0 + b, other(b), y, False, True)
        for b in range(4):
            copy("va"[b & 1], R("ht", 128 + 4 * at + b, 128 + 4 * (at + h), 4), bank(b0 + b, c0, c0 + h), scale=scale)

    def first():
        row, vals = tf(P), []
        for k in range(3):
            last = own_products(k, R("f", 128 * k, 128 * k + 128), 160, 128)
            vals.append(one(last, 159))
            turn(sub(row, k, 96, 3), sub(last, 128, 160))
        for i in range(2):
            copy("av"[i], sub(row, 96, 192, 1, 64 * i, 64 * i + 64), sub(row, 0, 96, 1, 64 - 64 * i, 128 - 64 * i))
        for i in range(8):
            q, r = i // 2, i % 2
            o = q ^ (3 - 2 * r)
            copy("av"[i & 1], sub(row, 192 + 96 * r, 288 + 96 * r, 1, 32 * q, 32 * q + 32), sub(row, 0, 96, 1, 32 * o, 32 * o + 32))
        L["l", 0] = half(P, row, vals)

    def up(l):
        n, s = NS[l], "s%d" % l
        h = n // 2
        m = max(h, 128)
        lw, win = L["l", l], R(("f", "nw0")[l], 0, P)
        for a, b in ((h, n), (96, h), (0, 96)) if l == 0 else ((h, n), (0, h)):
            pick(R(s, a, b), win, sub(lw, a // 16, b // 16))
        K, pb = h // 96, 96
        par, hi = take("col", K, pb), take("col", K, pb)
        pw = take("off", h // 16)
        L["p", l] = pw
        for k in range(K)[::-1]:
            mm(k, R(s, pb * k, pb * k + 128), R(s, h, h + m))
            rm = tf(16 + h, pb)
            fill(sub(rm, 0, 16), -1e29)
            scan(sub(rm, 16, 16 + h), bank(k, 0, h, pb), on(h, pb), -1e29, A.max, A.mult)
            count(rm, F.Sign, one(rm, 15 + h), -1.0, one(par, k), one(hi, k))
        for k in range(K)[::-1]:
            a = PPO[l] + pb * k
            ts(sub(pw, 6 * k, 6 * k + 6), spread(one(par, k), one(hi, k), 1, pb, ("xp", "xq")[k], 2 + k), float(h - 16), A.add)
            pick(R("pc", a, a + pb), R(s, 0, n), sub(pw, 6 * k, 6 * k + 6))
            joined(ET, EH, R(s, pb * k, pb * k + 128), R("pc", a, a + 128), pb, None, 4 * (k == K - 1), pb * k)

    def last_level():
        quant(R("s1", 320, 448), R("ht", 0, 512))
        exchange(R("s1", 352, 448), R("s1", 448, 544), PART[1], "ar1")
        quant(R("s1", 544, 672), R("ht", 128, 640))
        wins = [R("s1", 544, 672), R("s1", 448, 576)]
        rows, ds, fl, ks = [], [], [], []

        def at(t, j):
            return R("xb", 384 * j + t, 384 * j + 384, 4, p1=96)
        for s in range(2):
            row, unused, d, bound = sizes([wins[s]], ("aa", "av")[s])
            y = scores([wins[s]], wins[s], R("ur", 96 * s + 96, 96 * s + 224), s == 1)[0]
            rows.append(row)
            ds.append(d[0])
            tt(at(s, s), row, bound[0], A.is_le)
            if s:
                tt(at(1, 2), row, bound[0], A.is_gt)
            else:
                copy("a", at(0, 3), at(0, 0), scale=-1.0)
            c = take("col", 6, 96)
            ts(R("xv", s, 512, 2, p1=96), R("zr", 0, 256, p1=96), y, A.is_gt if s else A.is_le, -U, A.mult)
            w = R("xv", s, s + 1, p1=96)
            for k, (ca, cb) in enumerate(((2.0 ** -42, 0), (0, 2.0 ** -42), (0, -2.0 ** 96), (-2.0 ** 96, 0), (0, 96.0), (0, -192.0))[:6 - s]):
                act(one(c, k), w, F.Identity, bias=float(cb), scale=(cb - ca) / U)
            fl.append(c)
        ts(at(0, 1), rows[1], ds[0], A.is_le)
        ts(at(0, 2), rows[1], ds[0], A.is_lt, -1.0, A.mult)
        sg = tb(96, 96)
        act(sg, rows[0], F.Sign, bias=ds[1], scale=-1.0)
        act(at(1, 0), sg, F.Relu)
        act(at(1, 3), sg, F.Relu, scale=-1.0)
        quant(R("cb", 0, 192), R("xb", 0, 768))
        quant(R("cb", 192, 384), R("xb", 768, 1536))
        quant(R("wm", 128, 256), R("xv", 0, 512))
        mm(2, R("wm", 128, 256), R("cb", 0, 192))
        mm(7, R("wm", 384, 512), R("cb", 192, 384), True, False)
        mm(7, R("wm", 128, 256), R("cb", 192, 384), False, True)
        par, hi = take("col", 2, 96), take("col", 2, 96)
        for s in (1, 0):
            mm(s, wins[s], R("s1", 352, 640))
            ms, rm = [tf(192, 96), tf(192, 96)], tf(208, 96)
            for f in range(2):
                gs = tf(192, 96)
                act(gs, bank(s, 96 * f, 96 * f + 192, 96), F.Identity, bias=one(fl[s], 2 + f), scale=one(fl[s], f))
                tt(ms[f], bank((2, 7)[f], 0, 192, 96), gs, A.min)
            fill(sub(rm, 0, 16), -1e29)
            scan(sub(rm, 16, 208), ms[0], ms[1], -1e29, A.max, A.max)
            count(rm, F.Sign, one(rm, 207), -1.0, one(par, s), one(hi, s))
            mm(4 + s, R("cb", 96 * s, 96 * s + 128), R("wm", 254, 382), True, False)
            mm(4 + s, R("cb", 288 - 96 * s, 416 - 96 * s), R("wm", 258, 386), False, False)
            mm(4 + s, R("cb", 288 - 96 * s, 416 - 96 * s), R("wm", 2, 130), False, True)
            k = take("col", 2, 96)
            for f in range(2):
                ts(one(k, f), bank(4 + s, 126 * f, 126 * f + 1, 96), 0.0, A.max, one(fl[s], 2 + f), A.subtract)
            ks.insert(0, k)

        def digits(xp, cnt, sixteens, shift):
            act(sub(xp, 1, 24, 4), cc(OH, 6, 96), F.Copy, scale=shift)
            act(sub(xp, 2, 24, 4), cc(OHM, 6, 96), F.Relu, bias=cnt, scale=sixteens)
            copy("v", sub(xp, 3, 24, 4), cc(OHN, 6, 96), scale=sixteens)
        pw = take("off", 12)
        for s in (1, 0):
            xp, sq = take(("xp", "xq")[s], 24, 96), take("sq", 128)
            digits(xp, one(par, s), one(hi, s), one(fl[s], 4))
            quant(sq, R(xp[0], 0, 512))
            mm(2 + s, C2, sq)
            ts(sub(pw, 6 * s, 6 * s + 6), bank(2 + s, xp[3] // 4, xp[4] // 4), 336.0, A.add)
            pick(R("pc", 384 + 96 * s, 480 + 96 * s), R("s1", 0, 672), sub(pw, 6 * s, 6 * s + 6))

        def stage(s, k):
            pc, done = R("pc", 352 + 128 * s, 480 + 128 * s), R("s1", 640 + 128 * s, 768 + 128 * s)
            if k:
                joined(ET, ET, pc, done, 96, 0.5, 4 * s, 96 * s, 32 - 32 * s)
            else:
                joined(ET, EH, R("s1", 320 + 128 * s, 448 + 128 * s), pc, 96, None, 4 * s, 96 * s, 32 - 32 * s)
            quant(sub(done, 224 * k, 224 * k + 128), R("ht", 512 * s, 512 * s + 512))
        stage(1, 0)
        for t, (s, f) in enumerate(((0, 0), (1, 0), (1, 1), (0, 1))):
            ts(R("xc", t, 384, 4, p1=96), R("qrow", 208 + 96 * f, 304 + 96 * f, p1=96), one(par, s), A.subtract, one(ks[s], f), A.is_equal)
        sq, cnt, hi, kind = take("sq", 128), take("col", 1, 96), take("col", 1, 96), take("col", 2, 96)
        quant(sq, R("xc", 0, 512))
        mm(0, sq, TR)
        count(bank(0, 0, 208, 96), F.Relu, 1.0, -1.0, cnt, hi)
        stage(0, 0)
        stage(1, 1)
        xo, sq = take("xo", 48, 96), take("sq", 134)
        digits(sub(xo, 0, 24), cnt, hi, one(fl[0], 4))
        ts(sub(xo, 0, 24, 4), cc(OHF, 6, 96), cnt, A.is_lt, one(fl[0], 5), A.mult)
        ts(one(kind, 0), one(ks[0], 0), one(ks[0], 1), A.min, 0.0, A.is_equal)
        ts(sub(xo, 26, 48, 4), cc(OH, 6, 96), one(kind, 0), A.mult, 320.0, A.mult)
        ts(one(kind, 1), one(fl[0], 4), cc(PH, 1, 96), A.add, -32.0, A.add)
        for t, c in ((0, cc(PM, 1, 96)), (1, one(kind, 1)), (3, 704.0)):
            ts(sub(xo, 24 + t, 48, 4), cc(OHQ, 6, 96), cnt, A.is_lt, c, A.mult)
        quant(sq, R("xo", 0, 536))
        stage(0, 1)
        mm(7, C2, sub(sq, 0, 128), True, False)
        mm(7, C2, sub(sq, 6, 134), False, True)
        c0, ends = xo[3] // 4, take("off", 6)
        ts(ends, bank(7, c0, c0 + 6), 528.0, A.add)
        xp, sq, pa, z = take("xp", 8, 96), take("sq", 128), take("col", 4, 96), tf(832)
        for e, s in ((0, 0), (4, 1), (5, 0)):
            copy("a", one(xp, e), one(fl[s], 0), scale=2.0 ** 42)
        quant(sq, R("xp", 0, 512))
        mm(3, CX, sq)
        copy("v", sub(pa, 0, 2), bank(3, xp[3] // 4, xp[3] // 4 + 2, 96))
        for s in range(2):
            ts(one(pa, 2 + s), one(pa, s), one(ks[s], 0), A.add)
            ts(R("xk", s, 384, 4, p1=96), R("qrow", 192, 288, p1=96), one(pa, s), A.is_ge)
            ts(R("xk", 2 + s, 384, 4, p1=96), R("qrow", 193, 289, p1=96), one(pa, 2 + s), A.is_equal, 288.0, A.mult)
        by = take("off", 6)
        listed("xk", 0, 96, 128, 3, by)
        mm(3, R("wm", 128, 256), TR)
        act(sub(z, 352, 544), bank(3, 16, 208), F.Identity, bias=-1.0, scale=-0.5 / U)
        fill(sub(z, 544, 640), 0.0)
        act(sub(z, 640, 832), sub(z, 0, 640), F.Copy, off=pw)
        act(R("pat", PAO[2], PAO[2] + 96), sub(z, 352, 832), F.Copy, off=by)
        return ends

    def children(l):
        h = NS[l] // 2
        K, pb, k16 = h // 96, 96, h // 16
        prow, cnt, hi = tb(h), take("col", K, pb), take("col", K, pb)
        act(prow, R("iot", 0, 2 * h), F.Identity, bias=-float(h), off=L["p", l])
        for k in range(K):
            ne, cp = tb(h, pb), tb(h + 16, pb)
            fill(sub(cp, 0, 16), 1.0)
            ts(ne, sub(prow, 0, h, 1, 0, pb), cc(Q96 + k, 1, pb), A.not_equal)
            scan(sub(cp, 16, h + 16), ne, ne, 1.0, A.mult, A.mult)
            count(cp, F.Copy, 0.0, 1.0, one(cnt, k), one(hi, k))
        ow, v, win = take("off", k16), tf(2 * h), R("iot", 0, P)
        ts(ow, spread(cnt, hi, K, pb, "xo", 3, under=(OHQ, OHF)[l], step=PH + 2 * l), (-16.0, AV[1] - 16.0)[l], A.add)
        if l == 0:
            win = tf(P)
            for a in range(0, h, 96):
                scatter(sub(v, 0, h), sub(L["s"], a // 16, a // 16 + 6), R("iot", BE + a, BE + a + 96))
            act(sub(win, 0, h), sub(v, 0, h), F.Identity, bias=float(AV[0] - BE))
            copy("a", sub(win, h, P), R("iot", h, P))
        act(sub(v, h, 2 * h), win, F.Copy, off=ow)
        return v

    def through(row, off):
        n = 16 * width(off)
        got, out = tf(n), take("off", n // 16)
        act(got, row, F.Copy, off=off)
        wrap(got, out)
        return out

    def parents(l, at):
        n = NS[l]
        h = n // 2
        z, places = tf(n), L[("z0", "z")[l]]
        for a in range(0, h, 96):
            act(sub(z, a, a + 96), places, F.Copy, off=sub(L["p", l], a // 16, a // 16 + 6))
        copy("a", sub(z, h, n), sub(places, h, n))
        for a in range(0, n, 96):
            act(R("pat", PAO[l] + a, PAO[l] + a + 96), z, F.Copy, off=sub(at, a // 16, a // 16 + 6))

    first()
    up(0)
    where()
    candidates()
    v0 = children(0)
    up(1)
    v1 = children(1)
    z1, at1, inv = take("off", 12), take("off", 12), tf(192)
    wrap(L["z"], z1)
    for a in (0, 96):
        scatter(inv, sub(z1, a // 16, a // 16 + 6), R("iot", a, a + 96))
    wrap(inv, at1)
    pick(R("pd", 32, 224), R("pc", PPO[0], PPO[0] + 192), L["s"])
    ends = last_level()
    act(sub(v1, 0, 96), R("iot", 0, 768), F.Identity, bias=352.0, off=ends)
    pick(R("pc", 288, 384), R("s1", 352, 1088), ends)
    joined(ET, ET, R("pc", PPO[1], PPO[1] + 128), R("pc", 288, 416), 96, 0.5)
    quant(R("s1", AV[1], AV[1] + 128), R("ht", 128, 640))
    pick(R("dn1", 0, 96), R("s1", 0, 1088), through(v1, sub(at1, 6, 12)))
    exchange(R("dn1", 0, 96), R("s0", BE + 96, BE + 192), PART[0], "ar2")
    pick(R("s0", BE, BE + 96), R("s1", 0, 1088), through(v1, sub(at1, 0, 6)))
    fl0, fw = tf(P), take("off", 24)
    for a in range(0, P, 96):
        act(sub(fl0, a, a + 96), v0, F.Copy, off=sub(L["at0"], a // 16, a // 16 + 6))
    for a in (0, 192):
        wrap(sub(fl0, a, a + 192), sub(fw, a // 16, a // 16 + 12))
    parents(0, L["at0"])
    parents(1, at1)
    dma("y", T.pa[0:1, :], T.pat[0:1, :], [R("pat", 0, 672, p1=1)], [], "st1")
    yw = tf(832)
    mm(0, R("wq", 0, 128), R("s0", 192, P))
    copy("a", sub(yw, 192, P), bank(0, 0, 192))
    for k in range(2):
        a, c = BE + 96 * k, AV[0] + 96 * k
        joined(ET, ET, R("pd", 96 * k, 96 * k + 128), R("s0", a - 32, a + 96), 96, 0.5, 4 * k, 96 * k, 32)
        quant(R("s0", c - 32 + 32 * k, c + 96 + 32 * k), R("ht", 512 * k, 512 * k + 512))
        mm(0, R("wq", 0, 128), R("s0", a - 32, a + 96))
        copy("a", sub(yw, a, a + 96), bank(0, 32, 128))
        mm(1, R("wq", 0, 128), R("s0", c - 32 + 32 * k, c + 96 + 32 * k))
        copy("a", sub(yw, c, c + 96), bank(1, 32 - 32 * k, 128 - 32 * k))
    for a, b in ((0, 192), (192, P)):
        fin = R("fin", a, b)
        pick(fin, R("s0", 0, 832), sub(fw, a // 16, b // 16))
        dma("y", T.oc[:, 4 * a:4 * b], T.fin[:, a:b].bitcast(dt.uint8), [fin], [], "st1")
    for k in range(2):
        both("av"[k], R("yt", 192 * k, 192 * k + 192), yw, off=sub(fw, 12 * k, 12 * k + 12))
    for a in (0, 192):
        dma("y", T.y[:, a:a + 192], T.yt[:, a:a + 192], [R("yt", a, a + 192)], [], "st1")
    fin = R("fin", 0, P)
    for k in range(4):
        dma("yaya"[k], T.osc[4 * k:4 * k + 4, :], T.fins[32 * k:32 * k + 4, 0:P], [sc(fin)], [], "st1")

    order = arrange(ops)
    place = {j: i for i, j in enumerate(order)}
    total = {}
    for o in ops:
        if o["sem"]:
            total[o["sem"]] = total.get(o["sem"], 0) + o["inc"]
    clock = {q: {} for q in queue}
    for i in order:
        o = ops[i]
        o["need"], o["mark"], o["clk"] = [], False, {}
        q = o["q"]
        if q is None:
            continue
        want = {}
        for j in o["pre"]:
            key = ops[j]["sem"] or ops[j]["q"]
            if not (key == q == "t"):
                want[key] = max(want.get(key, -1), place[j])
        for key, pj in sorted(want.items(), key=lambda kv: -kv[1]):
            if clock[q].get(key, -1) >= pj:
                continue
            e = ops[order[pj]]
            o["need"].append(e)
            e["mark"] = True
            for k2, p2 in list(e["clk"].items()) + [(key, len(ops) if e["sem"] else pj)]:
                clock[q][k2] = max(clock[q].get(k2, -1), p2)
        o["clk"] = dict(clock[q])
    count_of = {q: 0 for q in queue}
    for i in order:
        o = ops[i]
        q = o["q"]
        if q is None:
            continue
        for e in o["need"]:
            if e["sem"]:
                queue[q].wait_ge(T.sem[e["sem"]], total[e["sem"]])
            else:
                queue[q].wait_ge(T.sem[e["q"]], e["n"])
        ins = o["fn"]()
        if o["sem"]:
            if o["sem"] != "sent":
                ins.then_inc(T.sem[o["sem"]], 16)
        elif o["mark"]:
            count_of[q] += 1
            o["n"] = count_of[q]
            ins.then_inc(T.sem[q], 1)
    for s in ("sent", "st1"):
        g.wait_ge(T.sem[s], total[s])
